import numpy as np
import ml_dtypes


def mxq(x, axis, fmt="e4m3"):
    dtype, down = {"e4m3": (ml_dtypes.float8_e4m3fn, 7), "e5m2": (ml_dtypes.float8_e5m2, 14)}[fmt]
    v = np.moveaxis(np.asarray(x, np.float32).astype(ml_dtypes.bfloat16).astype(np.float64), axis, -1)
    blocks = v.reshape(v.shape[:-1] + (-1, 32))
    amax = np.abs(blocks).max(-1, keepdims=True)
    byte = np.maximum(np.where(amax > 0, np.frexp(amax)[1] - 1 + 127, 0) - down, 1)
    scale = np.exp2(byte - 127.0)
    codes = (blocks / scale).astype(np.float32).astype(dtype).astype(np.float64)
    return np.moveaxis((codes * scale).reshape(v.shape), -1, axis)


WIDE = False


def mx_kscale(k):
    if not WIDE:
        return np.ones(k)
    levels = np.array([10, -10, 5, -5, 0])
    if k % 512:
        return np.exp2(np.random.permutation(np.resize(levels, k // 32))).repeat(32)
    a = np.empty((k // 512, 16))
    for p in range(k // 512):
        a[p, :8] = np.random.permutation(np.resize(levels, 8))
        for g in range(8):
            far = levels[np.abs(levels - a[p, g]) >= 10]
            a[p, g + 8] = far[np.random.randint(len(far))]
    return np.exp2(a.ravel()).repeat(32)


def f64(x):
    return np.asarray(x).astype(np.float64)


def striped(idx):
    return np.tile(np.asarray(idx).reshape(-1, 16).T, (8, 1)).astype(np.uint16)


def unstriped(offs):
    return offs[:16].T.reshape(-1).astype(np.int64)


E2M1 = np.array([0.0, 0.5, 1.0, 1.5, 2.0, 3.0, 4.0, 6.0, -0.0, -0.5, -1.0, -1.5, -2.0, -3.0, -4.0, -6.0])


def pack_weight(w, fmt):
    k, n = w.shape
    w = f64(np.asarray(w, np.float32).astype(ml_dtypes.bfloat16)).reshape(k // 32, 32, n)
    amax = np.abs(w).max(1)
    if fmt == "e4m3":
        byte = np.frexp(amax)[1] - 1 + 127 - 7
    else:
        mant, ex = np.frexp(amax / 6.0)
        byte = np.where(mant > 0.5, ex, ex - 1) + 127
    byte = np.clip(np.where(amax > 0, byte, 1), 1, 254)
    scaled = (w * np.exp2(127.0 - byte)[:, None, :]).reshape(k, n).astype(np.float32)
    by_word = np.ascontiguousarray(scaled.reshape(k // 512, 128, 4, n).transpose(0, 1, 3, 2))
    if fmt == "e4m3":
        words = by_word.astype(ml_dtypes.float8_e4m3fn).view(np.uint8)
    else:
        c = by_word.astype(ml_dtypes.float4_e2m1fn).view(np.uint8) & 0xF
        words = (c[..., 0::2] | (c[..., 1::2] << 4)).reshape(k // 512, 128, 2 * n)
    return np.ascontiguousarray(words), np.ascontiguousarray(byte.astype(np.uint8).reshape(k // 512, 16, n))


def unpack_weight(words, scales, fmt):
    g, _, n = scales.shape
    words = np.ascontiguousarray(words).reshape(g, 128, n, -1)
    if fmt == "e4m3":
        vals = words.view(ml_dtypes.float8_e4m3fn).astype(np.float64)
    else:
        nib = np.empty((g, 128, n, 4), np.uint8)
        nib[..., 0::2] = words & 0xF
        nib[..., 1::2] = words >> 4
        vals = E2M1[nib]
    vals = vals * np.repeat(np.exp2(scales.astype(np.float64) - 127.0), 8, axis=1)[..., None]
    return vals.transpose(0, 1, 3, 2).reshape(g * 512, n)


B, N, T, D, DV, NQ = 1, 2048, 4096, 1024, 128, 128
PAGE = 512
CAP = 2.0


def setup_inputs():
    n = np.random.standard_normal
    pages = np.random.permutation(T // PAGE)[:B * N // PAGE]
    idx = (pages[:, None] * PAGE + np.arange(PAGE)[None, :]).reshape(-1)
    s = mx_kscale(D)[:, None]
    u = np.ones(T)
    u[idx] = mx_kscale(B * N)
    r = np.random.uniform(0.5, 2.0, T)
    k = n((D, T)) / s
    v = n((DV, T)) / (u * r)
    kp = pack_weight(k, "e2m1")
    vp = pack_weight(v.T, "e4m3")
    return {
        "qT": (n((B, D, NQ)) * s * (1.00 / np.sqrt(D))).astype(np.float32),
        "k_words": np.ascontiguousarray(kp[0].reshape(D // 1024, 2, 128, T, 2).transpose(0, 2, 3, 1, 4)).reshape(D // 1024, 128, T, 4),
        "k_scales": kp[1],
        "v_words": vp[0],
        "v_scales": vp[1],
        "vs": np.tile(u * r, (128, 1)).astype(np.float32),
        "offs": striped(idx),
        "voffs": striped((pages[:, None] * DV + np.arange(DV)[None, :]).reshape(-1)),
    }


def reference(qT, k_words, k_scales, v_words, v_scales, vs, offs, voffs):
    idx = unstriped(offs)
    k = unpack_weight(k_words.reshape(D // 1024, 128, T, 2, 2).transpose(0, 3, 1, 2, 4).reshape(D // 512, 128, 2 * T), k_scales, "e2m1")
    v = unpack_weight(v_words, v_scales, "e4m3")
    v = v.reshape(T // 512, 512, DV)[unstriped(voffs)[::DV] // DV].reshape(B, N, DV)
    pick = lambda x: x[:, idx].reshape(x.shape[0], B, N).transpose(1, 0, 2)
    q = f64(qT)
    score = mxq(q, 1, "e4m3").transpose(0, 2, 1) @ pick(k)
    score = CAP * np.tanh(score / CAP)
    p = np.square(np.maximum(score, 0.0))
    total = p.sum(-1, keepdims=True) + 1.0
    w = p * pick(f64(vs))[:, :1, :]
    y = mxq(w, 2, "e4m3") @ v
    y = y / total
    return y

@@ -1,0 +1,182 @@
+from contextlib import ExitStack
+
+import concourse.mybir as mybir
+from concourse.masks import make_identity
+
+N, T, D, DV, NQ = 2048, 4096, 1024, 128, 128
+PAGE = 512
+CAP = 2.0
+FLOPS = 2 * NQ * N * (D + DV)
+
+F32 = mybir.dt.float32
+BF16 = mybir.dt.bfloat16
+I32 = mybir.dt.int32
+U32 = mybir.dt.uint32
+U16 = mybir.dt.uint16
+U8 = mybir.dt.uint8
+FP8X4 = mybir.dt.float8_e4m3fn_x4
+FP4X4 = mybir.dt.float4_e2m1fn_x4
+ACT = mybir.ActivationFunctionType
+ALU = mybir.AluOpType
+AX = mybir.AxisListType
+
+P = 128
+PACK = 4
+PAGES = N // PAGE
+POOL_PAGES = T // PAGE
+PASSES = D // (P * PACK)
+SCALE_ROWS = 16
+SPARE = P - SCALE_ROWS
+
+
+def tile_attend_pkv4_rel2_cap_kernel(tc, qT, k_words, k_scales, v_words, v_scales, vs, offs, voffs, out):
+    nc = tc.nc
+    with ExitStack() as ctx:
+        lists = ctx.enter_context(tc.tile_pool(name="lists", bufs=1))
+        keep = ctx.enter_context(tc.tile_pool(name="keep", bufs=1))
+        psum = ctx.enter_context(tc.psum_pool(name="psum", bufs=1))
+
+        slots = lists.tile([P, N // 16], U16, name="slots")
+        vcols = lists.tile([P, PAGES * DV // 16], U16, name="vcols")
+        nc.sync.dma_start(slots[:], offs)
+        nc.sync.dma_start(vcols[:], voffs)
+
+        ks_pool = keep.tile([P, T], U8, name="ks_pool", align_bytes=64)
+        vs_pool = keep.tile([P, T], F32, name="vs_pool", tag="early_late", align_bytes=64)
+        vsc_pool = keep.tile([P, POOL_PAGES * DV], U8, name="vsc_pool", align_bytes=64)
+        ks_second = keep.tile([P, N], U8, name="ks_second", align_bytes=64)
+        q_raw = keep.tile([P, PASSES, PACK, NQ], F32, name="q_raw", align_bytes=64)
+        kw_pool = keep.tile([P, T], I32, name="kw_pool", align_bytes=64)
+
+        nc.vector.memset(ks_pool[0:SPARE, :].bitcast(I32), 0)
+        nc.sync.dma_start(ks_pool[SPARE:P, :].bitcast(I32), k_scales[1].bitcast(I32))
+        nc.sync.dma_start(vs_pool[P - 1 : P, :], vs[0:1, :])
+        nc.sync.dma_start(q_raw[:], qT[0].rearrange("(g p j) w -> p g j w", g=PASSES, j=PACK))
+        nc.sync.dma_start(kw_pool[:], k_words[0].rearrange("p t b -> p (t b)").bitcast(I32))
+        ks_rows = k_scales[0].rearrange("(q r) t -> r q t", r=4)
+        for r in range(4):
+            nc.scalar.dma_start(ks_pool[r:P:32, :].bitcast(I32), ks_rows[r].bitcast(I32))
+
+        nc.vector.memset(vsc_pool[:].bitcast(I32), 0)
+        nc.vector.memset(ks_second[:].bitcast(I32), 0)
+        nc.vector.memset(vs_pool[0 : P - 1, :], 0.0)
+        vsc_rows = v_scales.rearrange("u (q r) e -> r q u e", r=4)
+        for r in range(4):
+            nc.gpsimd.dma_start(
+                vsc_pool[r:P:32, :].bitcast(I32).rearrange("q (u e) -> q u e", u=POOL_PAGES),
+                vsc_rows[r].bitcast(I32),
+            )
+        identity = keep.tile([P, P], F32, name="identity")
+        make_identity(nc, identity[:])
+
+        q_bf = keep.tile([P, PASSES, NQ, PACK], BF16, name="q_bf", align_bytes=64)
+        for g in range(PASSES):
+            nc.scalar.copy(q_bf[:, g], q_raw[:, g].rearrange("p j w -> p w j"))
+
+        ks_first = keep.tile([P, N], U8, name="ks_first", align_bytes=64)
+        nc.vector.tensor_copy(ks_first[:], ks_pool[:].indirect(slots[:]))
+        for r in range(4):
+            queue = nc.scalar if r < 3 else nc.gpsimd
+            queue.dma_start(ks_second[r:P:32, :].bitcast(I32), ks_first[SPARE + r : P : 4, :].bitcast(I32))
+        ks_planes = (ks_first, ks_second)
+
+        q_codes = keep.tile([P, PASSES * NQ], U32, name="q_codes", align_bytes=64)
+        q_scales = keep.tile([P, PASSES * NQ], U8, name="q_scales", align_bytes=64)
+        nc.vector.quantize_mx(
+            out=q_codes[:].bitcast(FP8X4), scales=q_scales[:], in_=q_bf[:].rearrange("p g w j -> p (g w j)")
+        )
+
+        vs_listed = keep.tile([P, N], F32, name="vs_listed", align_bytes=64)
+        nc.vector.tensor_copy(vs_listed[:], vs_pool[:].indirect(slots[:]))
+        vs_turned = [keep.tile([P, PACK], F32, name="vs_turned%d" % e) for e in range(PAGES)]
+        for e in range(PAGES):
+            nc.sync.dma_start(
+                vs_turned[e][:],
+                vs_listed[P - 1 : P, e * PAGE : (e + 1) * PAGE].rearrange("o (s t) -> o s t", t=PACK),
+            )
+        vw_pool = keep.tile([P, POOL_PAGES * DV], I32, name="vw_pool", tag="early_late", align_bytes=64)
+        nc.sync.dma_start(
+            vw_pool[:].rearrange("p (u e) -> p u e", u=POOL_PAGES),
+            v_words.rearrange("u p e r -> p u (e r)").bitcast(I32),
+        )
+
+        sums = keep.tile([P, PAGES + 1], F32, name="sums")
+        nc.vector.memset(sums[:, PAGES : PAGES + 1], 1.0)
+        vw = keep.tile([P, PAGES * DV], U32, name="vw", align_bytes=64)
+        vsc = keep.tile([P, PAGES * DV], U8, name="vsc", align_bytes=64)
+        acc = psum.tile([P, DV], F32, name="acc")
+        turned = []
+
+        def weigh(e):
+            pairs = keep.tile([P, PAGE], U32, name="pairs%d" % e, align_bytes=64)
+            cols = slice(e * PAGE // 16, (e + 1) * PAGE // 16)
+            nc.vector.tensor_copy(pairs[:], kw_pool[:].bitcast(U32).indirect(slots[:, cols]))
+            keys = keep.tile([P, PASSES, 2 * PAGE], U8, name="keys%d" % e, align_bytes=64)
+            nc.vector.tensor_copy(
+                keys[:].bitcast(U16), pairs[:].bitcast(U16).rearrange("p (n g) -> p g n", g=PASSES)
+            )
+            scores = psum.tile([P, PAGE], F32, name="scores%d" % e)
+            for g in range(PASSES):
+                nc.tensor.matmul_mx(
+                    out=scores[:],
+                    lhsT=q_codes[:, g * NQ : (g + 1) * NQ].bitcast(FP8X4),
+                    lhsT_scale=q_scales[:, g * NQ : (g + 1) * NQ],
+                    rhs=keys[:, g, :].bitcast(FP4X4),
+                    rhs_scale=ks_planes[g][:, e * PAGE : (e + 1) * PAGE],
+                    start=(g == 0),
+                    stop=(g == PASSES - 1),
+                )
+            capped = keep.tile([P, PACK, P], F32, name="capped%d" % e)
+            nc.scalar.activation(capped[:], scores[:].rearrange("q (s t) -> q t s", t=PACK), ACT.Tanh, scale=1.0 / CAP)
+            positive = keep.tile([P, PAGE], F32, name="positive%d" % e)
+            nc.scalar.activation(positive[:], capped[:].rearrange("q t s -> q (t s)"), ACT.Relu)
+            weights = keep.tile([P, PACK, P], F32, name="weights%d" % e)
+            nc.scalar.activation(
+                weights[:].rearrange("q t s -> q (t s)"), positive[:], ACT.Square, scale=CAP, accum_out=sums[:, e : e + 1]
+            )
+            bank = psum.tile([P, PACK, NQ], F32, name="turned%d" % e, tag="turned%d" % (e % 3))
+            for t in range(PACK):
+                nc.tensor.transpose(bank[:, t, :], weights[:, t, :], identity[:])
+            turned.append(bank)
+
+        def multiply(e):
+            w_bf = keep.tile([P, NQ, PACK], BF16, name="w_bf%d" % e, align_bytes=64)
+            nc.vector.tensor_tensor(
+                w_bf[:],
+                turned[e][:].rearrange("s t q -> s q t"),
+                vs_turned[e][:].unsqueeze(1).to_broadcast([P, NQ, PACK]),
+                ALU.mult,
+            )
+            if e == 0:
+                nc.vector.tensor_copy(vw[:], vw_pool[:].bitcast(U32).indirect(vcols[:]))
+                nc.vector.tensor_copy(vsc[:], vsc_pool[:].indirect(vcols[:]))
+            w_codes = keep.tile([P, NQ], U32, name="w_codes%d" % e, align_bytes=64)
+            w_scales = keep.tile([P, NQ], U8, name="w_scales%d" % e, align_bytes=64)
+            nc.vector.quantize_mx(
+                out=w_codes[:].bitcast(FP8X4), scales=w_scales[:], in_=w_bf[:].rearrange("s q t -> s (q t)")
+            )
+            nc.tensor.matmul_mx(
+                out=acc[:],
+                lhsT=w_codes[:].bitcast(FP8X4),
+                lhsT_scale=w_scales[:],
+                rhs=vw[:, e * DV : (e + 1) * DV].bitcast(FP8X4),
+                rhs_scale=vsc[:, e * DV : (e + 1) * DV],
+                start=(e == 0),
+                stop=(e == PAGES - 1),
+            )
+
+        weigh(0)
+        weigh(1)
+        weigh(2)
+        multiply(0)
+        weigh(3)
+        multiply(1)
+        multiply(2)
+        denom = keep.tile([P, 1], F32, name="denom")
+        nc.vector.tensor_reduce(denom[:], sums[:], axis=AX.X, op=ALU.add)
+        inverse = keep.tile([P, 1], F32, name="inverse")
+        nc.vector.reciprocal(inverse[:], denom[:])
+        multiply(3)
+        result = keep.tile([P, DV], F32, name="result")
+        nc.scalar.activation(result[:], acc[:], ACT.Copy, scale=inverse[:])
+        nc.sync.dma_start(out[0], result[:])

@@ -26,7 +26,8 @@ PAGES = N // PAGE
 POOL_PAGES = T // PAGE
 PASSES = D // (P * PACK)
 SCALE_ROWS = 16
-SPARE = P - SCALE_ROWS
+KS_ROW0 = P - PASSES * SCALE_ROWS
+ZERO_PIECES = 8
 
 
 def tile_attend_pkv4_rel2_cap_kernel(tc, qT, k_words, k_scales, v_words, v_scales, vs, offs, voffs, out):
@@ -34,38 +35,29 @@ def tile_attend_pkv4_rel2_cap_kernel(tc, qT, k_words, k_scales, v_words, v_scale
     with ExitStack() as ctx:
         lists = ctx.enter_context(tc.tile_pool(name="lists", bufs=1))
         keep = ctx.enter_context(tc.tile_pool(name="keep", bufs=1))
+        reused = ctx.enter_context(tc.tile_pool(name="reused", bufs=1))
         psum = ctx.enter_context(tc.psum_pool(name="psum", bufs=1))
 
         slots = lists.tile([P, N // 16], U16, name="slots")
         vcols = lists.tile([P, PAGES * DV // 16], U16, name="vcols")
-        nc.sync.dma_start(slots[:], offs)
-        nc.sync.dma_start(vcols[:], voffs)
-
         ks_pool = keep.tile([P, T], U8, name="ks_pool", align_bytes=64)
-        vs_pool = keep.tile([P, T], F32, name="vs_pool", tag="early_late", align_bytes=64)
-        vsc_pool = keep.tile([P, POOL_PAGES * DV], U8, name="vsc_pool", align_bytes=64)
-        ks_second = keep.tile([P, N], U8, name="ks_second", align_bytes=64)
+        vs_pool = reused.tile([P, T], F32, name="vs_pool", align_bytes=64, offset=0)
         q_raw = keep.tile([P, PASSES, PACK, NQ], F32, name="q_raw", align_bytes=64)
         kw_pool = keep.tile([P, T], I32, name="kw_pool", align_bytes=64)
-
-        nc.vector.memset(ks_pool[0:SPARE, :].bitcast(I32), 0)
-        nc.sync.dma_start(ks_pool[SPARE:P, :].bitcast(I32), k_scales[1].bitcast(I32))
-        nc.sync.dma_start(vs_pool[P - 1 : P, :], vs[0:1, :])
+        nc.sync.dma_start(slots[:], offs)
+        nc.scalar.dma_start(ks_pool[KS_ROW0:P, :].bitcast(I32), k_scales.rearrange("g f t -> (g f) t").bitcast(I32))
         nc.sync.dma_start(q_raw[:], qT[0].rearrange("(g p j) w -> p g j w", g=PASSES, j=PACK))
+        nc.sync.dma_start(vcols[:], voffs)
+        nc.sync.dma_start(vs_pool[P - 1 : P, :], vs[0:1, :])
         nc.sync.dma_start(kw_pool[:], k_words[0].rearrange("p t b -> p (t b)").bitcast(I32))
-        ks_rows = k_scales[0].rearrange("(q r) t -> r q t", r=4)
-        for r in range(4):
-            nc.scalar.dma_start(ks_pool[r:P:32, :].bitcast(I32), ks_rows[r].bitcast(I32))
 
-        nc.vector.memset(vsc_pool[:].bitcast(I32), 0)
-        nc.vector.memset(ks_second[:].bitcast(I32), 0)
-        nc.vector.memset(vs_pool[0 : P - 1, :], 0.0)
-        vsc_rows = v_scales.rearrange("u (q r) e -> r q u e", r=4)
-        for r in range(4):
-            nc.gpsimd.dma_start(
-                vsc_pool[r:P:32, :].bitcast(I32).rearrange("q (u e) -> q u e", u=POOL_PAGES),
-                vsc_rows[r].bitcast(I32),
-            )
+        sums = keep.tile([P, PAGES + 2], F32, name="sums")
+        nc.vector.memset(sums[:, PAGES + 1 : PAGES + 2], 1.0)
+        warm = keep.tile([P, 1], F32, name="warm")
+        nc.scalar.activation(warm[:], sums[:, PAGES + 1 : PAGES + 2], ACT.Tanh)
+        nc.vector.memset(ks_pool[0:KS_ROW0, :].bitcast(I32), 0)
+        ks_planes = keep.tile([P, PASSES, N], U8, name="ks_planes", align_bytes=64)
+        nc.vector.memset(ks_planes[:].bitcast(I32), 0)
         identity = keep.tile([P, P], F32, name="identity")
         make_identity(nc, identity[:])
 
@@ -73,19 +65,18 @@ def tile_attend_pkv4_rel2_cap_kernel(tc, qT, k_words, k_scales, v_words, v_scale
         for g in range(PASSES):
             nc.scalar.copy(q_bf[:, g], q_raw[:, g].rearrange("p j w -> p w j"))
 
-        ks_first = keep.tile([P, N], U8, name="ks_first", align_bytes=64)
-        nc.vector.tensor_copy(ks_first[:], ks_pool[:].indirect(slots[:]))
-        for r in range(4):
-            queue = nc.scalar if r < 3 else nc.gpsimd
-            queue.dma_start(ks_second[r:P:32, :].bitcast(I32), ks_first[SPARE + r : P : 4, :].bitcast(I32))
-        ks_planes = (ks_first, ks_second)
+        ks_listed = keep.tile([P, N], U8, name="ks_listed", align_bytes=64)
+        nc.vector.tensor_copy(ks_listed[:], ks_pool[:].indirect(slots[:]))
+        for g in range(PASSES):
+            for r in range(4):
+                row0 = KS_ROW0 + g * SCALE_ROWS
+                queue = nc.gpsimd if (g, r) == (PASSES - 1, 3) else nc.scalar
+                queue.dma_start(
+                    ks_planes[r:P:32, g, :].bitcast(I32), ks_listed[row0 + r : row0 + SCALE_ROWS : 4, :].bitcast(I32)
+                )
 
-        q_codes = keep.tile([P, PASSES * NQ], U32, name="q_codes", align_bytes=64)
-        q_scales = keep.tile([P, PASSES * NQ], U8, name="q_scales", align_bytes=64)
-        nc.vector.quantize_mx(
-            out=q_codes[:].bitcast(FP8X4), scales=q_scales[:], in_=q_bf[:].rearrange("p g w j -> p (g w j)")
-        )
-
+        for c in range(ZERO_PIECES):
+            nc.vector.memset(vs_pool[0 : P - 1, c * T // ZERO_PIECES : (c + 1) * T // ZERO_PIECES], 0.0)
         vs_listed = keep.tile([P, N], F32, name="vs_listed", align_bytes=64)
         nc.vector.tensor_copy(vs_listed[:], vs_pool[:].indirect(slots[:]))
         vs_turned = [keep.tile([P, PACK], F32, name="vs_turned%d" % e) for e in range(PAGES)]
@@ -94,52 +85,82 @@ def tile_attend_pkv4_rel2_cap_kernel(tc, qT, k_words, k_scales, v_words, v_scale
                 vs_turned[e][:],
                 vs_listed[P - 1 : P, e * PAGE : (e + 1) * PAGE].rearrange("o (s t) -> o s t", t=PACK),
             )
-        vw_pool = keep.tile([P, POOL_PAGES * DV], I32, name="vw_pool", tag="early_late", align_bytes=64)
+
+        q_codes = keep.tile([P, PASSES * NQ], U32, name="q_codes", align_bytes=64)
+        q_scales = keep.tile([P, PASSES * NQ], U8, name="q_scales", align_bytes=64)
+        nc.vector.quantize_mx(
+            out=q_codes[:].bitcast(FP8X4), scales=q_scales[:], in_=q_bf[:].rearrange("p g w j -> p (g w j)")
+        )
+
+        vw_pool = reused.tile([P, POOL_PAGES * DV], I32, name="vw_pool", align_bytes=64, offset=0)
         nc.sync.dma_start(
             vw_pool[:].rearrange("p (u e) -> p u e", u=POOL_PAGES),
             v_words.rearrange("u p e r -> p u (e r)").bitcast(I32),
         )
+        vsc_pool = reused.tile([P, POOL_PAGES * DV], U8, name="vsc_pool", align_bytes=64, offset=4 * POOL_PAGES * DV)
+        nc.vector.memset(vsc_pool[:].bitcast(I32), 0)
+        vsc_rows = v_scales.rearrange("u (q r) e -> r q u e", r=4)
+        for r in range(4):
+            nc.sync.dma_start(
+                vsc_pool[r:P:32, :].bitcast(I32).rearrange("q (u e) -> q u e", u=POOL_PAGES),
+                vsc_rows[r].bitcast(I32),
+            )
 
-        sums = keep.tile([P, PAGES + 1], F32, name="sums")
-        nc.vector.memset(sums[:, PAGES : PAGES + 1], 1.0)
-        vw = keep.tile([P, PAGES * DV], U32, name="vw", align_bytes=64)
-        vsc = keep.tile([P, PAGES * DV], U8, name="vsc", align_bytes=64)
-        acc = psum.tile([P, DV], F32, name="acc")
         turned = []
-
-        def weigh(e):
+        piece = 0
+        for e in range(PAGES):
             pairs = keep.tile([P, PAGE], U32, name="pairs%d" % e, align_bytes=64)
             cols = slice(e * PAGE // 16, (e + 1) * PAGE // 16)
             nc.vector.tensor_copy(pairs[:], kw_pool[:].bitcast(U32).indirect(slots[:, cols]))
-            keys = keep.tile([P, PASSES, 2 * PAGE], U8, name="keys%d" % e, align_bytes=64)
-            nc.vector.tensor_copy(
-                keys[:].bitcast(U16), pairs[:].bitcast(U16).rearrange("p (n g) -> p g n", g=PASSES)
-            )
-            scores = psum.tile([P, PAGE], F32, name="scores%d" % e)
-            for g in range(PASSES):
-                nc.tensor.matmul_mx(
-                    out=scores[:],
-                    lhsT=q_codes[:, g * NQ : (g + 1) * NQ].bitcast(FP8X4),
-                    lhsT_scale=q_scales[:, g * NQ : (g + 1) * NQ],
-                    rhs=keys[:, g, :].bitcast(FP4X4),
-                    rhs_scale=ks_planes[g][:, e * PAGE : (e + 1) * PAGE],
-                    start=(g == 0),
-                    stop=(g == PASSES - 1),
-                )
-            capped = keep.tile([P, PACK, P], F32, name="capped%d" % e)
-            nc.scalar.activation(capped[:], scores[:].rearrange("q (s t) -> q t s", t=PACK), ACT.Tanh, scale=1.0 / CAP)
-            positive = keep.tile([P, PAGE], F32, name="positive%d" % e)
-            nc.scalar.activation(positive[:], capped[:].rearrange("q t s -> q (t s)"), ACT.Relu)
             weights = keep.tile([P, PACK, P], F32, name="weights%d" % e)
-            nc.scalar.activation(
-                weights[:].rearrange("q t s -> q (t s)"), positive[:], ACT.Square, scale=CAP, accum_out=sums[:, e : e + 1]
-            )
-            bank = psum.tile([P, PACK, NQ], F32, name="turned%d" % e, tag="turned%d" % (e % 3))
+            parts = 2 if e == 0 else 1
+            width = PAGE // parts
+            step = PAGE if parts == 1 else P
+            for h in range(parts):
+                keys = keep.tile([P, PASSES, 2 * width], U8, name="keys%d" % piece, align_bytes=64)
+                nc.vector.tensor_copy(
+                    keys[:].bitcast(U16),
+                    pairs[:, h * width : (h + 1) * width].bitcast(U16).rearrange("p (n g) -> p g n", g=PASSES),
+                )
+                scores = psum.tile([P, width], F32, name="scores%d" % piece, tag="scores%d" % (piece % 4))
+                for n0 in range(0, width, step):
+                    slot0 = e * PAGE + h * width + n0
+                    for g in range(PASSES):
+                        nc.tensor.matmul_mx(
+                            out=scores[:, n0 : n0 + step],
+                            lhsT=q_codes[:, g * NQ : (g + 1) * NQ].bitcast(FP8X4),
+                            lhsT_scale=q_scales[:, g * NQ : (g + 1) * NQ],
+                            rhs=keys[:, g, 2 * n0 : 2 * (n0 + step)].bitcast(FP4X4),
+                            rhs_scale=ks_planes[:, g, slot0 : slot0 + step],
+                            start=(g == 0),
+                            stop=(g == PASSES - 1),
+                        )
+                rows = width // PACK
+                capped = keep.tile([P, PACK, rows], F32, name="capped%d" % piece)
+                nc.scalar.activation(capped[:], scores[:].rearrange("q (s t) -> q t s", t=PACK), ACT.Tanh, scale=1.0 / CAP)
+                positive = keep.tile([P, PACK, rows], F32, name="positive%d" % piece)
+                nc.scalar.activation(positive[:], capped[:], ACT.Relu)
+                nc.scalar.activation(
+                    weights[:, :, h * rows : (h + 1) * rows], positive[:], ACT.Square, scale=CAP,
+                    accum_out=sums[:, piece : piece + 1],
+                )
+                piece += 1
+            bank = psum.tile([P, PACK, NQ], F32, name="turned%d" % e, tag="turned%d" % e if e < PAGES - 1 else "scores1")
             for t in range(PACK):
                 nc.tensor.transpose(bank[:, t, :], weights[:, t, :], identity[:])
             turned.append(bank)
 
-        def multiply(e):
+        vw = keep.tile([P, PAGES * DV], U32, name="vw", align_bytes=64)
+        vsc = keep.tile([P, PAGES * DV], U8, name="vsc", align_bytes=64)
+        nc.vector.tensor_copy(vw[:], vw_pool[:].bitcast(U32).indirect(vcols[:]))
+        nc.vector.tensor_copy(vsc[:], vsc_pool[:].indirect(vcols[:]))
+        acc = psum.tile([P, DV], F32, name="acc")
+        denom = keep.tile([P, 1], F32, name="denom")
+        inverse = keep.tile([P, 1], F32, name="inverse")
+        for e in range(PAGES):
+            if e == PAGES - 1:
+                nc.vector.tensor_reduce(denom[:], sums[:], axis=AX.X, op=ALU.add)
+                nc.vector.reciprocal(inverse[:], denom[:])
             w_bf = keep.tile([P, NQ, PACK], BF16, name="w_bf%d" % e, align_bytes=64)
             nc.vector.tensor_tensor(
                 w_bf[:],
@@ -147,9 +168,6 @@ def tile_attend_pkv4_rel2_cap_kernel(tc, qT, k_words, k_scales, v_words, v_scale
                 vs_turned[e][:].unsqueeze(1).to_broadcast([P, NQ, PACK]),
                 ALU.mult,
             )
-            if e == 0:
-                nc.vector.tensor_copy(vw[:], vw_pool[:].bitcast(U32).indirect(vcols[:]))
-                nc.vector.tensor_copy(vsc[:], vsc_pool[:].indirect(vcols[:]))
             w_codes = keep.tile([P, NQ], U32, name="w_codes%d" % e, align_bytes=64)
             w_scales = keep.tile([P, NQ], U8, name="w_scales%d" % e, align_bytes=64)
             nc.vector.quantize_mx(
@@ -165,18 +183,6 @@ def tile_attend_pkv4_rel2_cap_kernel(tc, qT, k_words, k_scales, v_words, v_scale
                 stop=(e == PAGES - 1),
             )
 
-        weigh(0)
-        weigh(1)
-        weigh(2)
-        multiply(0)
-        weigh(3)
-        multiply(1)
-        multiply(2)
-        denom = keep.tile([P, 1], F32, name="denom")
-        nc.vector.tensor_reduce(denom[:], sums[:], axis=AX.X, op=ALU.add)
-        inverse = keep.tile([P, 1], F32, name="inverse")
-        nc.vector.reciprocal(inverse[:], denom[:])
-        multiply(3)
         result = keep.tile([P, DV], F32, name="result")
         nc.scalar.activation(result[:], acc[:], ACT.Copy, scale=inverse[:])
         nc.sync.dma_start(out[0], result[:])

@@ -28,6 +28,7 @@ PASSES = D // (P * PACK)
 SCALE_ROWS = 16
 KS_ROW0 = P - PASSES * SCALE_ROWS
 ZERO_PIECES = 8
+HALF = PAGE // 2
 
 
 def tile_attend_pkv4_rel2_cap_kernel(tc, qT, k_words, k_scales, v_words, v_scales, vs, offs, voffs, out):
@@ -40,21 +41,21 @@ def tile_attend_pkv4_rel2_cap_kernel(tc, qT, k_words, k_scales, v_words, v_scale
 
         slots = lists.tile([P, N // 16], U16, name="slots")
         vcols = lists.tile([P, PAGES * DV // 16], U16, name="vcols")
-        ks_pool = keep.tile([P, T], U8, name="ks_pool", align_bytes=64)
-        vs_pool = reused.tile([P, T], F32, name="vs_pool", align_bytes=64, offset=0)
+        ks_pool = reused.tile([P, T], U8, name="ks_pool", align_bytes=64, offset=0)
+        vs_pool = keep.tile([P, T], F32, name="vs_pool", align_bytes=64)
         q_raw = keep.tile([P, PASSES, PACK, NQ], F32, name="q_raw", align_bytes=64)
         kw_pool = keep.tile([P, T], I32, name="kw_pool", align_bytes=64)
         nc.sync.dma_start(slots[:], offs)
-        nc.scalar.dma_start(ks_pool[KS_ROW0:P, :].bitcast(I32), k_scales.rearrange("g f t -> (g f) t").bitcast(I32))
+        nc.scalar.dma_start(ks_pool[KS_ROW0:P, :].bitcast(I32), k_scales.rearrange("g f t -> f g t").bitcast(I32))
+        nc.scalar.dma_start(vs_pool[P - 1 : P, :], vs[0:1, :])
         nc.sync.dma_start(q_raw[:], qT[0].rearrange("(g p j) w -> p g j w", g=PASSES, j=PACK))
         nc.sync.dma_start(vcols[:], voffs)
-        nc.sync.dma_start(vs_pool[P - 1 : P, :], vs[0:1, :])
         nc.sync.dma_start(kw_pool[:], k_words[0].rearrange("p t b -> p (t b)").bitcast(I32))
 
-        sums = keep.tile([P, PAGES + 2], F32, name="sums")
-        nc.vector.memset(sums[:, PAGES + 1 : PAGES + 2], 1.0)
+        sums = keep.tile([P, 2 * PAGES + 1], F32, name="sums")
+        nc.vector.memset(sums[:, 2 * PAGES : 2 * PAGES + 1], 1.0)
         warm = keep.tile([P, 1], F32, name="warm")
-        nc.scalar.activation(warm[:], sums[:, PAGES + 1 : PAGES + 2], ACT.Tanh)
+        nc.scalar.activation(warm[:], sums[:, 2 * PAGES : 2 * PAGES + 1], ACT.Tanh)
         nc.vector.memset(ks_pool[0:KS_ROW0, :].bitcast(I32), 0)
         ks_planes = keep.tile([P, PASSES, N], U8, name="ks_planes", align_bytes=64)
         nc.vector.memset(ks_planes[:].bitcast(I32), 0)
@@ -67,24 +68,16 @@ def tile_attend_pkv4_rel2_cap_kernel(tc, qT, k_words, k_scales, v_words, v_scale
 
         ks_listed = keep.tile([P, N], U8, name="ks_listed", align_bytes=64)
         nc.vector.tensor_copy(ks_listed[:], ks_pool[:].indirect(slots[:]))
-        for g in range(PASSES):
-            for r in range(4):
-                row0 = KS_ROW0 + g * SCALE_ROWS
-                queue = nc.gpsimd if (g, r) == (PASSES - 1, 3) else nc.scalar
-                queue.dma_start(
-                    ks_planes[r:P:32, g, :].bitcast(I32), ks_listed[row0 + r : row0 + SCALE_ROWS : 4, :].bitcast(I32)
-                )
+        for quadrant in (0, 2, 1, 3):
+            row0 = KS_ROW0 + 4 * PASSES * quadrant
+            queue = nc.sync if quadrant < 2 else nc.scalar
+            queue.dma_start(
+                ks_planes[32 * quadrant : 32 * quadrant + 4, :, :].bitcast(I32),
+                ks_listed[row0 : row0 + 4 * PASSES, :].bitcast(I32),
+            )
 
         for c in range(ZERO_PIECES):
             nc.vector.memset(vs_pool[0 : P - 1, c * T // ZERO_PIECES : (c + 1) * T // ZERO_PIECES], 0.0)
-        vs_listed = keep.tile([P, N], F32, name="vs_listed", align_bytes=64)
-        nc.vector.tensor_copy(vs_listed[:], vs_pool[:].indirect(slots[:]))
-        vs_turned = [keep.tile([P, PACK], F32, name="vs_turned%d" % e) for e in range(PAGES)]
-        for e in range(PAGES):
-            nc.sync.dma_start(
-                vs_turned[e][:],
-                vs_listed[P - 1 : P, e * PAGE : (e + 1) * PAGE].rearrange("o (s t) -> o s t", t=PACK),
-            )
 
         q_codes = keep.tile([P, PASSES * NQ], U32, name="q_codes", align_bytes=64)
         q_scales = keep.tile([P, PASSES * NQ], U8, name="q_scales", align_bytes=64)
@@ -92,37 +85,33 @@ def tile_attend_pkv4_rel2_cap_kernel(tc, qT, k_words, k_scales, v_words, v_scale
             out=q_codes[:].bitcast(FP8X4), scales=q_scales[:], in_=q_bf[:].rearrange("p g w j -> p (g w j)")
         )
 
-        vw_pool = reused.tile([P, POOL_PAGES * DV], I32, name="vw_pool", align_bytes=64, offset=0)
-        nc.sync.dma_start(
-            vw_pool[:].rearrange("p (u e) -> p u e", u=POOL_PAGES),
-            v_words.rearrange("u p e r -> p u (e r)").bitcast(I32),
-        )
-        vsc_pool = reused.tile([P, POOL_PAGES * DV], U8, name="vsc_pool", align_bytes=64, offset=4 * POOL_PAGES * DV)
-        nc.vector.memset(vsc_pool[:].bitcast(I32), 0)
-        vsc_rows = v_scales.rearrange("u (q r) e -> r q u e", r=4)
-        for r in range(4):
-            nc.sync.dma_start(
-                vsc_pool[r:P:32, :].bitcast(I32).rearrange("q (u e) -> q u e", u=POOL_PAGES),
-                vsc_rows[r].bitcast(I32),
-            )
+        vs_turned = []
+
+        def token_scales(e):
+            listed = keep.tile([P, PAGE], F32, name="vs_listed%d" % e, tag="page%d" % ((e + PAGES) if e < 2 else e - 2), align_bytes=64)
+            nc.vector.tensor_copy(listed[:], vs_pool[:].indirect(slots[:, e * PAGE // 16 : (e + 1) * PAGE // 16]))
+            by_word = keep.tile([P, PACK], F32, name="vs_turned%d" % e)
+            nc.sync.dma_start(by_word[:], listed[P - 1 : P, :].rearrange("o (s t) -> o s t", t=PACK))
+            vs_turned.append(by_word)
 
         turned = []
-        piece = 0
-        for e in range(PAGES):
-            pairs = keep.tile([P, PAGE], U32, name="pairs%d" % e, align_bytes=64)
-            cols = slice(e * PAGE // 16, (e + 1) * PAGE // 16)
-            nc.vector.tensor_copy(pairs[:], kw_pool[:].bitcast(U32).indirect(slots[:, cols]))
-            weights = keep.tile([P, PACK, P], F32, name="weights%d" % e)
+
+        def weigh(e):
+            pairs = keep.tile([P, PAGE], U32, name="pairs%d" % e, tag="page%d" % e, align_bytes=64)
+            nc.vector.tensor_copy(
+                pairs[:], kw_pool[:].bitcast(U32).indirect(slots[:, e * PAGE // 16 : (e + 1) * PAGE // 16])
+            )
             parts = 2 if e == 0 else 1
             width = PAGE // parts
             step = PAGE if parts == 1 else P
+            halves = []
             for h in range(parts):
-                keys = keep.tile([P, PASSES, 2 * width], U8, name="keys%d" % piece, align_bytes=64)
+                keys = keep.tile([P, PASSES, 2 * width], U8, name="keys%d_%d" % (e, h), align_bytes=64)
                 nc.vector.tensor_copy(
                     keys[:].bitcast(U16),
                     pairs[:, h * width : (h + 1) * width].bitcast(U16).rearrange("p (n g) -> p g n", g=PASSES),
                 )
-                scores = psum.tile([P, width], F32, name="scores%d" % piece, tag="scores%d" % (piece % 4))
+                scores = psum.tile([P, width], F32, name="scores%d_%d" % (e, h), tag="scores%d" % ((e + h + (e > 0)) % 4))
                 for n0 in range(0, width, step):
                     slot0 = e * PAGE + h * width + n0
                     for g in range(PASSES):
@@ -135,21 +124,48 @@ def tile_attend_pkv4_rel2_cap_kernel(tc, qT, k_words, k_scales, v_words, v_scale
                             start=(g == 0),
                             stop=(g == PASSES - 1),
                         )
-                rows = width // PACK
-                capped = keep.tile([P, PACK, rows], F32, name="capped%d" % piece)
-                nc.scalar.activation(capped[:], scores[:].rearrange("q (s t) -> q t s", t=PACK), ACT.Tanh, scale=1.0 / CAP)
-                positive = keep.tile([P, PACK, rows], F32, name="positive%d" % piece)
-                nc.scalar.activation(positive[:], capped[:], ACT.Relu)
+                for n0 in range(0, width, HALF):
+                    halves.append(scores[:, n0 : n0 + HALF])
+            rows = HALF // PACK
+            capped = [keep.tile([P, PACK, rows], F32, name="capped%d_%d" % (e, h)) for h in range(2)]
+            positive = [keep.tile([P, PACK, rows], F32, name="positive%d_%d" % (e, h)) for h in range(2)]
+            weights = keep.tile([P, PACK, P], F32, name="weights%d" % e)
+            for h in range(2):
+                nc.scalar.activation(capped[h][:], halves[h].rearrange("q (s t) -> q t s", t=PACK), ACT.Tanh, scale=1.0 / CAP)
+            for h in range(2):
+                nc.scalar.activation(positive[h][:], capped[h][:], ACT.Relu)
+            for h in range(2):
                 nc.scalar.activation(
-                    weights[:, :, h * rows : (h + 1) * rows], positive[:], ACT.Square, scale=CAP,
-                    accum_out=sums[:, piece : piece + 1],
+                    weights[:, :, h * rows : (h + 1) * rows], positive[h][:], ACT.Square, scale=CAP,
+                    accum_out=sums[:, 2 * e + h : 2 * e + h + 1],
                 )
-                piece += 1
             bank = psum.tile([P, PACK, NQ], F32, name="turned%d" % e, tag="turned%d" % e if e < PAGES - 1 else "scores1")
             for t in range(PACK):
                 nc.tensor.transpose(bank[:, t, :], weights[:, t, :], identity[:])
             turned.append(bank)
 
+        token_scales(0)
+        token_scales(1)
+        weigh(0)
+        weigh(1)
+        token_scales(2)
+        weigh(2)
+        token_scales(3)
+        weigh(3)
+
+        vw_pool = reused.tile([P, POOL_PAGES * DV], I32, name="vw_pool", align_bytes=64, offset=POOL_PAGES * DV)
+        nc.sync.dma_start(
+            vw_pool[:].rearrange("p (u e) -> p u e", u=POOL_PAGES),
+            v_words.rearrange("u p e r -> p u (e r)").bitcast(I32),
+        )
+        vsc_pool = reused.tile([P, POOL_PAGES * DV], U8, name="vsc_pool", align_bytes=64, offset=0)
+        nc.vector.memset(vsc_pool[:].bitcast(I32), 0)
+        vsc_rows = v_scales.rearrange("u (q r) e -> r q u e", r=4)
+        for r in range(4):
+            nc.sync.dma_start(
+                vsc_pool[r:P:32, :].bitcast(I32).rearrange("q (u e) -> q u e", u=POOL_PAGES),
+                vsc_rows[r].bitcast(I32),
+            )
         vw = keep.tile([P, PAGES * DV], U32, name="vw", align_bytes=64)
         vsc = keep.tile([P, PAGES * DV], U8, name="vsc", align_bytes=64)
         nc.vector.tensor_copy(vw[:], vw_pool[:].bitcast(U32).indirect(vcols[:]))
@@ -161,18 +177,24 @@ def tile_attend_pkv4_rel2_cap_kernel(tc, qT, k_words, k_scales, v_words, v_scale
             if e == PAGES - 1:
                 nc.vector.tensor_reduce(denom[:], sums[:], axis=AX.X, op=ALU.add)
                 nc.vector.reciprocal(inverse[:], denom[:])
+            cuts = 2 if e == PAGES - 1 else 1
+            rows = NQ // cuts
             w_bf = keep.tile([P, NQ, PACK], BF16, name="w_bf%d" % e, align_bytes=64)
-            nc.vector.tensor_tensor(
-                w_bf[:],
-                turned[e][:].rearrange("s t q -> s q t"),
-                vs_turned[e][:].unsqueeze(1).to_broadcast([P, NQ, PACK]),
-                ALU.mult,
-            )
+            for c in range(cuts):
+                nc.vector.tensor_tensor(
+                    w_bf[:, c * rows : (c + 1) * rows, :],
+                    turned[e][:, :, c * rows : (c + 1) * rows].rearrange("s t q -> s q t"),
+                    vs_turned[e][:].unsqueeze(1).to_broadcast([P, rows, PACK]),
+                    ALU.mult,
+                )
             w_codes = keep.tile([P, NQ], U32, name="w_codes%d" % e, align_bytes=64)
             w_scales = keep.tile([P, NQ], U8, name="w_scales%d" % e, align_bytes=64)
-            nc.vector.quantize_mx(
-                out=w_codes[:].bitcast(FP8X4), scales=w_scales[:], in_=w_bf[:].rearrange("s q t -> s (q t)")
-            )
+            for c in range(cuts):
+                nc.vector.quantize_mx(
+                    out=w_codes[:, c * rows : (c + 1) * rows].bitcast(FP8X4),
+                    scales=w_scales[:, c * rows : (c + 1) * rows],
+                    in_=w_bf[:, c * rows : (c + 1) * rows, :].rearrange("s q t -> s (q t)"),
+                )
             nc.tensor.matmul_mx(
                 out=acc[:],
                 lhsT=w_codes[:].bitcast(FP8X4),

@@ -27,8 +27,11 @@ POOL_PAGES = T // PAGE
 PASSES = D // (P * PACK)
 SCALE_ROWS = 16
 KS_ROW0 = P - PASSES * SCALE_ROWS
-ZERO_PIECES = 8
 HALF = PAGE // 2
+RUN = T // P
+BANKS = 8
+SLOT_BYTES = 4 * PAGE
+WORK_SLOTS = 8
 
 
 def tile_attend_pkv4_rel2_cap_kernel(tc, qT, k_words, k_scales, v_words, v_scales, vs, offs, voffs, out):
@@ -37,20 +40,22 @@ def tile_attend_pkv4_rel2_cap_kernel(tc, qT, k_words, k_scales, v_words, v_scale
         lists = ctx.enter_context(tc.tile_pool(name="lists", bufs=1))
         keep = ctx.enter_context(tc.tile_pool(name="keep", bufs=1))
         reused = ctx.enter_context(tc.tile_pool(name="reused", bufs=1))
+        work = ctx.enter_context(tc.tile_pool(name="work", bufs=1))
         psum = ctx.enter_context(tc.psum_pool(name="psum", bufs=1))
 
         slots = lists.tile([P, N // 16], U16, name="slots")
         vcols = lists.tile([P, PAGES * DV // 16], U16, name="vcols")
         ks_pool = reused.tile([P, T], U8, name="ks_pool", align_bytes=64, offset=0)
+        vs_runs = work.tile([P, RUN], F32, name="vs_runs", align_bytes=64, offset=0)
         vs_pool = keep.tile([P, T], F32, name="vs_pool", align_bytes=64)
         q_raw = keep.tile([P, PASSES, PACK, NQ], F32, name="q_raw", align_bytes=64)
         kw_pool = keep.tile([P, T], I32, name="kw_pool", align_bytes=64)
         nc.sync.dma_start(slots[:], offs)
         nc.scalar.dma_start(ks_pool[KS_ROW0:P, :].bitcast(I32), k_scales.rearrange("g f t -> f g t").bitcast(I32))
-        nc.scalar.dma_start(vs_pool[P - 1 : P, :], vs[0:1, :])
+        nc.sync.dma_start(vs_runs[:], vs[0].rearrange("(p c) -> p c", c=RUN))
+        nc.sync.dma_start(kw_pool[:], k_words[0].rearrange("p t b -> p (t b)").bitcast(I32))
         nc.sync.dma_start(q_raw[:], qT[0].rearrange("(g p j) w -> p g j w", g=PASSES, j=PACK))
         nc.sync.dma_start(vcols[:], voffs)
-        nc.sync.dma_start(kw_pool[:], k_words[0].rearrange("p t b -> p (t b)").bitcast(I32))
 
         sums = keep.tile([P, 2 * PAGES + 1], F32, name="sums")
         nc.vector.memset(sums[:, 2 * PAGES : 2 * PAGES + 1], 1.0)
@@ -62,64 +67,76 @@ def tile_attend_pkv4_rel2_cap_kernel(tc, qT, k_words, k_scales, v_words, v_scale
         identity = keep.tile([P, P], F32, name="identity")
         make_identity(nc, identity[:])
 
-        q_bf = keep.tile([P, PASSES, NQ, PACK], BF16, name="q_bf", align_bytes=64)
+        vs_by_run = vs_pool[:].rearrange("i (p c) -> i p c", c=RUN)
+        for b in range(RUN // PACK):
+            spread = psum.tile([P, PACK, P], F32, name="spread%d" % b, tag="bank%d" % (b % BANKS))
+            for c in range(PACK):
+                column = b * PACK + c
+                nc.tensor.transpose(spread[:, c, :], vs_runs[:, column : column + 1].to_broadcast([P, P]), identity[:])
+            nc.scalar.copy(vs_by_run[:, :, b * PACK : (b + 1) * PACK], spread[:].rearrange("i c p -> i p c"))
+
+        q_area = work.tile([P, WORK_SLOTS * SLOT_BYTES // 2], BF16, name="q_area", align_bytes=64, offset=0)
+        q_flat = q_area[:, 0 : PASSES * NQ * PACK]
+        q_bf = q_flat.rearrange("p (g w j) -> p g w j", g=PASSES, j=PACK)
         for g in range(PASSES):
             nc.scalar.copy(q_bf[:, g], q_raw[:, g].rearrange("p j w -> p w j"))
 
         ks_listed = keep.tile([P, N], U8, name="ks_listed", align_bytes=64)
         nc.vector.tensor_copy(ks_listed[:], ks_pool[:].indirect(slots[:]))
-        for quadrant in (0, 2, 1, 3):
+        for quadrant in range(4):
             row0 = KS_ROW0 + 4 * PASSES * quadrant
-            queue = nc.sync if quadrant < 2 else nc.scalar
-            queue.dma_start(
+            nc.sync.dma_start(
                 ks_planes[32 * quadrant : 32 * quadrant + 4, :, :].bitcast(I32),
                 ks_listed[row0 : row0 + 4 * PASSES, :].bitcast(I32),
             )
 
-        for c in range(ZERO_PIECES):
-            nc.vector.memset(vs_pool[0 : P - 1, c * T // ZERO_PIECES : (c + 1) * T // ZERO_PIECES], 0.0)
-
         q_codes = keep.tile([P, PASSES * NQ], U32, name="q_codes", align_bytes=64)
         q_scales = keep.tile([P, PASSES * NQ], U8, name="q_scales", align_bytes=64)
-        nc.vector.quantize_mx(
-            out=q_codes[:].bitcast(FP8X4), scales=q_scales[:], in_=q_bf[:].rearrange("p g w j -> p (g w j)")
-        )
+        pairs = {}
+        keys = {}
+        vs_turned = {}
+        turned = {}
+        w_bf = {}
+        SCORE_BANKS = ((0, 1), (2,), (0,), (3,))
+        TURN_BANKS = (3, 4, 5, 1)
 
-        vs_turned = []
+        def gather_keys(e):
+            if e < 2:
+                pairs[e] = keep.tile([P, PAGE], U32, name="pairs%d" % e, align_bytes=64)
+            else:
+                pairs[e] = work.tile([P, PAGE], U32, name="pairs%d" % e, align_bytes=64, offset=(e - 2) * SLOT_BYTES)
+            nc.vector.tensor_copy(
+                pairs[e][:], kw_pool[:].bitcast(U32).indirect(slots[:, e * PAGE // 16 : (e + 1) * PAGE // 16])
+            )
+
+        def part_keys(e):
+            keys[e] = keep.tile([P, PASSES, 2 * PAGE], U8, name="keys%d" % e, align_bytes=64)
+            nc.vector.tensor_copy(
+                keys[e][:].bitcast(U16), pairs[e][:].bitcast(U16).rearrange("p (n g) -> p g n", g=PASSES)
+            )
 
         def token_scales(e):
-            listed = keep.tile([P, PAGE], F32, name="vs_listed%d" % e, tag="page%d" % ((e + PAGES) if e < 2 else e - 2), align_bytes=64)
+            listed = work.tile([P, PAGE], F32, name="vs_listed%d" % e, align_bytes=64, offset=(2 + e) * SLOT_BYTES)
             nc.vector.tensor_copy(listed[:], vs_pool[:].indirect(slots[:, e * PAGE // 16 : (e + 1) * PAGE // 16]))
-            by_word = keep.tile([P, PACK], F32, name="vs_turned%d" % e)
-            nc.sync.dma_start(by_word[:], listed[P - 1 : P, :].rearrange("o (s t) -> o s t", t=PACK))
-            vs_turned.append(by_word)
-
-        turned = []
+            vs_turned[e] = keep.tile([P, PACK], F32, name="vs_turned%d" % e)
+            nc.sync.dma_start(vs_turned[e][:], listed[0:1, :].rearrange("o (s t) -> o s t", t=PACK))
 
         def weigh(e):
-            pairs = keep.tile([P, PAGE], U32, name="pairs%d" % e, tag="page%d" % e, align_bytes=64)
-            nc.vector.tensor_copy(
-                pairs[:], kw_pool[:].bitcast(U32).indirect(slots[:, e * PAGE // 16 : (e + 1) * PAGE // 16])
-            )
-            parts = 2 if e == 0 else 1
+            parts = len(SCORE_BANKS[e])
             width = PAGE // parts
             step = PAGE if parts == 1 else P
             halves = []
             for h in range(parts):
-                keys = keep.tile([P, PASSES, 2 * width], U8, name="keys%d_%d" % (e, h), align_bytes=64)
-                nc.vector.tensor_copy(
-                    keys[:].bitcast(U16),
-                    pairs[:, h * width : (h + 1) * width].bitcast(U16).rearrange("p (n g) -> p g n", g=PASSES),
-                )
-                scores = psum.tile([P, width], F32, name="scores%d_%d" % (e, h), tag="scores%d" % ((e + h + (e > 0)) % 4))
+                scores = psum.tile([P, width], F32, name="scores%d_%d" % (e, h), tag="bank%d" % SCORE_BANKS[e][h])
                 for n0 in range(0, width, step):
-                    slot0 = e * PAGE + h * width + n0
+                    col0 = h * width + n0
+                    slot0 = e * PAGE + col0
                     for g in range(PASSES):
                         nc.tensor.matmul_mx(
                             out=scores[:, n0 : n0 + step],
                             lhsT=q_codes[:, g * NQ : (g + 1) * NQ].bitcast(FP8X4),
                             lhsT_scale=q_scales[:, g * NQ : (g + 1) * NQ],
-                            rhs=keys[:, g, 2 * n0 : 2 * (n0 + step)].bitcast(FP4X4),
+                            rhs=keys[e][:, g, 2 * col0 : 2 * (col0 + step)].bitcast(FP4X4),
                             rhs_scale=ks_planes[:, g, slot0 : slot0 + step],
                             start=(g == 0),
                             stop=(g == PASSES - 1),
@@ -139,19 +156,48 @@ def tile_attend_pkv4_rel2_cap_kernel(tc, qT, k_words, k_scales, v_words, v_scale
                     weights[:, :, h * rows : (h + 1) * rows], positive[h][:], ACT.Square, scale=CAP,
                     accum_out=sums[:, 2 * e + h : 2 * e + h + 1],
                 )
-            bank = psum.tile([P, PACK, NQ], F32, name="turned%d" % e, tag="turned%d" % e if e < PAGES - 1 else "scores1")
+            turned[e] = psum.tile([P, PACK, NQ], F32, name="turned%d" % e, tag="bank%d" % TURN_BANKS[e])
             for t in range(PACK):
-                nc.tensor.transpose(bank[:, t, :], weights[:, t, :], identity[:])
-            turned.append(bank)
+                nc.tensor.transpose(turned[e][:, t, :], weights[:, t, :], identity[:])
 
+        def scale_on_vector(e):
+            w_bf[e] = keep.tile([P, NQ, PACK], BF16, name="w_bf%d" % e, align_bytes=64)
+            nc.vector.tensor_tensor(
+                w_bf[e][:],
+                turned[e][:].rearrange("s t q -> s q t"),
+                vs_turned[e][:].unsqueeze(1).to_broadcast([P, NQ, PACK]),
+                ALU.mult,
+            )
+
+        def scale_on_scalar(e):
+            by_place = keep.tile([P, PACK, NQ], BF16, name="by_place%d" % e, align_bytes=64)
+            for t in range(PACK):
+                nc.scalar.activation(by_place[:, t, :], turned[e][:, t, :], ACT.Copy, scale=vs_turned[e][:, t : t + 1])
+            w_bf[e] = keep.tile([P, NQ, PACK], BF16, name="w_bf%d" % e, align_bytes=64)
+            nc.scalar.copy(w_bf[e][:], by_place[:].rearrange("s t q -> s q t"))
+
+        gather_keys(0)
+        part_keys(0)
+        gather_keys(1)
+        nc.vector.quantize_mx(
+            out=q_codes[:].bitcast(FP8X4), scales=q_scales[:], in_=q_flat
+        )
+        part_keys(1)
         token_scales(0)
-        token_scales(1)
         weigh(0)
         weigh(1)
-        token_scales(2)
+        scale_on_scalar(0)
+        gather_keys(2)
+        part_keys(2)
+        token_scales(1)
         weigh(2)
+        gather_keys(3)
+        part_keys(3)
+        token_scales(2)
         token_scales(3)
         weigh(3)
+        scale_on_scalar(1)
+        scale_on_scalar(2)
 
         vw_pool = reused.tile([P, POOL_PAGES * DV], I32, name="vw_pool", align_bytes=64, offset=POOL_PAGES * DV)
         nc.sync.dma_start(
@@ -166,43 +212,34 @@ def tile_attend_pkv4_rel2_cap_kernel(tc, qT, k_words, k_scales, v_words, v_scale
                 vsc_pool[r:P:32, :].bitcast(I32).rearrange("q (u e) -> q u e", u=POOL_PAGES),
                 vsc_rows[r].bitcast(I32),
             )
-        vw = keep.tile([P, PAGES * DV], U32, name="vw", align_bytes=64)
-        vsc = keep.tile([P, PAGES * DV], U8, name="vsc", align_bytes=64)
+        vw = work.tile([P, PAGES * DV], U32, name="vw", align_bytes=64, offset=6 * SLOT_BYTES)
+        vsc = work.tile([P, PAGES * DV], U8, name="vsc", align_bytes=64, offset=7 * SLOT_BYTES)
         nc.vector.tensor_copy(vw[:], vw_pool[:].bitcast(U32).indirect(vcols[:]))
         nc.vector.tensor_copy(vsc[:], vsc_pool[:].indirect(vcols[:]))
-        acc = psum.tile([P, DV], F32, name="acc")
+        acc = psum.tile([P, DV], F32, name="acc", tag="bank7")
         denom = keep.tile([P, 1], F32, name="denom")
         inverse = keep.tile([P, 1], F32, name="inverse")
-        for e in range(PAGES):
+        order = (0, 1, 3, 2)
+        for e in order:
             if e == PAGES - 1:
+                scale_on_vector(e)
                 nc.vector.tensor_reduce(denom[:], sums[:], axis=AX.X, op=ALU.add)
                 nc.vector.reciprocal(inverse[:], denom[:])
-            cuts = 2 if e == PAGES - 1 else 1
-            rows = NQ // cuts
-            w_bf = keep.tile([P, NQ, PACK], BF16, name="w_bf%d" % e, align_bytes=64)
-            for c in range(cuts):
-                nc.vector.tensor_tensor(
-                    w_bf[:, c * rows : (c + 1) * rows, :],
-                    turned[e][:, :, c * rows : (c + 1) * rows].rearrange("s t q -> s q t"),
-                    vs_turned[e][:].unsqueeze(1).to_broadcast([P, rows, PACK]),
-                    ALU.mult,
-                )
             w_codes = keep.tile([P, NQ], U32, name="w_codes%d" % e, align_bytes=64)
             w_scales = keep.tile([P, NQ], U8, name="w_scales%d" % e, align_bytes=64)
-            for c in range(cuts):
-                nc.vector.quantize_mx(
-                    out=w_codes[:, c * rows : (c + 1) * rows].bitcast(FP8X4),
-                    scales=w_scales[:, c * rows : (c + 1) * rows],
-                    in_=w_bf[:, c * rows : (c + 1) * rows, :].rearrange("s q t -> s (q t)"),
-                )
+            nc.vector.quantize_mx(
+                out=w_codes[:].bitcast(FP8X4),
+                scales=w_scales[:],
+                in_=w_bf[e][:].rearrange("s q t -> s (q t)"),
+            )
             nc.tensor.matmul_mx(
                 out=acc[:],
                 lhsT=w_codes[:].bitcast(FP8X4),
                 lhsT_scale=w_scales[:],
                 rhs=vw[:, e * DV : (e + 1) * DV].bitcast(FP8X4),
                 rhs_scale=vsc[:, e * DV : (e + 1) * DV],
-                start=(e == 0),
-                stop=(e == PAGES - 1),
+                start=(e == order[0]),
+                stop=(e == order[-1]),
             )
 
         result = keep.tile([P, DV], F32, name="result")

@@ -97,11 +97,11 @@ def tile_attend_pkv4_rel2_cap_kernel(tc, qT, k_words, k_scales, v_words, v_scale
         vs_turned = {}
         turned = {}
         w_bf = {}
-        SCORE_BANKS = ((0, 1), (2,), (0,), (3,))
-        TURN_BANKS = (3, 4, 5, 1)
+        SCORE_BANKS = ((0, 1), (2,), (3,), (0,))
+        TURN_BANKS = (4, 5, 6, 1)
 
         def gather_keys(e):
-            if e < 2:
+            if e < 3:
                 pairs[e] = keep.tile([P, PAGE], U32, name="pairs%d" % e, align_bytes=64)
             else:
                 pairs[e] = work.tile([P, PAGE], U32, name="pairs%d" % e, align_bytes=64, offset=(e - 2) * SLOT_BYTES)
@@ -169,35 +169,20 @@ def tile_attend_pkv4_rel2_cap_kernel(tc, qT, k_words, k_scales, v_words, v_scale
                 ALU.mult,
             )
 
-        def scale_on_scalar(e):
-            by_place = keep.tile([P, PACK, NQ], BF16, name="by_place%d" % e, align_bytes=64)
-            for t in range(PACK):
-                nc.scalar.activation(by_place[:, t, :], turned[e][:, t, :], ACT.Copy, scale=vs_turned[e][:, t : t + 1])
-            w_bf[e] = keep.tile([P, NQ, PACK], BF16, name="w_bf%d" % e, align_bytes=64)
-            nc.scalar.copy(w_bf[e][:], by_place[:].rearrange("s t q -> s q t"))
-
         gather_keys(0)
         part_keys(0)
         gather_keys(1)
+        part_keys(1)
+        gather_keys(2)
+        part_keys(2)
         nc.vector.quantize_mx(
             out=q_codes[:].bitcast(FP8X4), scales=q_scales[:], in_=q_flat
         )
-        part_keys(1)
-        token_scales(0)
-        weigh(0)
-        weigh(1)
-        scale_on_scalar(0)
-        gather_keys(2)
-        part_keys(2)
-        token_scales(1)
-        weigh(2)
         gather_keys(3)
         part_keys(3)
-        token_scales(2)
-        token_scales(3)
-        weigh(3)
-        scale_on_scalar(1)
-        scale_on_scalar(2)
+        for e in range(PAGES):
+            token_scales(e)
+            weigh(e)
 
         vw_pool = reused.tile([P, POOL_PAGES * DV], I32, name="vw_pool", align_bytes=64, offset=POOL_PAGES * DV)
         nc.sync.dma_start(
@@ -219,10 +204,10 @@ def tile_attend_pkv4_rel2_cap_kernel(tc, qT, k_words, k_scales, v_words, v_scale
         acc = psum.tile([P, DV], F32, name="acc", tag="bank7")
         denom = keep.tile([P, 1], F32, name="denom")
         inverse = keep.tile([P, 1], F32, name="inverse")
-        order = (0, 1, 3, 2)
+        order = (0, 1, 2, 3)
         for e in order:
+            scale_on_vector(e)
             if e == PAGES - 1:
-                scale_on_vector(e)
                 nc.vector.tensor_reduce(denom[:], sums[:], axis=AX.X, op=ALU.add)
                 nc.vector.reciprocal(inverse[:], denom[:])
             w_codes = keep.tile([P, NQ], U32, name="w_codes%d" % e, align_bytes=64)

@@ -28,7 +28,9 @@ PASSES = D // (P * PACK)
 SCALE_ROWS = 16
 KS_ROW0 = P - PASSES * SCALE_ROWS
 HALF = PAGE // 2
-RUN = T // P
+SPREAD = T // 2
+RUN = SPREAD // P
+ZERO_PIECES = 2
 BANKS = 8
 SLOT_BYTES = 4 * PAGE
 WORK_SLOTS = 8
@@ -52,9 +54,10 @@ def tile_attend_pkv4_rel2_cap_kernel(tc, qT, k_words, k_scales, v_words, v_scale
         kw_pool = keep.tile([P, T], I32, name="kw_pool", align_bytes=64)
         nc.sync.dma_start(slots[:], offs)
         nc.scalar.dma_start(ks_pool[KS_ROW0:P, :].bitcast(I32), k_scales.rearrange("g f t -> f g t").bitcast(I32))
-        nc.sync.dma_start(vs_runs[:], vs[0].rearrange("(p c) -> p c", c=RUN))
-        nc.sync.dma_start(kw_pool[:], k_words[0].rearrange("p t b -> p (t b)").bitcast(I32))
+        nc.sync.dma_start(vs_runs[:], vs[0, 0:SPREAD].rearrange("(p c) -> p c", c=RUN))
+        nc.scalar.dma_start(vs_pool[P - 1 : P, SPREAD:T], vs[0:1, SPREAD:T])
         nc.sync.dma_start(q_raw[:], qT[0].rearrange("(g p j) w -> p g j w", g=PASSES, j=PACK))
+        nc.sync.dma_start(kw_pool[:], k_words[0].rearrange("p t b -> p (t b)").bitcast(I32))
         nc.sync.dma_start(vcols[:], voffs)
 
         sums = keep.tile([P, 2 * PAGES + 1], F32, name="sums")
@@ -64,10 +67,11 @@ def tile_attend_pkv4_rel2_cap_kernel(tc, qT, k_words, k_scales, v_words, v_scale
         nc.vector.memset(ks_pool[0:KS_ROW0, :].bitcast(I32), 0)
         ks_planes = keep.tile([P, PASSES, N], U8, name="ks_planes", align_bytes=64)
         nc.vector.memset(ks_planes[:].bitcast(I32), 0)
+        nc.vector.memset(vs_pool[0 : P - 1, SPREAD:T], 0.0)
         identity = keep.tile([P, P], F32, name="identity")
         make_identity(nc, identity[:])
 
-        vs_by_run = vs_pool[:].rearrange("i (p c) -> i p c", c=RUN)
+        vs_by_run = vs_pool[:, 0:SPREAD].rearrange("i (p c) -> i p c", c=RUN)
         for b in range(RUN // PACK):
             spread = psum.tile([P, PACK, P], F32, name="spread%d" % b, tag="bank%d" % (b % BANKS))
             for c in range(PACK):
@@ -75,7 +79,7 @@ def tile_attend_pkv4_rel2_cap_kernel(tc, qT, k_words, k_scales, v_words, v_scale
                 nc.tensor.transpose(spread[:, c, :], vs_runs[:, column : column + 1].to_broadcast([P, P]), identity[:])
             nc.scalar.copy(vs_by_run[:, :, b * PACK : (b + 1) * PACK], spread[:].rearrange("i c p -> i p c"))
 
-        q_area = work.tile([P, WORK_SLOTS * SLOT_BYTES // 2], BF16, name="q_area", align_bytes=64, offset=0)
+        q_area = work.tile([P, PAGES * SLOT_BYTES // 2], BF16, name="q_area", align_bytes=64, offset=0)
         q_flat = q_area[:, 0 : PASSES * NQ * PACK]
         q_bf = q_flat.rearrange("p (g w j) -> p g w j", g=PASSES, j=PACK)
         for g in range(PASSES):
@@ -101,25 +105,36 @@ def tile_attend_pkv4_rel2_cap_kernel(tc, qT, k_words, k_scales, v_words, v_scale
         TURN_BANKS = (4, 5, 6, 1)
 
         def gather_keys(e):
-            if e < 3:
-                pairs[e] = keep.tile([P, PAGE], U32, name="pairs%d" % e, align_bytes=64)
+            if e == 0:
+                area = work.tile([P, 3 * PAGE], U32, name="first_pairs", align_bytes=64, offset=3 * SLOT_BYTES)
+                pairs[e] = area[:, 0:PAGE]
             else:
-                pairs[e] = work.tile([P, PAGE], U32, name="pairs%d" % e, align_bytes=64, offset=(e - 2) * SLOT_BYTES)
+                own = work.tile([P, PAGE], U32, name="pairs%d" % e, align_bytes=64, offset=(e - 1) * SLOT_BYTES)
+                pairs[e] = own[:]
             nc.vector.tensor_copy(
-                pairs[e][:], kw_pool[:].bitcast(U32).indirect(slots[:, e * PAGE // 16 : (e + 1) * PAGE // 16])
+                pairs[e], kw_pool[:].bitcast(U32).indirect(slots[:, e * PAGE // 16 : (e + 1) * PAGE // 16])
             )
 
         def part_keys(e):
-            keys[e] = keep.tile([P, PASSES, 2 * PAGE], U8, name="keys%d" % e, align_bytes=64)
-            nc.vector.tensor_copy(
-                keys[e][:].bitcast(U16), pairs[e][:].bitcast(U16).rearrange("p (n g) -> p g n", g=PASSES)
-            )
+            parts = len(SCORE_BANKS[e])
+            width = PAGE // parts
+            keys[e] = []
+            for h in range(parts):
+                part = keep.tile([P, PASSES, 2 * width], U8, name="keys%d_%d" % (e, h), align_bytes=64)
+                nc.vector.tensor_copy(
+                    part[:].bitcast(U16),
+                    pairs[e][:, h * width : (h + 1) * width].bitcast(U16).rearrange("p (n g) -> p g n", g=PASSES),
+                )
+                keys[e].append(part)
 
         def token_scales(e):
-            listed = work.tile([P, PAGE], F32, name="vs_listed%d" % e, align_bytes=64, offset=(2 + e) * SLOT_BYTES)
+            if e < PAGES - 1:
+                listed = keep.tile([P, PAGE], F32, name="vs_listed%d" % e, align_bytes=64)
+            else:
+                listed = work.tile([P, PAGE], F32, name="vs_listed%d" % e, align_bytes=64, offset=3 * SLOT_BYTES)
             nc.vector.tensor_copy(listed[:], vs_pool[:].indirect(slots[:, e * PAGE // 16 : (e + 1) * PAGE // 16]))
             vs_turned[e] = keep.tile([P, PACK], F32, name="vs_turned%d" % e)
-            nc.sync.dma_start(vs_turned[e][:], listed[0:1, :].rearrange("o (s t) -> o s t", t=PACK))
+            nc.sync.dma_start(vs_turned[e][:], listed[P - 1 : P, :].rearrange("o (s t) -> o s t", t=PACK))
 
         def weigh(e):
             parts = len(SCORE_BANKS[e])
@@ -136,7 +151,7 @@ def tile_attend_pkv4_rel2_cap_kernel(tc, qT, k_words, k_scales, v_words, v_scale
                             out=scores[:, n0 : n0 + step],
                             lhsT=q_codes[:, g * NQ : (g + 1) * NQ].bitcast(FP8X4),
                             lhsT_scale=q_scales[:, g * NQ : (g + 1) * NQ],
-                            rhs=keys[e][:, g, 2 * col0 : 2 * (col0 + step)].bitcast(FP4X4),
+                            rhs=keys[e][h][:, g, 2 * n0 : 2 * (n0 + step)].bitcast(FP4X4),
                             rhs_scale=ks_planes[:, g, slot0 : slot0 + step],
                             start=(g == 0),
                             stop=(g == PASSES - 1),
@@ -169,20 +184,17 @@ def tile_attend_pkv4_rel2_cap_kernel(tc, qT, k_words, k_scales, v_words, v_scale
                 ALU.mult,
             )
 
-        gather_keys(0)
-        part_keys(0)
-        gather_keys(1)
-        part_keys(1)
-        gather_keys(2)
-        part_keys(2)
+        token_scales(0)
+        token_scales(1)
         nc.vector.quantize_mx(
             out=q_codes[:].bitcast(FP8X4), scales=q_scales[:], in_=q_flat
         )
-        gather_keys(3)
-        part_keys(3)
+        token_scales(2)
         for e in range(PAGES):
-            token_scales(e)
+            gather_keys(e)
+            part_keys(e)
             weigh(e)
+        token_scales(3)
 
         vw_pool = reused.tile([P, POOL_PAGES * DV], I32, name="vw_pool", align_bytes=64, offset=POOL_PAGES * DV)
         nc.sync.dma_start(
@@ -197,8 +209,8 @@ def tile_attend_pkv4_rel2_cap_kernel(tc, qT, k_words, k_scales, v_words, v_scale
                 vsc_pool[r:P:32, :].bitcast(I32).rearrange("q (u e) -> q u e", u=POOL_PAGES),
                 vsc_rows[r].bitcast(I32),
             )
-        vw = work.tile([P, PAGES * DV], U32, name="vw", align_bytes=64, offset=6 * SLOT_BYTES)
-        vsc = work.tile([P, PAGES * DV], U8, name="vsc", align_bytes=64, offset=7 * SLOT_BYTES)
+        vw = work.tile([P, PAGES * DV], U32, name="vw", align_bytes=64, offset=4 * SLOT_BYTES)
+        vsc = work.tile([P, PAGES * DV], U8, name="vsc", align_bytes=64, offset=5 * SLOT_BYTES)
         nc.vector.tensor_copy(vw[:], vw_pool[:].bitcast(U32).indirect(vcols[:]))
         nc.vector.tensor_copy(vsc[:], vsc_pool[:].indirect(vcols[:]))
         acc = psum.tile([P, DV], F32, name="acc", tag="bank7")

@@ -26,9 +26,10 @@ PAGES = N // PAGE
 POOL_PAGES = T // PAGE
 PASSES = D // (P * PACK)
 SCALE_ROWS = 16
+ON_VECTOR = 2
 KS_ROW0 = P - PASSES * SCALE_ROWS
 HALF = PAGE // 2
-SPREAD = T // 2
+SPREAD = 5 * PAGE
 RUN = SPREAD // P
 ZERO_PIECES = 2
 BANKS = 8
@@ -60,10 +61,10 @@ def tile_attend_pkv4_rel2_cap_kernel(tc, qT, k_words, k_scales, v_words, v_scale
         nc.sync.dma_start(kw_pool[:], k_words[0].rearrange("p t b -> p (t b)").bitcast(I32))
         nc.sync.dma_start(vcols[:], voffs)
 
-        sums = keep.tile([P, 2 * PAGES + 1], F32, name="sums")
-        nc.vector.memset(sums[:, 2 * PAGES : 2 * PAGES + 1], 1.0)
+        sums = keep.tile([P, 2 * PAGES], F32, name="sums")
+        nc.vector.memset(sums[:, 0:1], 1.0 / (CAP * CAP))
         warm = keep.tile([P, 1], F32, name="warm")
-        nc.scalar.activation(warm[:], sums[:, 2 * PAGES : 2 * PAGES + 1], ACT.Tanh)
+        nc.scalar.activation(warm[:], sums[:, 0:1], ACT.Tanh)
         nc.vector.memset(ks_pool[0:KS_ROW0, :].bitcast(I32), 0)
         ks_planes = keep.tile([P, PASSES, N], U8, name="ks_planes", align_bytes=64)
         nc.vector.memset(ks_planes[:].bitcast(I32), 0)
@@ -101,12 +102,12 @@ def tile_attend_pkv4_rel2_cap_kernel(tc, qT, k_words, k_scales, v_words, v_scale
         vs_turned = {}
         turned = {}
         w_bf = {}
-        SCORE_BANKS = ((0, 1), (2,), (3,), (0,))
-        TURN_BANKS = (4, 5, 6, 1)
+        SCORE_BANKS = ((0, 1), (2,), (3,), (4,))
+        TURN_BANKS = (5, 6, 0, 1)
 
         def gather_keys(e):
             if e == 0:
-                area = work.tile([P, 3 * PAGE], U32, name="first_pairs", align_bytes=64, offset=3 * SLOT_BYTES)
+                area = work.tile([P, 4 * PAGE], U32, name="first_pairs", align_bytes=64, offset=3 * SLOT_BYTES)
                 pairs[e] = area[:, 0:PAGE]
             else:
                 own = work.tile([P, PAGE], U32, name="pairs%d" % e, align_bytes=64, offset=(e - 1) * SLOT_BYTES)
@@ -156,20 +157,39 @@ def tile_attend_pkv4_rel2_cap_kernel(tc, qT, k_words, k_scales, v_words, v_scale
                             start=(g == 0),
                             stop=(g == PASSES - 1),
                         )
-                for n0 in range(0, width, HALF):
-                    halves.append(scores[:, n0 : n0 + HALF])
-            rows = HALF // PACK
-            capped = [keep.tile([P, PACK, rows], F32, name="capped%d_%d" % (e, h)) for h in range(2)]
-            positive = [keep.tile([P, PACK, rows], F32, name="positive%d_%d" % (e, h)) for h in range(2)]
+                by_place = scores[:].rearrange("q (s t) -> q t s", t=PACK)
+                if e == ON_VECTOR:
+                    whole = by_place
+                elif parts == 2:
+                    halves.append(by_place)
+                else:
+                    halves.extend([by_place[:, 0:2, :], by_place[:, 2:4, :]])
             weights = keep.tile([P, PACK, P], F32, name="weights%d" % e)
-            for h in range(2):
-                nc.scalar.activation(capped[h][:], halves[h].rearrange("q (s t) -> q t s", t=PACK), ACT.Tanh, scale=1.0 / CAP)
-            for h in range(2):
+            if parts == 2:
+                shape = [P, PACK, P // 2]
+                targets = [weights[:, :, 0 : P // 2], weights[:, :, P // 2 : P]]
+            else:
+                shape = [P, 2, P]
+                targets = [weights[:, 0:2, :], weights[:, 2:4, :]]
+            column = 1 + 2 * e - (e > ON_VECTOR)
+            if e == ON_VECTOR:
+                capped_page = keep.tile([P, PACK, P], F32, name="capped_page")
+                nc.scalar.activation(capped_page[:], whole, ACT.Tanh, scale=1.0 / CAP)
+                flat = capped_page[:].rearrange("q t s -> q (t s)")
+                nc.vector.scalar_tensor_tensor(
+                    weights[:].rearrange("q t s -> q (t s)"), flat, 0.0, flat, ALU.max, ALU.mult,
+                    accum_out=sums[:, column : column + 1],
+                )
+            capped = [keep.tile(shape, F32, name="capped%d_%d" % (e, h)) for h in range(len(halves))]
+            positive = [keep.tile(shape, F32, name="positive%d_%d" % (e, h)) for h in range(len(halves))]
+            for h in range(len(halves)):
+                nc.scalar.activation(capped[h][:], halves[h], ACT.Tanh, scale=1.0 / CAP)
+            for h in range(len(halves)):
                 nc.scalar.activation(positive[h][:], capped[h][:], ACT.Relu)
-            for h in range(2):
+            for h in range(len(halves)):
                 nc.scalar.activation(
-                    weights[:, :, h * rows : (h + 1) * rows], positive[h][:], ACT.Square, scale=CAP,
-                    accum_out=sums[:, 2 * e + h : 2 * e + h + 1],
+                    targets[h], positive[h][:], ACT.Square,
+                    accum_out=sums[:, column + h : column + h + 1],
                 )
             turned[e] = psum.tile([P, PACK, NQ], F32, name="turned%d" % e, tag="bank%d" % TURN_BANKS[e])
             for t in range(PACK):
@@ -193,8 +213,9 @@ def tile_attend_pkv4_rel2_cap_kernel(tc, qT, k_words, k_scales, v_words, v_scale
         for e in range(PAGES):
             gather_keys(e)
             part_keys(e)
-            weigh(e)
         token_scales(3)
+        for e in range(PAGES):
+            weigh(e)
 
         vw_pool = reused.tile([P, POOL_PAGES * DV], I32, name="vw_pool", align_bytes=64, offset=POOL_PAGES * DV)
         nc.sync.dma_start(
@@ -209,8 +230,8 @@ def tile_attend_pkv4_rel2_cap_kernel(tc, qT, k_words, k_scales, v_words, v_scale
                 vsc_pool[r:P:32, :].bitcast(I32).rearrange("q (u e) -> q u e", u=POOL_PAGES),
                 vsc_rows[r].bitcast(I32),
             )
-        vw = work.tile([P, PAGES * DV], U32, name="vw", align_bytes=64, offset=4 * SLOT_BYTES)
-        vsc = work.tile([P, PAGES * DV], U8, name="vsc", align_bytes=64, offset=5 * SLOT_BYTES)
+        vw = work.tile([P, PAGES * DV], U32, name="vw", align_bytes=64, offset=5 * SLOT_BYTES)
+        vsc = work.tile([P, PAGES * DV], U8, name="vsc", align_bytes=64, offset=6 * SLOT_BYTES)
         nc.vector.tensor_copy(vw[:], vw_pool[:].bitcast(U32).indirect(vcols[:]))
         nc.vector.tensor_copy(vsc[:], vsc_pool[:].indirect(vcols[:]))
         acc = psum.tile([P, DV], F32, name="acc", tag="bank7")

@@ -27,6 +27,7 @@ POOL_PAGES = T // PAGE
 PASSES = D // (P * PACK)
 SCALE_ROWS = 16
 ON_VECTOR = 2
+ON_SCALAR = 0
 KS_ROW0 = P - PASSES * SCALE_ROWS
 HALF = PAGE // 2
 SPREAD = 5 * PAGE
@@ -204,6 +205,13 @@ def tile_attend_pkv4_rel2_cap_kernel(tc, qT, k_words, k_scales, v_words, v_scale
                 ALU.mult,
             )
 
+        def scale_on_scalar(e):
+            by_place = keep.tile([P, PACK, NQ], BF16, name="by_place%d" % e, align_bytes=64)
+            for t in range(PACK):
+                nc.scalar.activation(by_place[:, t, :], turned[e][:, t, :], ACT.Copy, scale=vs_turned[e][:, t : t + 1])
+            w_bf[e] = keep.tile([P, NQ, PACK], BF16, name="w_bf%d" % e, align_bytes=64)
+            nc.scalar.copy(w_bf[e][:], by_place[:].rearrange("s t q -> s q t"))
+
         token_scales(0)
         token_scales(1)
         nc.vector.quantize_mx(
@@ -216,6 +224,7 @@ def tile_attend_pkv4_rel2_cap_kernel(tc, qT, k_words, k_scales, v_words, v_scale
         token_scales(3)
         for e in range(PAGES):
             weigh(e)
+        scale_on_scalar(ON_SCALAR)
 
         vw_pool = reused.tile([P, POOL_PAGES * DV], I32, name="vw_pool", align_bytes=64, offset=POOL_PAGES * DV)
         nc.sync.dma_start(
@@ -237,9 +246,10 @@ def tile_attend_pkv4_rel2_cap_kernel(tc, qT, k_words, k_scales, v_words, v_scale
         acc = psum.tile([P, DV], F32, name="acc", tag="bank7")
         denom = keep.tile([P, 1], F32, name="denom")
         inverse = keep.tile([P, 1], F32, name="inverse")
-        order = (0, 1, 2, 3)
+        order = [e for e in range(PAGES) if e != ON_SCALAR] + [ON_SCALAR]
         for e in order:
-            scale_on_vector(e)
+            if e != ON_SCALAR:
+                scale_on_vector(e)
             if e == PAGES - 1:
                 nc.vector.tensor_reduce(denom[:], sums[:], axis=AX.X, op=ALU.add)
                 nc.vector.reciprocal(inverse[:], denom[:])

@@ -27,6 +27,7 @@ POOL_PAGES = T // PAGE
 PASSES = D // (P * PACK)
 SCALE_ROWS = 16
 ON_VECTOR = 2
+WARM_PASSES = 4
 ON_SCALAR = 0
 KS_ROW0 = P - PASSES * SCALE_ROWS
 HALF = PAGE // 2
@@ -217,6 +218,17 @@ def tile_attend_pkv4_rel2_cap_kernel(tc, qT, k_words, k_scales, v_words, v_scale
         nc.vector.quantize_mx(
             out=q_codes[:].bitcast(FP8X4), scales=q_scales[:], in_=q_flat
         )
+        clock_up = psum.tile([P, 2, PASSES * NQ], F32, name="clock_up", tag="bank7")
+        for i in range(WARM_PASSES):
+            nc.tensor.matmul_mx(
+                out=clock_up[:, i % 2, :],
+                lhsT=q_codes[:, 0:NQ].bitcast(FP8X4),
+                lhsT_scale=q_scales[:, 0:NQ],
+                rhs=q_codes[:].bitcast(FP8X4),
+                rhs_scale=q_scales[:],
+                start=True,
+                stop=True,
+            )
         token_scales(2)
         for e in range(PAGES):
             gather_keys(e)

@@ -31,7 +31,7 @@ WARM_PASSES = 4
 ON_SCALAR = 0
 KS_ROW0 = P - PASSES * SCALE_ROWS
 HALF = PAGE // 2
-SPREAD = 5 * PAGE
+SPREAD = 3 * PAGE
 RUN = SPREAD // P
 ZERO_PIECES = 2
 BANKS = 8
@@ -53,11 +53,11 @@ def tile_attend_pkv4_rel2_cap_kernel(tc, qT, k_words, k_scales, v_words, v_scale
         ks_pool = reused.tile([P, T], U8, name="ks_pool", align_bytes=64, offset=0)
         vs_runs = work.tile([P, RUN], F32, name="vs_runs", align_bytes=64, offset=0)
         vs_pool = keep.tile([P, T], F32, name="vs_pool", align_bytes=64)
-        q_raw = keep.tile([P, PASSES, PACK, NQ], F32, name="q_raw", align_bytes=64)
+        q_raw = reused.tile([P, PASSES, PACK, NQ], F32, name="q_raw", align_bytes=64, offset=T)
         kw_pool = keep.tile([P, T], I32, name="kw_pool", align_bytes=64)
+        nc.sync.dma_start(ks_pool[KS_ROW0:P, :].bitcast(I32), k_scales.rearrange("g f t -> f g t").bitcast(I32))
         nc.sync.dma_start(slots[:], offs)
-        nc.scalar.dma_start(ks_pool[KS_ROW0:P, :].bitcast(I32), k_scales.rearrange("g f t -> f g t").bitcast(I32))
-        nc.sync.dma_start(vs_runs[:], vs[0, 0:SPREAD].rearrange("(p c) -> p c", c=RUN))
+        nc.scalar.dma_start(vs_runs[:], vs[0, 0:SPREAD].rearrange("(p c) -> p c", c=RUN))
         nc.scalar.dma_start(vs_pool[P - 1 : P, SPREAD:T], vs[0:1, SPREAD:T])
         nc.sync.dma_start(q_raw[:], qT[0].rearrange("(g p j) w -> p g j w", g=PASSES, j=PACK))
         nc.sync.dma_start(kw_pool[:], k_words[0].rearrange("p t b -> p (t b)").bitcast(I32))
@@ -68,8 +68,6 @@ def tile_attend_pkv4_rel2_cap_kernel(tc, qT, k_words, k_scales, v_words, v_scale
         warm = keep.tile([P, 1], F32, name="warm")
         nc.scalar.activation(warm[:], sums[:, 0:1], ACT.Tanh)
         nc.vector.memset(ks_pool[0:KS_ROW0, :].bitcast(I32), 0)
-        ks_planes = keep.tile([P, PASSES, N], U8, name="ks_planes", align_bytes=64)
-        nc.vector.memset(ks_planes[:].bitcast(I32), 0)
         nc.vector.memset(vs_pool[0 : P - 1, SPREAD:T], 0.0)
         identity = keep.tile([P, P], F32, name="identity")
         make_identity(nc, identity[:])
@@ -90,6 +88,7 @@ def tile_attend_pkv4_rel2_cap_kernel(tc, qT, k_words, k_scales, v_words, v_scale
 
         ks_listed = keep.tile([P, N], U8, name="ks_listed", align_bytes=64)
         nc.vector.tensor_copy(ks_listed[:], ks_pool[:].indirect(slots[:]))
+        ks_planes = reused.tile([P, PASSES, N], U8, name="ks_planes", align_bytes=64, offset=0)
         for quadrant in range(4):
             row0 = KS_ROW0 + 4 * PASSES * quadrant
             nc.sync.dma_start(
@@ -238,12 +237,12 @@ def tile_attend_pkv4_rel2_cap_kernel(tc, qT, k_words, k_scales, v_words, v_scale
             weigh(e)
         scale_on_scalar(ON_SCALAR)
 
-        vw_pool = reused.tile([P, POOL_PAGES * DV], I32, name="vw_pool", align_bytes=64, offset=POOL_PAGES * DV)
+        vw_pool = reused.tile([P, POOL_PAGES * DV], I32, name="vw_pool", align_bytes=64, offset=T + POOL_PAGES * DV)
         nc.sync.dma_start(
             vw_pool[:].rearrange("p (u e) -> p u e", u=POOL_PAGES),
             v_words.rearrange("u p e r -> p u (e r)").bitcast(I32),
         )
-        vsc_pool = reused.tile([P, POOL_PAGES * DV], U8, name="vsc_pool", align_bytes=64, offset=0)
+        vsc_pool = reused.tile([P, POOL_PAGES * DV], U8, name="vsc_pool", align_bytes=64, offset=T)
         nc.vector.memset(vsc_pool[:].bitcast(I32), 0)
         vsc_rows = v_scales.rearrange("u (q r) e -> r q u e", r=4)
         for r in range(4):

@@ -46,22 +46,33 @@ def tile_attend_pkv4_rel2_cap_kernel(tc, qT, k_words, k_scales, v_words, v_scale
         keep = ctx.enter_context(tc.tile_pool(name="keep", bufs=1))
         reused = ctx.enter_context(tc.tile_pool(name="reused", bufs=1))
         work = ctx.enter_context(tc.tile_pool(name="work", bufs=1))
+        early = ctx.enter_context(tc.tile_pool(name="early", bufs=1))
         psum = ctx.enter_context(tc.psum_pool(name="psum", bufs=1))
 
         slots = lists.tile([P, N // 16], U16, name="slots")
         vcols = lists.tile([P, PAGES * DV // 16], U16, name="vcols")
         ks_pool = reused.tile([P, T], U8, name="ks_pool", align_bytes=64, offset=0)
-        vs_runs = work.tile([P, RUN], F32, name="vs_runs", align_bytes=64, offset=0)
+        vs_runs = early.tile([P, RUN], F32, name="vs_runs", align_bytes=64, offset=0)
         vs_pool = keep.tile([P, T], F32, name="vs_pool", align_bytes=64)
-        q_raw = reused.tile([P, PASSES, PACK, NQ], F32, name="q_raw", align_bytes=64, offset=T)
+        raw_area = work.tile([P, WORK_SLOTS * PAGE], F32, name="raw_area", align_bytes=64, offset=0)
+        q_raw = raw_area[:, 0 : PASSES * PACK * NQ].rearrange("p (g j w) -> p g j w", g=PASSES, j=PACK)
         kw_pool = keep.tile([P, T], I32, name="kw_pool", align_bytes=64)
         nc.sync.dma_start(ks_pool[KS_ROW0:P, :].bitcast(I32), k_scales.rearrange("g f t -> f g t").bitcast(I32))
         nc.sync.dma_start(slots[:], offs)
         nc.scalar.dma_start(vs_runs[:], vs[0, 0:SPREAD].rearrange("(p c) -> p c", c=RUN))
         nc.scalar.dma_start(vs_pool[P - 1 : P, SPREAD:T], vs[0:1, SPREAD:T])
-        nc.sync.dma_start(q_raw[:], qT[0].rearrange("(g p j) w -> p g j w", g=PASSES, j=PACK))
-        nc.sync.dma_start(kw_pool[:], k_words[0].rearrange("p t b -> p (t b)").bitcast(I32))
+        nc.sync.dma_start(q_raw, qT[0].rearrange("(g p j) w -> p g j w", g=PASSES, j=PACK))
         nc.sync.dma_start(vcols[:], voffs)
+        vsc_pool = keep.tile([P, POOL_PAGES * DV], U8, name="vsc_pool", align_bytes=64)
+        nc.vector.memset(vsc_pool[:].bitcast(I32), 0)
+        vsc_rows = v_scales.rearrange("u (q r) e -> r q u e", r=4)
+        for r in range(4):
+            nc.sync.dma_start(
+                vsc_pool[r:P:32, :].bitcast(I32).rearrange("q (u e) -> q u e", u=POOL_PAGES),
+                vsc_rows[r].bitcast(I32),
+            )
+            if r == 0:
+                nc.sync.dma_start(kw_pool[:], k_words[0].rearrange("p t b -> p (t b)").bitcast(I32))
 
         sums = keep.tile([P, 2 * PAGES], F32, name="sums")
         nc.vector.memset(sums[:, 0:1], 1.0 / (CAP * CAP))
@@ -80,7 +91,7 @@ def tile_attend_pkv4_rel2_cap_kernel(tc, qT, k_words, k_scales, v_words, v_scale
                 nc.tensor.transpose(spread[:, c, :], vs_runs[:, column : column + 1].to_broadcast([P, P]), identity[:])
             nc.scalar.copy(vs_by_run[:, :, b * PACK : (b + 1) * PACK], spread[:].rearrange("i c p -> i p c"))
 
-        q_area = work.tile([P, PAGES * SLOT_BYTES // 2], BF16, name="q_area", align_bytes=64, offset=0)
+        q_area = early.tile([P, PASSES * NQ * PACK], BF16, name="q_area", align_bytes=64, offset=0)
         q_flat = q_area[:, 0 : PASSES * NQ * PACK]
         q_bf = q_flat.rearrange("p (g w j) -> p g w j", g=PASSES, j=PACK)
         for g in range(PASSES):
@@ -96,12 +107,22 @@ def tile_attend_pkv4_rel2_cap_kernel(tc, qT, k_words, k_scales, v_words, v_scale
                 ks_listed[row0 : row0 + 4 * PASSES, :].bitcast(I32),
             )
 
+        vw_pool = work.tile([P, POOL_PAGES * DV], I32, name="vw_pool", align_bytes=64, offset=(WORK_SLOTS - 1) * SLOT_BYTES)
+        nc.sync.dma_start(
+            vw_pool[:].rearrange("p (u e) -> p u e", u=POOL_PAGES),
+            v_words.rearrange("u p e r -> p u (e r)").bitcast(I32),
+        )
+
         q_codes = keep.tile([P, PASSES * NQ], U32, name="q_codes", align_bytes=64)
         q_scales = keep.tile([P, PASSES * NQ], U8, name="q_scales", align_bytes=64)
         pairs = {}
         keys = {}
         vs_turned = {}
         turned = {}
+        weights = {}
+        pieces = {}
+        capped = {}
+        positive = {}
         w_bf = {}
         SCORE_BANKS = ((0, 1), (2,), (3,), (4,))
         TURN_BANKS = (5, 6, 0, 1)
@@ -129,25 +150,28 @@ def tile_attend_pkv4_rel2_cap_kernel(tc, qT, k_words, k_scales, v_words, v_scale
                 )
                 keys[e].append(part)
 
-        def token_scales(e):
-            if e < PAGES - 1:
-                listed = keep.tile([P, PAGE], F32, name="vs_listed%d" % e, align_bytes=64)
+        def token_scales(first, count):
+            if first < PAGES - 1:
+                listed = keep.tile([P, count, PAGE], F32, name="vs_listed%d" % first, align_bytes=64)
             else:
-                listed = work.tile([P, PAGE], F32, name="vs_listed%d" % e, align_bytes=64, offset=3 * SLOT_BYTES)
-            nc.vector.tensor_copy(listed[:], vs_pool[:].indirect(slots[:, e * PAGE // 16 : (e + 1) * PAGE // 16]))
-            vs_turned[e] = keep.tile([P, PACK], F32, name="vs_turned%d" % e)
-            nc.sync.dma_start(vs_turned[e][:], listed[P - 1 : P, :].rearrange("o (s t) -> o s t", t=PACK))
+                listed = work.tile([P, count, PAGE], F32, name="vs_listed%d" % first, align_bytes=64, offset=3 * SLOT_BYTES)
+            nc.vector.tensor_copy(
+                listed[:].rearrange("p e n -> p (e n)"),
+                vs_pool[:].indirect(slots[:, first * PAGE // 16 : (first + count) * PAGE // 16]),
+            )
+            for e in range(first, first + count):
+                vs_turned[e] = keep.tile([P, PACK], F32, name="vs_turned%d" % e)
+                nc.sync.dma_start(vs_turned[e][:], listed[P - 1 : P, e - first, :].rearrange("o (s t) -> o s t", t=PACK))
 
-        def weigh(e):
+        def score(e):
             parts = len(SCORE_BANKS[e])
             width = PAGE // parts
             step = PAGE if parts == 1 else P
-            halves = []
+            placed = []
             for h in range(parts):
                 scores = psum.tile([P, width], F32, name="scores%d_%d" % (e, h), tag="bank%d" % SCORE_BANKS[e][h])
                 for n0 in range(0, width, step):
-                    col0 = h * width + n0
-                    slot0 = e * PAGE + col0
+                    slot0 = e * PAGE + h * width + n0
                     for g in range(PASSES):
                         nc.tensor.matmul_mx(
                             out=scores[:, n0 : n0 + step],
@@ -158,43 +182,45 @@ def tile_attend_pkv4_rel2_cap_kernel(tc, qT, k_words, k_scales, v_words, v_scale
                             start=(g == 0),
                             stop=(g == PASSES - 1),
                         )
-                by_place = scores[:].rearrange("q (s t) -> q t s", t=PACK)
-                if e == ON_VECTOR:
-                    whole = by_place
-                elif parts == 2:
-                    halves.append(by_place)
-                else:
-                    halves.extend([by_place[:, 0:2, :], by_place[:, 2:4, :]])
-            weights = keep.tile([P, PACK, P], F32, name="weights%d" % e)
-            if parts == 2:
-                shape = [P, PACK, P // 2]
-                targets = [weights[:, :, 0 : P // 2], weights[:, :, P // 2 : P]]
+                placed.append(scores[:].rearrange("q (s t) -> q t s", t=PACK))
+            weights[e] = keep.tile([P, PACK, P], F32, name="weights%d" % e, tag="weights%d" % (e - (e == ON_VECTOR)))
+            if e == ON_VECTOR:
+                pieces[e] = [(placed[0], weights[e][:])]
+            elif parts == 2:
+                pieces[e] = [(placed[h], weights[e][:, :, h * P // 2 : (h + 1) * P // 2]) for h in range(2)]
             else:
-                shape = [P, 2, P]
-                targets = [weights[:, 0:2, :], weights[:, 2:4, :]]
+                pieces[e] = [(placed[0][:, 2 * h : 2 * h + 2, :], weights[e][:, 2 * h : 2 * h + 2, :]) for h in range(2)]
+
+        def cap(e):
+            capped[e] = []
+            for h, (source, target) in enumerate(pieces[e]):
+                tile = keep.tile(list(target.shape), F32, name="capped%d_%d" % (e, h))
+                nc.scalar.activation(tile[:], source, ACT.Tanh, scale=1.0 / CAP)
+                capped[e].append(tile)
+
+        def rectify(e):
+            positive[e] = []
+            for h, tile in enumerate(capped[e]):
+                kept = keep.tile(list(pieces[e][h][1].shape), F32, name="positive%d_%d" % (e, h))
+                nc.scalar.activation(kept[:], tile[:], ACT.Relu)
+                positive[e].append(kept)
+
+        def square(e):
             column = 1 + 2 * e - (e > ON_VECTOR)
             if e == ON_VECTOR:
-                capped_page = keep.tile([P, PACK, P], F32, name="capped_page")
-                nc.scalar.activation(capped_page[:], whole, ACT.Tanh, scale=1.0 / CAP)
-                flat = capped_page[:].rearrange("q t s -> q (t s)")
+                flat = capped[e][0][:].rearrange("q t s -> q (t s)")
                 nc.vector.scalar_tensor_tensor(
-                    weights[:].rearrange("q t s -> q (t s)"), flat, 0.0, flat, ALU.max, ALU.mult,
+                    weights[e][:].rearrange("q t s -> q (t s)"), flat, 0.0, flat, ALU.max, ALU.mult,
                     accum_out=sums[:, column : column + 1],
                 )
-            capped = [keep.tile(shape, F32, name="capped%d_%d" % (e, h)) for h in range(len(halves))]
-            positive = [keep.tile(shape, F32, name="positive%d_%d" % (e, h)) for h in range(len(halves))]
-            for h in range(len(halves)):
-                nc.scalar.activation(capped[h][:], halves[h], ACT.Tanh, scale=1.0 / CAP)
-            for h in range(len(halves)):
-                nc.scalar.activation(positive[h][:], capped[h][:], ACT.Relu)
-            for h in range(len(halves)):
-                nc.scalar.activation(
-                    targets[h], positive[h][:], ACT.Square,
-                    accum_out=sums[:, column + h : column + h + 1],
-                )
+            else:
+                for h, kept in enumerate(positive[e]):
+                    nc.scalar.activation(
+                        pieces[e][h][1], kept[:], ACT.Square, accum_out=sums[:, column + h : column + h + 1]
+                    )
             turned[e] = psum.tile([P, PACK, NQ], F32, name="turned%d" % e, tag="bank%d" % TURN_BANKS[e])
             for t in range(PACK):
-                nc.tensor.transpose(turned[e][:, t, :], weights[:, t, :], identity[:])
+                nc.tensor.transpose(turned[e][:, t, :], weights[e][:, t, :], identity[:])
 
         def scale_on_vector(e):
             w_bf[e] = keep.tile([P, NQ, PACK], BF16, name="w_bf%d" % e, align_bytes=64)
@@ -212,8 +238,7 @@ def tile_attend_pkv4_rel2_cap_kernel(tc, qT, k_words, k_scales, v_words, v_scale
             w_bf[e] = keep.tile([P, NQ, PACK], BF16, name="w_bf%d" % e, align_bytes=64)
             nc.scalar.copy(w_bf[e][:], by_place[:].rearrange("s t q -> s q t"))
 
-        token_scales(0)
-        token_scales(1)
+        token_scales(0, 3)
         nc.vector.quantize_mx(
             out=q_codes[:].bitcast(FP8X4), scales=q_scales[:], in_=q_flat
         )
@@ -228,33 +253,30 @@ def tile_attend_pkv4_rel2_cap_kernel(tc, qT, k_words, k_scales, v_words, v_scale
                 start=True,
                 stop=True,
             )
-        token_scales(2)
         for e in range(PAGES):
             gather_keys(e)
             part_keys(e)
-        token_scales(3)
+        token_scales(3, 1)
         for e in range(PAGES):
-            weigh(e)
+            score(e)
+        cap(0)
+        rectify(0)
+        square(0)
+        cap(1)
+        rectify(1)
+        cap(2)
+        square(1)
+        square(2)
+        cap(3)
+        rectify(3)
+        square(3)
         scale_on_scalar(ON_SCALAR)
 
-        vw_pool = reused.tile([P, POOL_PAGES * DV], I32, name="vw_pool", align_bytes=64, offset=T + POOL_PAGES * DV)
-        nc.sync.dma_start(
-            vw_pool[:].rearrange("p (u e) -> p u e", u=POOL_PAGES),
-            v_words.rearrange("u p e r -> p u (e r)").bitcast(I32),
-        )
-        vsc_pool = reused.tile([P, POOL_PAGES * DV], U8, name="vsc_pool", align_bytes=64, offset=T)
-        nc.vector.memset(vsc_pool[:].bitcast(I32), 0)
-        vsc_rows = v_scales.rearrange("u (q r) e -> r q u e", r=4)
-        for r in range(4):
-            nc.sync.dma_start(
-                vsc_pool[r:P:32, :].bitcast(I32).rearrange("q (u e) -> q u e", u=POOL_PAGES),
-                vsc_rows[r].bitcast(I32),
-            )
         vw = work.tile([P, PAGES * DV], U32, name="vw", align_bytes=64, offset=5 * SLOT_BYTES)
         vsc = work.tile([P, PAGES * DV], U8, name="vsc", align_bytes=64, offset=6 * SLOT_BYTES)
         nc.vector.tensor_copy(vw[:], vw_pool[:].bitcast(U32).indirect(vcols[:]))
         nc.vector.tensor_copy(vsc[:], vsc_pool[:].indirect(vcols[:]))
-        acc = psum.tile([P, DV], F32, name="acc", tag="bank7")
+        acc = psum.tile([P, DV], F32, name="acc", tag="bank%d" % TURN_BANKS[PAGES - 1])
         denom = keep.tile([P, 1], F32, name="denom")
         inverse = keep.tile([P, 1], F32, name="inverse")
         order = [e for e in range(PAGES) if e != ON_SCALAR] + [ON_SCALAR]

@@ -26,7 +26,7 @@ PAGES = N // PAGE
 POOL_PAGES = T // PAGE
 PASSES = D // (P * PACK)
 SCALE_ROWS = 16
-ON_VECTOR = 2
+ON_VECTOR = (2, 3)
 WARM_PASSES = 4
 ON_SCALAR = 0
 KS_ROW0 = P - PASSES * SCALE_ROWS
@@ -62,24 +62,17 @@ def tile_attend_pkv4_rel2_cap_kernel(tc, qT, k_words, k_scales, v_words, v_scale
         nc.scalar.dma_start(vs_runs[:], vs[0, 0:SPREAD].rearrange("(p c) -> p c", c=RUN))
         nc.scalar.dma_start(vs_pool[P - 1 : P, SPREAD:T], vs[0:1, SPREAD:T])
         nc.sync.dma_start(q_raw, qT[0].rearrange("(g p j) w -> p g j w", g=PASSES, j=PACK))
+        nc.sync.dma_start(kw_pool[:], k_words[0].rearrange("p t b -> p (t b)").bitcast(I32))
         nc.sync.dma_start(vcols[:], voffs)
-        vsc_pool = keep.tile([P, POOL_PAGES * DV], U8, name="vsc_pool", align_bytes=64)
-        nc.vector.memset(vsc_pool[:].bitcast(I32), 0)
-        vsc_rows = v_scales.rearrange("u (q r) e -> r q u e", r=4)
-        for r in range(4):
-            nc.sync.dma_start(
-                vsc_pool[r:P:32, :].bitcast(I32).rearrange("q (u e) -> q u e", u=POOL_PAGES),
-                vsc_rows[r].bitcast(I32),
-            )
-            if r == 0:
-                nc.sync.dma_start(kw_pool[:], k_words[0].rearrange("p t b -> p (t b)").bitcast(I32))
 
-        sums = keep.tile([P, 2 * PAGES], F32, name="sums")
+        sums = keep.tile([P, 1 + 2 * PAGES - len(ON_VECTOR)], F32, name="sums")
         nc.vector.memset(sums[:, 0:1], 1.0 / (CAP * CAP))
         warm = keep.tile([P, 1], F32, name="warm")
         nc.scalar.activation(warm[:], sums[:, 0:1], ACT.Tanh)
         nc.vector.memset(ks_pool[0:KS_ROW0, :].bitcast(I32), 0)
         nc.vector.memset(vs_pool[0 : P - 1, SPREAD:T], 0.0)
+        vsc_pool = keep.tile([P, POOL_PAGES * DV], U8, name="vsc_pool", align_bytes=64)
+        nc.vector.memset(vsc_pool[:].bitcast(I32), 0)
         identity = keep.tile([P, P], F32, name="identity")
         make_identity(nc, identity[:])
 
@@ -112,6 +105,12 @@ def tile_attend_pkv4_rel2_cap_kernel(tc, qT, k_words, k_scales, v_words, v_scale
             vw_pool[:].rearrange("p (u e) -> p u e", u=POOL_PAGES),
             v_words.rearrange("u p e r -> p u (e r)").bitcast(I32),
         )
+        vsc_rows = v_scales.rearrange("u (q r) e -> r q u e", r=4)
+        for r in range(4):
+            nc.sync.dma_start(
+                vsc_pool[r:P:32, :].bitcast(I32).rearrange("q (u e) -> q u e", u=POOL_PAGES),
+                vsc_rows[r].bitcast(I32),
+            )
 
         q_codes = keep.tile([P, PASSES * NQ], U32, name="q_codes", align_bytes=64)
         q_scales = keep.tile([P, PASSES * NQ], U8, name="q_scales", align_bytes=64)
@@ -183,8 +182,8 @@ def tile_attend_pkv4_rel2_cap_kernel(tc, qT, k_words, k_scales, v_words, v_scale
                             stop=(g == PASSES - 1),
                         )
                 placed.append(scores[:].rearrange("q (s t) -> q t s", t=PACK))
-            weights[e] = keep.tile([P, PACK, P], F32, name="weights%d" % e, tag="weights%d" % (e - (e == ON_VECTOR)))
-            if e == ON_VECTOR:
+            weights[e] = keep.tile([P, PACK, P], F32, name="weights%d" % e)
+            if e in ON_VECTOR:
                 pieces[e] = [(placed[0], weights[e][:])]
             elif parts == 2:
                 pieces[e] = [(placed[h], weights[e][:, :, h * P // 2 : (h + 1) * P // 2]) for h in range(2)]
@@ -206,8 +205,8 @@ def tile_attend_pkv4_rel2_cap_kernel(tc, qT, k_words, k_scales, v_words, v_scale
                 positive[e].append(kept)
 
         def square(e):
-            column = 1 + 2 * e - (e > ON_VECTOR)
-            if e == ON_VECTOR:
+            column = 1 + 2 * e - len([other for other in ON_VECTOR if other < e])
+            if e in ON_VECTOR:
                 flat = capped[e][0][:].rearrange("q t s -> q (t s)")
                 nc.vector.scalar_tensor_tensor(
                     weights[e][:].rearrange("q t s -> q (t s)"), flat, 0.0, flat, ALU.max, ALU.mult,
@@ -238,7 +237,7 @@ def tile_attend_pkv4_rel2_cap_kernel(tc, qT, k_words, k_scales, v_words, v_scale
             w_bf[e] = keep.tile([P, NQ, PACK], BF16, name="w_bf%d" % e, align_bytes=64)
             nc.scalar.copy(w_bf[e][:], by_place[:].rearrange("s t q -> s q t"))
 
-        token_scales(0, 3)
+        token_scales(0, PAGES)
         nc.vector.quantize_mx(
             out=q_codes[:].bitcast(FP8X4), scales=q_scales[:], in_=q_flat
         )
@@ -256,7 +255,6 @@ def tile_attend_pkv4_rel2_cap_kernel(tc, qT, k_words, k_scales, v_words, v_scale
         for e in range(PAGES):
             gather_keys(e)
             part_keys(e)
-        token_scales(3, 1)
         for e in range(PAGES):
             score(e)
         cap(0)
@@ -265,27 +263,25 @@ def tile_attend_pkv4_rel2_cap_kernel(tc, qT, k_words, k_scales, v_words, v_scale
         cap(1)
         rectify(1)
         cap(2)
-        square(1)
-        square(2)
         cap(3)
-        rectify(3)
+        square(2)
         square(3)
+        square(1)
         scale_on_scalar(ON_SCALAR)
 
         vw = work.tile([P, PAGES * DV], U32, name="vw", align_bytes=64, offset=5 * SLOT_BYTES)
         vsc = work.tile([P, PAGES * DV], U8, name="vsc", align_bytes=64, offset=6 * SLOT_BYTES)
         nc.vector.tensor_copy(vw[:], vw_pool[:].bitcast(U32).indirect(vcols[:]))
         nc.vector.tensor_copy(vsc[:], vsc_pool[:].indirect(vcols[:]))
-        acc = psum.tile([P, DV], F32, name="acc", tag="bank%d" % TURN_BANKS[PAGES - 1])
+        acc = psum.tile([P, DV], F32, name="acc", tag="bank%d" % TURN_BANKS[1])
         denom = keep.tile([P, 1], F32, name="denom")
         inverse = keep.tile([P, 1], F32, name="inverse")
-        order = [e for e in range(PAGES) if e != ON_SCALAR] + [ON_SCALAR]
+        for e in (2, 3, 1):
+            scale_on_vector(e)
+        nc.vector.tensor_reduce(denom[:], sums[:], axis=AX.X, op=ALU.add)
+        nc.vector.reciprocal(inverse[:], denom[:])
+        order = (2, 3, 0, 1)
         for e in order:
-            if e != ON_SCALAR:
-                scale_on_vector(e)
-            if e == PAGES - 1:
-                nc.vector.tensor_reduce(denom[:], sums[:], axis=AX.X, op=ALU.add)
-                nc.vector.reciprocal(inverse[:], denom[:])
             w_codes = keep.tile([P, NQ], U32, name="w_codes%d" % e, align_bytes=64)
             w_scales = keep.tile([P, NQ], U8, name="w_scales%d" % e, align_bytes=64)
             nc.vector.quantize_mx(

@@ -100,11 +100,6 @@ def tile_attend_pkv4_rel2_cap_kernel(tc, qT, k_words, k_scales, v_words, v_scale
                 ks_listed[row0 : row0 + 4 * PASSES, :].bitcast(I32),
             )
 
-        vw_pool = work.tile([P, POOL_PAGES * DV], I32, name="vw_pool", align_bytes=64, offset=(WORK_SLOTS - 1) * SLOT_BYTES)
-        nc.sync.dma_start(
-            vw_pool[:].rearrange("p (u e) -> p u e", u=POOL_PAGES),
-            v_words.rearrange("u p e r -> p u (e r)").bitcast(I32),
-        )
         vsc_rows = v_scales.rearrange("u (q r) e -> r q u e", r=4)
         for r in range(4):
             nc.sync.dma_start(
@@ -238,6 +233,11 @@ def tile_attend_pkv4_rel2_cap_kernel(tc, qT, k_words, k_scales, v_words, v_scale
             nc.scalar.copy(w_bf[e][:], by_place[:].rearrange("s t q -> s q t"))
 
         token_scales(0, PAGES)
+        vw_pool = work.tile([P, POOL_PAGES * DV], I32, name="vw_pool", align_bytes=64, offset=(WORK_SLOTS - 1) * SLOT_BYTES)
+        nc.sync.dma_start(
+            vw_pool[:].rearrange("p (u e) -> p u e", u=POOL_PAGES),
+            v_words.rearrange("u p e r -> p u (e r)").bitcast(I32),
+        )
         nc.vector.quantize_mx(
             out=q_codes[:].bitcast(FP8X4), scales=q_scales[:], in_=q_flat
         )

@@ -60,7 +60,6 @@ def tile_attend_pkv4_rel2_cap_kernel(tc, qT, k_words, k_scales, v_words, v_scale
         nc.sync.dma_start(ks_pool[KS_ROW0:P, :].bitcast(I32), k_scales.rearrange("g f t -> f g t").bitcast(I32))
         nc.sync.dma_start(slots[:], offs)
         nc.scalar.dma_start(vs_runs[:], vs[0, 0:SPREAD].rearrange("(p c) -> p c", c=RUN))
-        nc.scalar.dma_start(vs_pool[P - 1 : P, SPREAD:T], vs[0:1, SPREAD:T])
         nc.sync.dma_start(q_raw, qT[0].rearrange("(g p j) w -> p g j w", g=PASSES, j=PACK))
         nc.sync.dma_start(kw_pool[:], k_words[0].rearrange("p t b -> p (t b)").bitcast(I32))
         nc.sync.dma_start(vcols[:], voffs)
@@ -69,6 +68,7 @@ def tile_attend_pkv4_rel2_cap_kernel(tc, qT, k_words, k_scales, v_words, v_scale
         nc.vector.memset(sums[:, 0:1], 1.0 / (CAP * CAP))
         warm = keep.tile([P, 1], F32, name="warm")
         nc.scalar.activation(warm[:], sums[:, 0:1], ACT.Tanh)
+        nc.scalar.dma_start(vs_pool[P - 1 : P, SPREAD:T], vs[0:1, SPREAD:T])
         nc.vector.memset(ks_pool[0:KS_ROW0, :].bitcast(I32), 0)
         nc.vector.memset(vs_pool[0 : P - 1, SPREAD:T], 0.0)
         vsc_pool = keep.tile([P, POOL_PAGES * DV], U8, name="vsc_pool", align_bytes=64)
@@ -192,12 +192,10 @@ def tile_attend_pkv4_rel2_cap_kernel(tc, qT, k_words, k_scales, v_words, v_scale
                 nc.scalar.activation(tile[:], source, ACT.Tanh, scale=1.0 / CAP)
                 capped[e].append(tile)
 
-        def rectify(e):
-            positive[e] = []
-            for h, tile in enumerate(capped[e]):
-                kept = keep.tile(list(pieces[e][h][1].shape), F32, name="positive%d_%d" % (e, h))
-                nc.scalar.activation(kept[:], tile[:], ACT.Relu)
-                positive[e].append(kept)
+        def rectify(e, h):
+            kept = keep.tile(list(pieces[e][h][1].shape), F32, name="positive%d_%d" % (e, h))
+            nc.scalar.activation(kept[:], capped[e][h][:], ACT.Relu)
+            positive.setdefault(e, []).append(kept)
 
         def square(e):
             column = 1 + 2 * e - len([other for other in ON_VECTOR if other < e])
@@ -258,12 +256,14 @@ def tile_attend_pkv4_rel2_cap_kernel(tc, qT, k_words, k_scales, v_words, v_scale
         for e in range(PAGES):
             score(e)
         cap(0)
-        rectify(0)
+        rectify(0, 0)
+        rectify(0, 1)
         square(0)
         cap(1)
-        rectify(1)
+        rectify(1, 0)
         cap(2)
         cap(3)
+        rectify(1, 1)
         square(2)
         square(3)
         square(1)

@@ -31,7 +31,9 @@ WARM_PASSES = 4
 ON_SCALAR = 0
 KS_ROW0 = P - PASSES * SCALE_ROWS
 HALF = PAGE // 2
-SPREAD = 3 * PAGE
+SPREAD = 4 * PAGE
+GROUPS = 1
+GROUP = N // GROUPS
 RUN = SPREAD // P
 ZERO_PIECES = 2
 BANKS = 8
@@ -47,22 +49,26 @@ def tile_attend_pkv4_rel2_cap_kernel(tc, qT, k_words, k_scales, v_words, v_scale
         reused = ctx.enter_context(tc.tile_pool(name="reused", bufs=1))
         work = ctx.enter_context(tc.tile_pool(name="work", bufs=1))
         early = ctx.enter_context(tc.tile_pool(name="early", bufs=1))
+        late = ctx.enter_context(tc.tile_pool(name="late", bufs=1))
+        wide = ctx.enter_context(tc.tile_pool(name="wide", bufs=1))
         psum = ctx.enter_context(tc.psum_pool(name="psum", bufs=1))
 
         slots = lists.tile([P, N // 16], U16, name="slots")
         vcols = lists.tile([P, PAGES * DV // 16], U16, name="vcols")
         ks_pool = reused.tile([P, T], U8, name="ks_pool", align_bytes=64, offset=0)
         vs_runs = early.tile([P, RUN], F32, name="vs_runs", align_bytes=64, offset=0)
-        vs_pool = keep.tile([P, T], F32, name="vs_pool", align_bytes=64)
+        vs_pool = wide.tile([P, T], F32, name="vs_pool", align_bytes=64, offset=0)
         raw_area = work.tile([P, WORK_SLOTS * PAGE], F32, name="raw_area", align_bytes=64, offset=0)
-        q_raw = raw_area[:, 0 : PASSES * PACK * NQ].rearrange("p (g j w) -> p g j w", g=PASSES, j=PACK)
+        late_area = late.tile([P, 4 * PAGE], F32, name="late_area", align_bytes=64, offset=0)
+        q_raw = [area[:, 0 : PACK * NQ].rearrange("p (j w) -> p j w", j=PACK) for area in (raw_area, late_area)]
+        q_rows = qT[0].rearrange("(g p j) w -> g p j w", g=PASSES, j=PACK)
         kw_pool = keep.tile([P, T], I32, name="kw_pool", align_bytes=64)
         nc.sync.dma_start(ks_pool[KS_ROW0:P, :].bitcast(I32), k_scales.rearrange("g f t -> f g t").bitcast(I32))
         nc.sync.dma_start(slots[:], offs)
         nc.scalar.dma_start(vs_runs[:], vs[0, 0:SPREAD].rearrange("(p c) -> p c", c=RUN))
-        nc.sync.dma_start(q_raw, qT[0].rearrange("(g p j) w -> p g j w", g=PASSES, j=PACK))
+        nc.sync.dma_start(q_raw[0], q_rows[0])
         nc.sync.dma_start(kw_pool[:], k_words[0].rearrange("p t b -> p (t b)").bitcast(I32))
-        nc.sync.dma_start(vcols[:], voffs)
+        nc.sync.dma_start(q_raw[1], q_rows[1])
 
         sums = keep.tile([P, 1 + 2 * PAGES - len(ON_VECTOR)], F32, name="sums")
         nc.vector.memset(sums[:, 0:1], 1.0 / (CAP * CAP))
@@ -73,6 +79,10 @@ def tile_attend_pkv4_rel2_cap_kernel(tc, qT, k_words, k_scales, v_words, v_scale
         nc.vector.memset(vs_pool[0 : P - 1, SPREAD:T], 0.0)
         vsc_pool = keep.tile([P, POOL_PAGES * DV], U8, name="vsc_pool", align_bytes=64)
         nc.vector.memset(vsc_pool[:].bitcast(I32), 0)
+        q_codes = [keep.tile([P, (2 - g) * NQ], U32, name="q_codes%d" % g, align_bytes=64) for g in range(PASSES)]
+        q_scales = [keep.tile([P, (2 - g) * NQ], U8, name="q_scales%d" % g, align_bytes=64) for g in range(PASSES)]
+        nc.vector.memset(q_codes[0][:, NQ : 2 * NQ].bitcast(I32), 0)
+        nc.vector.memset(q_scales[0][:, NQ : 2 * NQ].bitcast(I32), 0)
         identity = keep.tile([P, P], F32, name="identity")
         make_identity(nc, identity[:])
 
@@ -84,21 +94,39 @@ def tile_attend_pkv4_rel2_cap_kernel(tc, qT, k_words, k_scales, v_words, v_scale
                 nc.tensor.transpose(spread[:, c, :], vs_runs[:, column : column + 1].to_broadcast([P, P]), identity[:])
             nc.scalar.copy(vs_by_run[:, :, b * PACK : (b + 1) * PACK], spread[:].rearrange("i c p -> i p c"))
 
-        q_area = early.tile([P, PASSES * NQ * PACK], BF16, name="q_area", align_bytes=64, offset=0)
-        q_flat = q_area[:, 0 : PASSES * NQ * PACK]
-        q_bf = q_flat.rearrange("p (g w j) -> p g w j", g=PASSES, j=PACK)
-        for g in range(PASSES):
-            nc.scalar.copy(q_bf[:, g], q_raw[:, g].rearrange("p j w -> p w j"))
+        q_bf = {}
+
+        def cast_queries(g):
+            q_bf[g] = (early, wide)[g].tile([P, NQ, PACK], BF16, name="q_bf%d" % g, align_bytes=64, offset=0)
+            nc.scalar.copy(q_bf[g][:], q_raw[g].rearrange("p j w -> p w j"))
+
+        cast_queries(0)
+
+        def quantise_queries(g):
+            nc.vector.quantize_mx(
+                out=q_codes[g][:, 0:NQ].bitcast(FP8X4),
+                scales=q_scales[g][:, 0:NQ],
+                in_=q_bf[g][:].rearrange("p w j -> p (w j)"),
+            )
 
         ks_listed = keep.tile([P, N], U8, name="ks_listed", align_bytes=64)
         nc.vector.tensor_copy(ks_listed[:], ks_pool[:].indirect(slots[:]))
-        ks_planes = reused.tile([P, PASSES, N], U8, name="ks_planes", align_bytes=64, offset=0)
-        for quadrant in range(4):
-            row0 = KS_ROW0 + 4 * PASSES * quadrant
-            nc.sync.dma_start(
-                ks_planes[32 * quadrant : 32 * quadrant + 4, :, :].bitcast(I32),
-                ks_listed[row0 : row0 + 4 * PASSES, :].bitcast(I32),
+        ks_planes = []
+
+        def move_key_scales(a):
+            plane = reused.tile(
+                [P, PASSES, GROUP], U8, name="ks_planes%d" % a, align_bytes=64, offset=a * PASSES * GROUP
             )
+            ks_planes.append(plane)
+            for quadrant in (0, 2, 1, 3):
+                row0 = KS_ROW0 + 4 * PASSES * quadrant
+                nc.sync.dma_start(
+                    plane[32 * quadrant : 32 * quadrant + 4, :, :].bitcast(I32),
+                    ks_listed[row0 : row0 + 4 * PASSES, a * GROUP : (a + 1) * GROUP].bitcast(I32),
+                )
+
+        move_key_scales(0)
+        nc.sync.dma_start(vcols[:], voffs)
 
         vsc_rows = v_scales.rearrange("u (q r) e -> r q u e", r=4)
         for r in range(4):
@@ -107,8 +135,6 @@ def tile_attend_pkv4_rel2_cap_kernel(tc, qT, k_words, k_scales, v_words, v_scale
                 vsc_rows[r].bitcast(I32),
             )
 
-        q_codes = keep.tile([P, PASSES * NQ], U32, name="q_codes", align_bytes=64)
-        q_scales = keep.tile([P, PASSES * NQ], U8, name="q_scales", align_bytes=64)
         pairs = {}
         keys = {}
         vs_turned = {}
@@ -125,8 +151,11 @@ def tile_attend_pkv4_rel2_cap_kernel(tc, qT, k_words, k_scales, v_words, v_scale
             if e == 0:
                 area = work.tile([P, 4 * PAGE], U32, name="first_pairs", align_bytes=64, offset=3 * SLOT_BYTES)
                 pairs[e] = area[:, 0:PAGE]
+            elif e == 1:
+                own = work.tile([P, PAGE], U32, name="pairs%d" % e, align_bytes=64, offset=0)
+                pairs[e] = own[:]
             else:
-                own = work.tile([P, PAGE], U32, name="pairs%d" % e, align_bytes=64, offset=(e - 1) * SLOT_BYTES)
+                own = late.tile([P, PAGE], U32, name="pairs%d" % e, align_bytes=64, offset=e * SLOT_BYTES)
                 pairs[e] = own[:]
             nc.vector.tensor_copy(
                 pairs[e], kw_pool[:].bitcast(U32).indirect(slots[:, e * PAGE // 16 : (e + 1) * PAGE // 16])
@@ -137,7 +166,10 @@ def tile_attend_pkv4_rel2_cap_kernel(tc, qT, k_words, k_scales, v_words, v_scale
             width = PAGE // parts
             keys[e] = []
             for h in range(parts):
-                part = keep.tile([P, PASSES, 2 * width], U8, name="keys%d_%d" % (e, h), align_bytes=64)
+                if e + h == 1:
+                    part = late.tile([P, PASSES, 2 * width], U8, name="keys%d_%d" % (e, h), align_bytes=64, offset=e * SLOT_BYTES)
+                else:
+                    part = keep.tile([P, PASSES, 2 * width], U8, name="keys%d_%d" % (e, h), align_bytes=64)
                 nc.vector.tensor_copy(
                     part[:].bitcast(U16),
                     pairs[e][:, h * width : (h + 1) * width].bitcast(U16).rearrange("p (n g) -> p g n", g=PASSES),
@@ -169,10 +201,10 @@ def tile_attend_pkv4_rel2_cap_kernel(tc, qT, k_words, k_scales, v_words, v_scale
                     for g in range(PASSES):
                         nc.tensor.matmul_mx(
                             out=scores[:, n0 : n0 + step],
-                            lhsT=q_codes[:, g * NQ : (g + 1) * NQ].bitcast(FP8X4),
-                            lhsT_scale=q_scales[:, g * NQ : (g + 1) * NQ],
+                            lhsT=q_codes[g][:, 0:NQ].bitcast(FP8X4),
+                            lhsT_scale=q_scales[g][:, 0:NQ],
                             rhs=keys[e][h][:, g, 2 * n0 : 2 * (n0 + step)].bitcast(FP4X4),
-                            rhs_scale=ks_planes[:, g, slot0 : slot0 + step],
+                            rhs_scale=ks_planes[slot0 // GROUP][:, g, slot0 % GROUP : slot0 % GROUP + step],
                             start=(g == 0),
                             stop=(g == PASSES - 1),
                         )
@@ -227,29 +259,32 @@ def tile_attend_pkv4_rel2_cap_kernel(tc, qT, k_words, k_scales, v_words, v_scale
             by_place = keep.tile([P, PACK, NQ], BF16, name="by_place%d" % e, align_bytes=64)
             for t in range(PACK):
                 nc.scalar.activation(by_place[:, t, :], turned[e][:, t, :], ACT.Copy, scale=vs_turned[e][:, t : t + 1])
+            nc.scalar.activation(sums_copy[:], sums[:], ACT.Copy, accum_out=denom[:])
             w_bf[e] = keep.tile([P, NQ, PACK], BF16, name="w_bf%d" % e, align_bytes=64)
             nc.scalar.copy(w_bf[e][:], by_place[:].rearrange("s t q -> s q t"))
 
+        denom = keep.tile([P, 1], F32, name="denom")
+        sums_copy = keep.tile(list(sums.shape), F32, name="sums_copy")
         token_scales(0, PAGES)
         vw_pool = work.tile([P, POOL_PAGES * DV], I32, name="vw_pool", align_bytes=64, offset=(WORK_SLOTS - 1) * SLOT_BYTES)
         nc.sync.dma_start(
             vw_pool[:].rearrange("p (u e) -> p u e", u=POOL_PAGES),
             v_words.rearrange("u p e r -> p u (e r)").bitcast(I32),
         )
-        nc.vector.quantize_mx(
-            out=q_codes[:].bitcast(FP8X4), scales=q_scales[:], in_=q_flat
-        )
+        quantise_queries(0)
         clock_up = psum.tile([P, 2, PASSES * NQ], F32, name="clock_up", tag="bank7")
         for i in range(WARM_PASSES):
             nc.tensor.matmul_mx(
                 out=clock_up[:, i % 2, :],
-                lhsT=q_codes[:, 0:NQ].bitcast(FP8X4),
-                lhsT_scale=q_scales[:, 0:NQ],
-                rhs=q_codes[:].bitcast(FP8X4),
-                rhs_scale=q_scales[:],
+                lhsT=q_codes[0][:, 0:NQ].bitcast(FP8X4),
+                lhsT_scale=q_scales[0][:, 0:NQ],
+                rhs=q_codes[0][:].bitcast(FP8X4),
+                rhs_scale=q_scales[0][:],
                 start=True,
                 stop=True,
             )
+        cast_queries(1)
+        quantise_queries(1)
         for e in range(PAGES):
             gather_keys(e)
             part_keys(e)
@@ -274,11 +309,9 @@ def tile_attend_pkv4_rel2_cap_kernel(tc, qT, k_words, k_scales, v_words, v_scale
         nc.vector.tensor_copy(vw[:], vw_pool[:].bitcast(U32).indirect(vcols[:]))
         nc.vector.tensor_copy(vsc[:], vsc_pool[:].indirect(vcols[:]))
         acc = psum.tile([P, DV], F32, name="acc", tag="bank%d" % TURN_BANKS[1])
-        denom = keep.tile([P, 1], F32, name="denom")
         inverse = keep.tile([P, 1], F32, name="inverse")
         for e in (2, 3, 1):
             scale_on_vector(e)
-        nc.vector.tensor_reduce(denom[:], sums[:], axis=AX.X, op=ALU.add)
         nc.vector.reciprocal(inverse[:], denom[:])
         order = (2, 3, 0, 1)
         for e in order:

@@ -26,7 +26,8 @@ PAGES = N // PAGE
 POOL_PAGES = T // PAGE
 PASSES = D // (P * PACK)
 SCALE_ROWS = 16
-ON_VECTOR = (2, 3)
+ON_VECTOR = (2,)
+RECTIFIED_ON_VECTOR = 3
 WARM_PASSES = 4
 ON_SCALAR = 0
 KS_ROW0 = P - PASSES * SCALE_ROWS
@@ -51,6 +52,7 @@ def tile_attend_pkv4_rel2_cap_kernel(tc, qT, k_words, k_scales, v_words, v_scale
         early = ctx.enter_context(tc.tile_pool(name="early", bufs=1))
         late = ctx.enter_context(tc.tile_pool(name="late", bufs=1))
         wide = ctx.enter_context(tc.tile_pool(name="wide", bufs=1))
+        last = ctx.enter_context(tc.tile_pool(name="last", bufs=1))
         psum = ctx.enter_context(tc.psum_pool(name="psum", bufs=1))
 
         slots = lists.tile([P, N // 16], U16, name="slots")
@@ -70,7 +72,7 @@ def tile_attend_pkv4_rel2_cap_kernel(tc, qT, k_words, k_scales, v_words, v_scale
         nc.sync.dma_start(kw_pool[:], k_words[0].rearrange("p t b -> p (t b)").bitcast(I32))
         nc.sync.dma_start(q_raw[1], q_rows[1])
 
-        sums = keep.tile([P, 1 + 2 * PAGES - len(ON_VECTOR)], F32, name="sums")
+        sums = keep.tile([P, 1 + PAGES], F32, name="sums")
         nc.vector.memset(sums[:, 0:1], 1.0 / (CAP * CAP))
         warm = keep.tile([P, 1], F32, name="warm")
         nc.scalar.activation(warm[:], sums[:, 0:1], ACT.Tanh)
@@ -209,28 +211,36 @@ def tile_attend_pkv4_rel2_cap_kernel(tc, qT, k_words, k_scales, v_words, v_scale
                             stop=(g == PASSES - 1),
                         )
                 placed.append(scores[:].rearrange("q (s t) -> q t s", t=PACK))
-            weights[e] = keep.tile([P, PACK, P], F32, name="weights%d" % e)
-            if e in ON_VECTOR:
-                pieces[e] = [(placed[0], weights[e][:])]
-            elif parts == 2:
-                pieces[e] = [(placed[h], weights[e][:, :, h * P // 2 : (h + 1) * P // 2]) for h in range(2)]
+            if e == RECTIFIED_ON_VECTOR:
+                weights[e] = last.tile([P, PACK, P], F32, name="weights%d" % e, align_bytes=64, offset=SLOT_BYTES)
             else:
-                pieces[e] = [(placed[0][:, 2 * h : 2 * h + 2, :], weights[e][:, 2 * h : 2 * h + 2, :]) for h in range(2)]
+                weights[e] = keep.tile([P, PACK, P], F32, name="weights%d" % e)
+            pieces[e] = placed
 
         def cap(e):
             capped[e] = []
-            for h, (source, target) in enumerate(pieces[e]):
-                tile = keep.tile(list(target.shape), F32, name="capped%d_%d" % (e, h))
+            for h, source in enumerate(pieces[e]):
+                if e == RECTIFIED_ON_VECTOR:
+                    tile = last.tile(list(source.shape), F32, name="capped%d_%d" % (e, h), align_bytes=64, offset=0)
+                elif e in ON_VECTOR:
+                    tile = work.tile(list(source.shape), F32, name="capped%d_%d" % (e, h), align_bytes=64, offset=5 * SLOT_BYTES)
+                else:
+                    tile = keep.tile(list(source.shape), F32, name="capped%d_%d" % (e, h))
                 nc.scalar.activation(tile[:], source, ACT.Tanh, scale=1.0 / CAP)
                 capped[e].append(tile)
 
-        def rectify(e, h):
-            kept = keep.tile(list(pieces[e][h][1].shape), F32, name="positive%d_%d" % (e, h))
-            nc.scalar.activation(kept[:], capped[e][h][:], ACT.Relu)
-            positive.setdefault(e, []).append(kept)
+        def rectify(e):
+            positive[e] = keep.tile([P, PACK, P], F32, name="positive%d" % e)
+            width = P // len(capped[e])
+            for h, tile in enumerate(capped[e]):
+                target = positive[e][:, :, h * width : (h + 1) * width]
+                if e == RECTIFIED_ON_VECTOR:
+                    nc.vector.tensor_scalar_max(target, tile[:], 0.0)
+                else:
+                    nc.scalar.activation(target, tile[:], ACT.Relu)
 
         def square(e):
-            column = 1 + 2 * e - len([other for other in ON_VECTOR if other < e])
+            column = 1 + e
             if e in ON_VECTOR:
                 flat = capped[e][0][:].rearrange("q t s -> q (t s)")
                 nc.vector.scalar_tensor_tensor(
@@ -238,10 +248,7 @@ def tile_attend_pkv4_rel2_cap_kernel(tc, qT, k_words, k_scales, v_words, v_scale
                     accum_out=sums[:, column : column + 1],
                 )
             else:
-                for h, kept in enumerate(positive[e]):
-                    nc.scalar.activation(
-                        pieces[e][h][1], kept[:], ACT.Square, accum_out=sums[:, column + h : column + h + 1]
-                    )
+                nc.scalar.activation(weights[e][:], positive[e][:], ACT.Square, accum_out=sums[:, column : column + 1])
             turned[e] = psum.tile([P, PACK, NQ], F32, name="turned%d" % e, tag="bank%d" % TURN_BANKS[e])
             for t in range(PACK):
                 nc.tensor.transpose(turned[e][:, t, :], weights[e][:, t, :], identity[:])
@@ -256,7 +263,7 @@ def tile_attend_pkv4_rel2_cap_kernel(tc, qT, k_words, k_scales, v_words, v_scale
             )
 
         def scale_on_scalar(e):
-            by_place = keep.tile([P, PACK, NQ], BF16, name="by_place%d" % e, align_bytes=64)
+            by_place = last.tile([P, PACK, NQ], BF16, name="by_place%d" % e, align_bytes=64, offset=0)
             for t in range(PACK):
                 nc.scalar.activation(by_place[:, t, :], turned[e][:, t, :], ACT.Copy, scale=vs_turned[e][:, t : t + 1])
             nc.scalar.activation(sums_copy[:], sums[:], ACT.Copy, accum_out=denom[:])
@@ -265,12 +272,12 @@ def tile_attend_pkv4_rel2_cap_kernel(tc, qT, k_words, k_scales, v_words, v_scale
 
         denom = keep.tile([P, 1], F32, name="denom")
         sums_copy = keep.tile(list(sums.shape), F32, name="sums_copy")
-        token_scales(0, PAGES)
         vw_pool = work.tile([P, POOL_PAGES * DV], I32, name="vw_pool", align_bytes=64, offset=(WORK_SLOTS - 1) * SLOT_BYTES)
         nc.sync.dma_start(
             vw_pool[:].rearrange("p (u e) -> p u e", u=POOL_PAGES),
             v_words.rearrange("u p e r -> p u (e r)").bitcast(I32),
         )
+        token_scales(0, PAGES)
         quantise_queries(0)
         clock_up = psum.tile([P, 2, PASSES * NQ], F32, name="clock_up", tag="bank7")
         for i in range(WARM_PASSES):
@@ -291,31 +298,30 @@ def tile_attend_pkv4_rel2_cap_kernel(tc, qT, k_words, k_scales, v_words, v_scale
         for e in range(PAGES):
             score(e)
         cap(0)
-        rectify(0, 0)
-        rectify(0, 1)
-        square(0)
+        rectify(0)
         cap(1)
-        rectify(1, 0)
+        square(0)
+        rectify(1)
         cap(2)
         cap(3)
-        rectify(1, 1)
         square(2)
-        square(3)
+        rectify(3)
         square(1)
+        square(3)
         scale_on_scalar(ON_SCALAR)
 
         vw = work.tile([P, PAGES * DV], U32, name="vw", align_bytes=64, offset=5 * SLOT_BYTES)
         vsc = work.tile([P, PAGES * DV], U8, name="vsc", align_bytes=64, offset=6 * SLOT_BYTES)
         nc.vector.tensor_copy(vw[:], vw_pool[:].bitcast(U32).indirect(vcols[:]))
         nc.vector.tensor_copy(vsc[:], vsc_pool[:].indirect(vcols[:]))
-        acc = psum.tile([P, DV], F32, name="acc", tag="bank%d" % TURN_BANKS[1])
+        acc = psum.tile([P, DV], F32, name="acc", tag="bank%d" % TURN_BANKS[3])
         inverse = keep.tile([P, 1], F32, name="inverse")
-        for e in (2, 3, 1):
+        for e in (2, 1, 3):
             scale_on_vector(e)
         nc.vector.reciprocal(inverse[:], denom[:])
-        order = (2, 3, 0, 1)
+        order = (2, 1, 3, 0)
         for e in order:
-            w_codes = keep.tile([P, NQ], U32, name="w_codes%d" % e, align_bytes=64)
+            w_codes = last.tile([P, NQ], U32, name="w_codes%d" % e, align_bytes=64, offset=SLOT_BYTES + e * NQ * 4)
             w_scales = keep.tile([P, NQ], U8, name="w_scales%d" % e, align_bytes=64)
             nc.vector.quantize_mx(
                 out=w_codes[:].bitcast(FP8X4),

@@ -28,7 +28,6 @@ PASSES = D // (P * PACK)
 SCALE_ROWS = 16
 ON_VECTOR = (2,)
 RECTIFIED_ON_VECTOR = 3
-WARM_PASSES = 4
 ON_SCALAR = 0
 KS_ROW0 = P - PASSES * SCALE_ROWS
 HALF = PAGE // 2
@@ -81,10 +80,8 @@ def tile_attend_pkv4_rel2_cap_kernel(tc, qT, k_words, k_scales, v_words, v_scale
         nc.vector.memset(vs_pool[0 : P - 1, SPREAD:T], 0.0)
         vsc_pool = keep.tile([P, POOL_PAGES * DV], U8, name="vsc_pool", align_bytes=64)
         nc.vector.memset(vsc_pool[:].bitcast(I32), 0)
-        q_codes = [keep.tile([P, (2 - g) * NQ], U32, name="q_codes%d" % g, align_bytes=64) for g in range(PASSES)]
-        q_scales = [keep.tile([P, (2 - g) * NQ], U8, name="q_scales%d" % g, align_bytes=64) for g in range(PASSES)]
-        nc.vector.memset(q_codes[0][:, NQ : 2 * NQ].bitcast(I32), 0)
-        nc.vector.memset(q_scales[0][:, NQ : 2 * NQ].bitcast(I32), 0)
+        q_codes = [keep.tile([P, NQ], U32, name="q_codes%d" % g, align_bytes=64) for g in range(PASSES)]
+        q_scales = [keep.tile([P, NQ], U8, name="q_scales%d" % g, align_bytes=64) for g in range(PASSES)]
         identity = keep.tile([P, P], F32, name="identity")
         make_identity(nc, identity[:])
 
@@ -279,17 +276,6 @@ def tile_attend_pkv4_rel2_cap_kernel(tc, qT, k_words, k_scales, v_words, v_scale
         )
         token_scales(0, PAGES)
         quantise_queries(0)
-        clock_up = psum.tile([P, 2, PASSES * NQ], F32, name="clock_up", tag="bank7")
-        for i in range(WARM_PASSES):
-            nc.tensor.matmul_mx(
-                out=clock_up[:, i % 2, :],
-                lhsT=q_codes[0][:, 0:NQ].bitcast(FP8X4),
-                lhsT_scale=q_scales[0][:, 0:NQ],
-                rhs=q_codes[0][:].bitcast(FP8X4),
-                rhs_scale=q_scales[0][:],
-                start=True,
-                stop=True,
-            )
         cast_queries(1)
         quantise_queries(1)
         for e in range(PAGES):

@@ -144,6 +144,7 @@ def tile_attend_pkv4_rel2_cap_kernel(tc, qT, k_words, k_scales, v_words, v_scale
         positive = {}
         w_bf = {}
         SCORE_BANKS = ((0, 1), (2,), (3,), (4,))
+        PARTS = (2, 2, 2, 1)
         TURN_BANKS = (5, 6, 0, 1)
 
         def gather_keys(e):
@@ -161,12 +162,15 @@ def tile_attend_pkv4_rel2_cap_kernel(tc, qT, k_words, k_scales, v_words, v_scale
             )
 
         def part_keys(e):
-            parts = len(SCORE_BANKS[e])
+            parts = PARTS[e]
             width = PAGE // parts
             keys[e] = []
             for h in range(parts):
-                if e + h == 1:
-                    part = late.tile([P, PASSES, 2 * width], U8, name="keys%d_%d" % (e, h), align_bytes=64, offset=e * SLOT_BYTES)
+                if e == 1 or e + h == 1:
+                    part = late.tile(
+                        [P, PASSES, 2 * width], U8, name="keys%d_%d" % (e, h), align_bytes=64,
+                        offset=e * SLOT_BYTES + e * h * SLOT_BYTES // 2,
+                    )
                 else:
                     part = keep.tile([P, PASSES, 2 * width], U8, name="keys%d_%d" % (e, h), align_bytes=64)
                 nc.vector.tensor_copy(
@@ -191,7 +195,7 @@ def tile_attend_pkv4_rel2_cap_kernel(tc, qT, k_words, k_scales, v_words, v_scale
         def score(e):
             parts = len(SCORE_BANKS[e])
             width = PAGE // parts
-            step = PAGE if parts == 1 else P
+            step = PAGE // PARTS[e]
             placed = []
             for h in range(parts):
                 scores = psum.tile([P, width], F32, name="scores%d_%d" % (e, h), tag="bank%d" % SCORE_BANKS[e][h])
@@ -202,7 +206,7 @@ def tile_attend_pkv4_rel2_cap_kernel(tc, qT, k_words, k_scales, v_words, v_scale
                             out=scores[:, n0 : n0 + step],
                             lhsT=q_codes[g][:, 0:NQ].bitcast(FP8X4),
                             lhsT_scale=q_scales[g][:, 0:NQ],
-                            rhs=keys[e][h][:, g, 2 * n0 : 2 * (n0 + step)].bitcast(FP4X4),
+                            rhs=keys[e][(h * width + n0) // step][:, g, :].bitcast(FP4X4),
                             rhs_scale=ks_planes[slot0 // GROUP][:, g, slot0 % GROUP : slot0 % GROUP + step],
                             start=(g == 0),
                             stop=(g == PASSES - 1),

@@ -48,7 +48,6 @@ def tile_attend_pkv4_rel2_cap_kernel(tc, qT, k_words, k_scales, v_words, v_scale
         keep = ctx.enter_context(tc.tile_pool(name="keep", bufs=1))
         reused = ctx.enter_context(tc.tile_pool(name="reused", bufs=1))
         work = ctx.enter_context(tc.tile_pool(name="work", bufs=1))
-        early = ctx.enter_context(tc.tile_pool(name="early", bufs=1))
         late = ctx.enter_context(tc.tile_pool(name="late", bufs=1))
         wide = ctx.enter_context(tc.tile_pool(name="wide", bufs=1))
         last = ctx.enter_context(tc.tile_pool(name="last", bufs=1))
@@ -57,7 +56,7 @@ def tile_attend_pkv4_rel2_cap_kernel(tc, qT, k_words, k_scales, v_words, v_scale
         slots = lists.tile([P, N // 16], U16, name="slots")
         vcols = lists.tile([P, PAGES * DV // 16], U16, name="vcols")
         ks_pool = reused.tile([P, T], U8, name="ks_pool", align_bytes=64, offset=0)
-        vs_runs = early.tile([P, RUN], F32, name="vs_runs", align_bytes=64, offset=0)
+        vs_runs = keep.tile([P, RUN], F32, name="vs_runs", align_bytes=64)
         vs_pool = wide.tile([P, T], F32, name="vs_pool", align_bytes=64, offset=0)
         raw_area = work.tile([P, WORK_SLOTS * PAGE], F32, name="raw_area", align_bytes=64, offset=0)
         late_area = late.tile([P, 4 * PAGE], F32, name="late_area", align_bytes=64, offset=0)
@@ -96,10 +95,13 @@ def tile_attend_pkv4_rel2_cap_kernel(tc, qT, k_words, k_scales, v_words, v_scale
         q_bf = {}
 
         def cast_queries(g):
-            q_bf[g] = (early, wide)[g].tile([P, NQ, PACK], BF16, name="q_bf%d" % g, align_bytes=64, offset=0)
-            nc.scalar.copy(q_bf[g][:], q_raw[g].rearrange("p j w -> p w j"))
+            if g == 0:
+                q_bf[g] = keep.tile([P, NQ, PACK], BF16, name="q_bf%d" % g, align_bytes=64)
+                nc.vector.tensor_copy(q_bf[g][:], q_raw[g].rearrange("p j w -> p w j"))
+            else:
+                q_bf[g] = wide.tile([P, NQ, PACK], BF16, name="q_bf%d" % g, align_bytes=64, offset=0)
+                nc.scalar.copy(q_bf[g][:], q_raw[g].rearrange("p j w -> p w j"))
 
-        cast_queries(0)
 
         def quantise_queries(g):
             nc.vector.quantize_mx(
@@ -110,6 +112,8 @@ def tile_attend_pkv4_rel2_cap_kernel(tc, qT, k_words, k_scales, v_words, v_scale
 
         ks_listed = keep.tile([P, N], U8, name="ks_listed", align_bytes=64)
         nc.vector.tensor_copy(ks_listed[:], ks_pool[:].indirect(slots[:]))
+        cast_queries(0)
+        quantise_queries(0)
         ks_planes = []
 
         def move_key_scales(a):
@@ -149,10 +153,10 @@ def tile_attend_pkv4_rel2_cap_kernel(tc, qT, k_words, k_scales, v_words, v_scale
 
         def gather_keys(e):
             if e == 0:
-                area = work.tile([P, 4 * PAGE], U32, name="first_pairs", align_bytes=64, offset=3 * SLOT_BYTES)
-                pairs[e] = area[:, 0:PAGE]
+                own = wide.tile([P, PAGE], U32, name="pairs%d" % e, align_bytes=64, offset=SLOT_BYTES)
+                pairs[e] = own[:]
             elif e == 1:
-                own = work.tile([P, PAGE], U32, name="pairs%d" % e, align_bytes=64, offset=0)
+                own = wide.tile([P, PAGE], U32, name="pairs%d" % e, align_bytes=64, offset=2 * SLOT_BYTES)
                 pairs[e] = own[:]
             else:
                 own = late.tile([P, PAGE], U32, name="pairs%d" % e, align_bytes=64, offset=e * SLOT_BYTES)
@@ -180,14 +184,12 @@ def tile_attend_pkv4_rel2_cap_kernel(tc, qT, k_words, k_scales, v_words, v_scale
                 keys[e].append(part)
 
         def token_scales(first, count):
-            if first < PAGES - 1:
-                listed = keep.tile([P, count, PAGE], F32, name="vs_listed%d" % first, align_bytes=64)
+            listed = keep.tile([P, count, PAGE], F32, name="vs_listed%d" % first, align_bytes=64)
+            looked_up = vs_pool[:].indirect(slots[:, first * PAGE // 16 : (first + count) * PAGE // 16])
+            if first == 0:
+                nc.vector.tensor_copy(listed[:].rearrange("p e n -> p (e n)"), looked_up)
             else:
-                listed = work.tile([P, count, PAGE], F32, name="vs_listed%d" % first, align_bytes=64, offset=3 * SLOT_BYTES)
-            nc.vector.tensor_copy(
-                listed[:].rearrange("p e n -> p (e n)"),
-                vs_pool[:].indirect(slots[:, first * PAGE // 16 : (first + count) * PAGE // 16]),
-            )
+                nc.scalar.activation(listed[:].rearrange("p e n -> p (e n)"), looked_up, ACT.Copy)
             for e in range(first, first + count):
                 vs_turned[e] = keep.tile([P, PACK], F32, name="vs_turned%d" % e)
                 nc.sync.dma_start(vs_turned[e][:], listed[P - 1 : P, e - first, :].rearrange("o (s t) -> o s t", t=PACK))
@@ -278,8 +280,8 @@ def tile_attend_pkv4_rel2_cap_kernel(tc, qT, k_words, k_scales, v_words, v_scale
             vw_pool[:].rearrange("p (u e) -> p u e", u=POOL_PAGES),
             v_words.rearrange("u p e r -> p u (e r)").bitcast(I32),
         )
-        token_scales(0, PAGES)
-        quantise_queries(0)
+        token_scales(0, PAGES // 2)
+        token_scales(PAGES // 2, PAGES // 2)
         cast_queries(1)
         quantise_queries(1)
         for e in range(PAGES):

@@ -18,7 +18,6 @@ FP8X4 = mybir.dt.float8_e4m3fn_x4
 FP4X4 = mybir.dt.float4_e2m1fn_x4
 ACT = mybir.ActivationFunctionType
 ALU = mybir.AluOpType
-AX = mybir.AxisListType
 
 P = 128
 PACK = 4
@@ -26,19 +25,15 @@ PAGES = N // PAGE
 POOL_PAGES = T // PAGE
 PASSES = D // (P * PACK)
 SCALE_ROWS = 16
-ON_VECTOR = (2,)
-RECTIFIED_ON_VECTOR = 3
-ON_SCALAR = 0
 KS_ROW0 = P - PASSES * SCALE_ROWS
-HALF = PAGE // 2
-SPREAD = 4 * PAGE
-GROUPS = 1
-GROUP = N // GROUPS
-RUN = SPREAD // P
-ZERO_PIECES = 2
-BANKS = 8
-SLOT_BYTES = 4 * PAGE
-WORK_SLOTS = 8
+VS_ROW = 0
+VSC_ROW0 = 16
+VS_ON_VECTOR = 1
+PARTS = (2, 1, 1, 2)
+SCORE_BANKS = ((0, 1), (2,), (3,), (4, 5))
+TURN_BANKS = (6, 7, 0, 1)
+ACC_BANK = 2
+SLOT = 4 * PAGE
 
 
 def tile_attend_pkv4_rel2_cap_kernel(tc, qT, k_words, k_scales, v_words, v_scales, vs, offs, voffs, out):
@@ -46,144 +41,61 @@ def tile_attend_pkv4_rel2_cap_kernel(tc, qT, k_words, k_scales, v_words, v_scale
     with ExitStack() as ctx:
         lists = ctx.enter_context(tc.tile_pool(name="lists", bufs=1))
         keep = ctx.enter_context(tc.tile_pool(name="keep", bufs=1))
-        reused = ctx.enter_context(tc.tile_pool(name="reused", bufs=1))
-        work = ctx.enter_context(tc.tile_pool(name="work", bufs=1))
+        ks_bytes = ctx.enter_context(tc.tile_pool(name="ks_bytes", bufs=1))
+        vsc_bytes = ctx.enter_context(tc.tile_pool(name="vsc_bytes", bufs=1))
         late = ctx.enter_context(tc.tile_pool(name="late", bufs=1))
-        wide = ctx.enter_context(tc.tile_pool(name="wide", bufs=1))
-        last = ctx.enter_context(tc.tile_pool(name="last", bufs=1))
         psum = ctx.enter_context(tc.psum_pool(name="psum", bufs=1))
 
         slots = lists.tile([P, N // 16], U16, name="slots")
         vcols = lists.tile([P, PAGES * DV // 16], U16, name="vcols")
-        ks_pool = reused.tile([P, T], U8, name="ks_pool", align_bytes=64, offset=0)
-        vs_runs = keep.tile([P, RUN], F32, name="vs_runs", align_bytes=64)
-        vs_pool = wide.tile([P, T], F32, name="vs_pool", align_bytes=64, offset=0)
-        raw_area = work.tile([P, WORK_SLOTS * PAGE], F32, name="raw_area", align_bytes=64, offset=0)
-        late_area = late.tile([P, 4 * PAGE], F32, name="late_area", align_bytes=64, offset=0)
-        q_raw = [area[:, 0 : PACK * NQ].rearrange("p (j w) -> p j w", j=PACK) for area in (raw_area, late_area)]
-        q_rows = qT[0].rearrange("(g p j) w -> g p j w", g=PASSES, j=PACK)
+        ks_pool = ks_bytes.tile([P, T], U8, name="ks_pool", align_bytes=64, offset=0)
+        vsc_pool = vsc_bytes.tile([P, POOL_PAGES * DV], U8, name="vsc_pool", align_bytes=64, offset=0)
+        vs_pool = keep.tile([P, T], F32, name="vs_pool", align_bytes=64)
         kw_pool = keep.tile([P, T], I32, name="kw_pool", align_bytes=64)
+        q_first = keep.tile([P, PACK * NQ], F32, name="q_first", align_bytes=64)
+        late_area = late.tile([P, 6 * PAGE], F32, name="late_area", align_bytes=64, offset=0)
+        q_raw = [area[:, 0 : PACK * NQ].rearrange("p (j w) -> p j w", j=PACK) for area in (q_first, late_area)]
+        q_rows = qT[0].rearrange("(g p j) w -> g p j w", g=PASSES, j=PACK)
+
         nc.sync.dma_start(ks_pool[KS_ROW0:P, :].bitcast(I32), k_scales.rearrange("g f t -> f g t").bitcast(I32))
         nc.sync.dma_start(slots[:], offs)
-        nc.scalar.dma_start(vs_runs[:], vs[0, 0:SPREAD].rearrange("(p c) -> p c", c=RUN))
+        nc.sync.dma_start(vcols[:], voffs)
         nc.sync.dma_start(q_raw[0], q_rows[0])
         nc.sync.dma_start(kw_pool[:], k_words[0].rearrange("p t b -> p (t b)").bitcast(I32))
         nc.sync.dma_start(q_raw[1], q_rows[1])
 
-        sums = keep.tile([P, 1 + PAGES], F32, name="sums")
+        nc.vector.memset(vsc_pool[:].bitcast(I32), 0)
+        nc.scalar.dma_start(
+            vsc_pool[VSC_ROW0 : VSC_ROW0 + SCALE_ROWS, :].bitcast(I32).rearrange("f (u e) -> f u e", u=POOL_PAGES),
+            v_scales.rearrange("u f e -> f u e").bitcast(I32),
+        )
+        sums = keep.tile([P, 2 + PAGES], F32, name="sums")
         nc.vector.memset(sums[:, 0:1], 1.0 / (CAP * CAP))
         warm = keep.tile([P, 1], F32, name="warm")
         nc.scalar.activation(warm[:], sums[:, 0:1], ACT.Tanh)
-        nc.scalar.dma_start(vs_pool[P - 1 : P, SPREAD:T], vs[0:1, SPREAD:T])
+        for h in range(2):
+            cols = slice(h * T // 2, (h + 1) * T // 2)
+            nc.vector.memset(vs_pool[:, cols], 0.0)
+            nc.scalar.dma_start(vs_pool[VS_ROW : VS_ROW + 1, cols], vs[0:1, cols])
         nc.vector.memset(ks_pool[0:KS_ROW0, :].bitcast(I32), 0)
-        nc.vector.memset(vs_pool[0 : P - 1, SPREAD:T], 0.0)
-        vsc_pool = keep.tile([P, POOL_PAGES * DV], U8, name="vsc_pool", align_bytes=64)
-        nc.vector.memset(vsc_pool[:].bitcast(I32), 0)
-        q_codes = [keep.tile([P, NQ], U32, name="q_codes%d" % g, align_bytes=64) for g in range(PASSES)]
-        q_scales = [keep.tile([P, NQ], U8, name="q_scales%d" % g, align_bytes=64) for g in range(PASSES)]
         identity = keep.tile([P, P], F32, name="identity")
         make_identity(nc, identity[:])
 
-        vs_by_run = vs_pool[:, 0:SPREAD].rearrange("i (p c) -> i p c", c=RUN)
-        for b in range(RUN // PACK):
-            spread = psum.tile([P, PACK, P], F32, name="spread%d" % b, tag="bank%d" % (b % BANKS))
-            for c in range(PACK):
-                column = b * PACK + c
-                nc.tensor.transpose(spread[:, c, :], vs_runs[:, column : column + 1].to_broadcast([P, P]), identity[:])
-            nc.scalar.copy(vs_by_run[:, :, b * PACK : (b + 1) * PACK], spread[:].rearrange("i c p -> i p c"))
-
-        q_bf = {}
+        q_bf = [keep.tile([P, NQ, PACK], BF16, name="q_bf%d" % g, align_bytes=64) for g in range(PASSES)]
+        q_codes = [keep.tile([P, NQ], U32, name="q_codes%d" % g, align_bytes=64) for g in range(PASSES)]
+        q_scales = [keep.tile([P, NQ], U8, name="q_scales%d" % g, align_bytes=64) for g in range(PASSES)]
 
         def cast_queries(g):
-            if g == 0:
-                q_bf[g] = keep.tile([P, NQ, PACK], BF16, name="q_bf%d" % g, align_bytes=64)
-                nc.vector.tensor_copy(q_bf[g][:], q_raw[g].rearrange("p j w -> p w j"))
-            else:
-                q_bf[g] = wide.tile([P, NQ, PACK], BF16, name="q_bf%d" % g, align_bytes=64, offset=0)
-                nc.scalar.copy(q_bf[g][:], q_raw[g].rearrange("p j w -> p w j"))
-
+            nc.scalar.copy(q_bf[g][:], q_raw[g].rearrange("p j w -> p w j"))
 
         def quantise_queries(g):
             nc.vector.quantize_mx(
-                out=q_codes[g][:, 0:NQ].bitcast(FP8X4),
-                scales=q_scales[g][:, 0:NQ],
-                in_=q_bf[g][:].rearrange("p w j -> p (w j)"),
+                out=q_codes[g][:].bitcast(FP8X4), scales=q_scales[g][:], in_=q_bf[g][:].rearrange("p w j -> p (w j)")
             )
 
-        ks_listed = keep.tile([P, N], U8, name="ks_listed", align_bytes=64)
-        nc.vector.tensor_copy(ks_listed[:], ks_pool[:].indirect(slots[:]))
-        cast_queries(0)
-        quantise_queries(0)
-        ks_planes = []
+        vs_listed = {}
 
-        def move_key_scales(a):
-            plane = reused.tile(
-                [P, PASSES, GROUP], U8, name="ks_planes%d" % a, align_bytes=64, offset=a * PASSES * GROUP
-            )
-            ks_planes.append(plane)
-            for quadrant in (0, 2, 1, 3):
-                row0 = KS_ROW0 + 4 * PASSES * quadrant
-                nc.sync.dma_start(
-                    plane[32 * quadrant : 32 * quadrant + 4, :, :].bitcast(I32),
-                    ks_listed[row0 : row0 + 4 * PASSES, a * GROUP : (a + 1) * GROUP].bitcast(I32),
-                )
-
-        move_key_scales(0)
-        nc.sync.dma_start(vcols[:], voffs)
-
-        vsc_rows = v_scales.rearrange("u (q r) e -> r q u e", r=4)
-        for r in range(4):
-            nc.sync.dma_start(
-                vsc_pool[r:P:32, :].bitcast(I32).rearrange("q (u e) -> q u e", u=POOL_PAGES),
-                vsc_rows[r].bitcast(I32),
-            )
-
-        pairs = {}
-        keys = {}
-        vs_turned = {}
-        turned = {}
-        weights = {}
-        pieces = {}
-        capped = {}
-        positive = {}
-        w_bf = {}
-        SCORE_BANKS = ((0, 1), (2,), (3,), (4,))
-        PARTS = (2, 2, 2, 1)
-        TURN_BANKS = (5, 6, 0, 1)
-
-        def gather_keys(e):
-            if e == 0:
-                own = wide.tile([P, PAGE], U32, name="pairs%d" % e, align_bytes=64, offset=SLOT_BYTES)
-                pairs[e] = own[:]
-            elif e == 1:
-                own = wide.tile([P, PAGE], U32, name="pairs%d" % e, align_bytes=64, offset=2 * SLOT_BYTES)
-                pairs[e] = own[:]
-            else:
-                own = late.tile([P, PAGE], U32, name="pairs%d" % e, align_bytes=64, offset=e * SLOT_BYTES)
-                pairs[e] = own[:]
-            nc.vector.tensor_copy(
-                pairs[e], kw_pool[:].bitcast(U32).indirect(slots[:, e * PAGE // 16 : (e + 1) * PAGE // 16])
-            )
-
-        def part_keys(e):
-            parts = PARTS[e]
-            width = PAGE // parts
-            keys[e] = []
-            for h in range(parts):
-                if e == 1 or e + h == 1:
-                    part = late.tile(
-                        [P, PASSES, 2 * width], U8, name="keys%d_%d" % (e, h), align_bytes=64,
-                        offset=e * SLOT_BYTES + e * h * SLOT_BYTES // 2,
-                    )
-                else:
-                    part = keep.tile([P, PASSES, 2 * width], U8, name="keys%d_%d" % (e, h), align_bytes=64)
-                nc.vector.tensor_copy(
-                    part[:].bitcast(U16),
-                    pairs[e][:, h * width : (h + 1) * width].bitcast(U16).rearrange("p (n g) -> p g n", g=PASSES),
-                )
-                keys[e].append(part)
-
-        def token_scales(first, count):
+        def gather_vs(first, count):
             listed = keep.tile([P, count, PAGE], F32, name="vs_listed%d" % first, align_bytes=64)
             looked_up = vs_pool[:].indirect(slots[:, first * PAGE // 16 : (first + count) * PAGE // 16])
             if first == 0:
@@ -191,73 +103,126 @@ def tile_attend_pkv4_rel2_cap_kernel(tc, qT, k_words, k_scales, v_words, v_scale
             else:
                 nc.scalar.activation(listed[:].rearrange("p e n -> p (e n)"), looked_up, ACT.Copy)
             for e in range(first, first + count):
-                vs_turned[e] = keep.tile([P, PACK], F32, name="vs_turned%d" % e)
-                nc.sync.dma_start(vs_turned[e][:], listed[P - 1 : P, e - first, :].rearrange("o (s t) -> o s t", t=PACK))
+                vs_listed[e] = listed[VS_ROW : VS_ROW + 1, e - first, :]
 
-        def score(e):
-            parts = len(SCORE_BANKS[e])
-            width = PAGE // parts
-            step = PAGE // PARTS[e]
-            placed = []
-            for h in range(parts):
-                scores = psum.tile([P, width], F32, name="scores%d_%d" % (e, h), tag="bank%d" % SCORE_BANKS[e][h])
-                for n0 in range(0, width, step):
-                    slot0 = e * PAGE + h * width + n0
-                    for g in range(PASSES):
-                        nc.tensor.matmul_mx(
-                            out=scores[:, n0 : n0 + step],
-                            lhsT=q_codes[g][:, 0:NQ].bitcast(FP8X4),
-                            lhsT_scale=q_scales[g][:, 0:NQ],
-                            rhs=keys[e][(h * width + n0) // step][:, g, :].bitcast(FP4X4),
-                            rhs_scale=ks_planes[slot0 // GROUP][:, g, slot0 % GROUP : slot0 % GROUP + step],
-                            start=(g == 0),
-                            stop=(g == PASSES - 1),
-                        )
-                placed.append(scores[:].rearrange("q (s t) -> q t s", t=PACK))
-            if e == RECTIFIED_ON_VECTOR:
-                weights[e] = last.tile([P, PACK, P], F32, name="weights%d" % e, align_bytes=64, offset=SLOT_BYTES)
+        ks_listed = keep.tile([P, N], U8, name="ks_listed", align_bytes=64)
+        nc.vector.tensor_copy(ks_listed[:], ks_pool[:].indirect(slots[:]))
+        cast_queries(0)
+        quantise_queries(0)
+        vsc_listed = keep.tile([P, PAGES * DV], U8, name="vsc_listed", align_bytes=64)
+        nc.vector.tensor_copy(vsc_listed[:], vsc_pool[:].indirect(vcols[:]))
+        gather_vs(0, VS_ON_VECTOR)
+        gather_vs(VS_ON_VECTOR, PAGES - VS_ON_VECTOR)
+
+        ks_planes = ks_bytes.tile([P, PASSES, N], U8, name="ks_planes", align_bytes=64, offset=0)
+        for quadrant in (0, 2, 1, 3):
+            row0 = KS_ROW0 + 4 * PASSES * quadrant
+            nc.sync.dma_start(
+                ks_planes[32 * quadrant : 32 * quadrant + 4, :, :].bitcast(I32),
+                ks_listed[row0 : row0 + 4 * PASSES, :].bitcast(I32),
+            )
+        vs_turned = []
+        for e in range(PAGES):
+            vs_turned.append(keep.tile([P, PACK], F32, name="vs_turned%d" % e))
+            nc.sync.dma_start(vs_turned[e][:], vs_listed[e].rearrange("o (s t) -> o s t", t=PACK))
+        vsc_plane = vsc_bytes.tile([P, PAGES * DV], U8, name="vsc_plane", align_bytes=64, offset=0)
+        for quadrant in (0, 2, 1, 3):
+            nc.sync.dma_start(
+                vsc_plane[32 * quadrant : 32 * quadrant + 4, :].bitcast(I32),
+                vsc_listed[VSC_ROW0 + 4 * quadrant : VSC_ROW0 + 4 * quadrant + 4, :].bitcast(I32),
+            )
+
+        cast_queries(1)
+        vw_pool = late.tile([P, POOL_PAGES * DV], I32, name="vw_pool", align_bytes=64, offset=4 * SLOT)
+        nc.scalar.dma_start(
+            vw_pool[:].rearrange("p (u e) -> p u e", u=POOL_PAGES),
+            v_words.rearrange("u p e r -> p u (e r)").bitcast(I32),
+        )
+
+        pairs = {}
+        keys = {}
+
+        def gather_keys(e):
+            if e < 2:
+                pairs[e] = keep.tile([P, PAGE], U32, name="pairs%d" % e, align_bytes=64)
             else:
-                weights[e] = keep.tile([P, PACK, P], F32, name="weights%d" % e)
-            pieces[e] = placed
+                pairs[e] = late.tile([P, PAGE], U32, name="pairs%d" % e, align_bytes=64, offset=e * SLOT)
+            nc.vector.tensor_copy(
+                pairs[e][:], kw_pool[:].bitcast(U32).indirect(slots[:, e * PAGE // 16 : (e + 1) * PAGE // 16])
+            )
 
-        def cap(e):
-            capped[e] = []
-            for h, source in enumerate(pieces[e]):
-                if e == RECTIFIED_ON_VECTOR:
-                    tile = last.tile(list(source.shape), F32, name="capped%d_%d" % (e, h), align_bytes=64, offset=0)
-                elif e in ON_VECTOR:
-                    tile = work.tile(list(source.shape), F32, name="capped%d_%d" % (e, h), align_bytes=64, offset=5 * SLOT_BYTES)
-                else:
-                    tile = keep.tile(list(source.shape), F32, name="capped%d_%d" % (e, h))
-                nc.scalar.activation(tile[:], source, ACT.Tanh, scale=1.0 / CAP)
-                capped[e].append(tile)
-
-        def rectify(e):
-            positive[e] = keep.tile([P, PACK, P], F32, name="positive%d" % e)
-            width = P // len(capped[e])
-            for h, tile in enumerate(capped[e]):
-                target = positive[e][:, :, h * width : (h + 1) * width]
-                if e == RECTIFIED_ON_VECTOR:
-                    nc.vector.tensor_scalar_max(target, tile[:], 0.0)
-                else:
-                    nc.scalar.activation(target, tile[:], ACT.Relu)
-
-        def square(e):
-            column = 1 + e
-            if e in ON_VECTOR:
-                flat = capped[e][0][:].rearrange("q t s -> q (t s)")
-                nc.vector.scalar_tensor_tensor(
-                    weights[e][:].rearrange("q t s -> q (t s)"), flat, 0.0, flat, ALU.max, ALU.mult,
-                    accum_out=sums[:, column : column + 1],
-                )
+        def part_keys(e, h):
+            width = PAGE // PARTS[e]
+            if e + h == 1:
+                part = late.tile([P, PASSES, 2 * width], U8, name="keys%d_%d" % (e, h), align_bytes=64, offset=e * SLOT)
             else:
-                nc.scalar.activation(weights[e][:], positive[e][:], ACT.Square, accum_out=sums[:, column : column + 1])
+                part = keep.tile([P, PASSES, 2 * width], U8, name="keys%d_%d" % (e, h), align_bytes=64)
+            nc.vector.tensor_copy(
+                part[:].bitcast(U16),
+                pairs[e][:, h * width : (h + 1) * width].bitcast(U16).rearrange("p (n g) -> p g n", g=PASSES),
+            )
+            keys[e, h] = part
+
+        gather_keys(0)
+        gather_keys(1)
+        part_keys(0, 0)
+        quantise_queries(1)
+        part_keys(0, 1)
+        part_keys(1, 0)
+        gather_keys(2)
+        gather_keys(3)
+        part_keys(2, 0)
+        part_keys(3, 0)
+        part_keys(3, 1)
+        vw = keep.tile([P, PAGES * DV], U32, name="vw", align_bytes=64)
+        nc.vector.tensor_copy(vw[:], vw_pool[:].bitcast(U32).indirect(vcols[:]))
+
+        scores = {}
+        for e in range(PAGES):
+            width = PAGE // PARTS[e]
+            for h in range(PARTS[e]):
+                bank = psum.tile([P, width], F32, name="scores%d_%d" % (e, h), tag="bank%d" % SCORE_BANKS[e][h])
+                slot0 = e * PAGE + h * width
+                for g in range(PASSES):
+                    nc.tensor.matmul_mx(
+                        out=bank[:],
+                        lhsT=q_codes[g][:].bitcast(FP8X4),
+                        lhsT_scale=q_scales[g][:],
+                        rhs=keys[e, h][:, g, :].bitcast(FP4X4),
+                        rhs_scale=ks_planes[:, g, slot0 : slot0 + width],
+                        start=(g == 0),
+                        stop=(g == PASSES - 1),
+                    )
+                scores[e, h] = bank[:].rearrange("q (s t) -> q t s", t=PACK)
+
+        capped = {}
+        weights = [keep.tile([P, PACK, P], F32, name="weights%d" % e) for e in range(PAGES)]
+        positive = keep.tile([P, PACK, P], F32, name="positive")
+        turned = {}
+        w_bf = [keep.tile([P, NQ, PACK], BF16, name="w_bf%d" % e, align_bytes=64) for e in range(PAGES)]
+
+        def cap(e, h):
+            capped[e, h] = keep.tile(list(scores[e, h].shape), F32, name="capped%d_%d" % (e, h))
+            nc.scalar.activation(capped[e, h][:], scores[e, h], ACT.Tanh, scale=1.0 / CAP)
+
+        def rectify_first(h):
+            width = P // PARTS[0]
+            nc.scalar.activation(positive[:, :, h * width : (h + 1) * width], capped[0, h][:], ACT.Relu)
+
+        def square_on_vector(e, h):
+            width = P // PARTS[e]
+            column = 1 + e + h
+            nc.vector.scalar_tensor_tensor(
+                weights[e][:, :, h * width : (h + 1) * width], capped[e, h][:], 0.0, capped[e, h][:], ALU.max, ALU.mult,
+                accum_out=sums[:, column : column + 1],
+            )
+
+        def turn(e):
             turned[e] = psum.tile([P, PACK, NQ], F32, name="turned%d" % e, tag="bank%d" % TURN_BANKS[e])
             for t in range(PACK):
                 nc.tensor.transpose(turned[e][:, t, :], weights[e][:, t, :], identity[:])
 
         def scale_on_vector(e):
-            w_bf[e] = keep.tile([P, NQ, PACK], BF16, name="w_bf%d" % e, align_bytes=64)
             nc.vector.tensor_tensor(
                 w_bf[e][:],
                 turned[e][:].rearrange("s t q -> s q t"),
@@ -265,70 +230,58 @@ def tile_attend_pkv4_rel2_cap_kernel(tc, qT, k_words, k_scales, v_words, v_scale
                 ALU.mult,
             )
 
-        def scale_on_scalar(e):
-            by_place = last.tile([P, PACK, NQ], BF16, name="by_place%d" % e, align_bytes=64, offset=0)
-            for t in range(PACK):
-                nc.scalar.activation(by_place[:, t, :], turned[e][:, t, :], ACT.Copy, scale=vs_turned[e][:, t : t + 1])
-            nc.scalar.activation(sums_copy[:], sums[:], ACT.Copy, accum_out=denom[:])
-            w_bf[e] = keep.tile([P, NQ, PACK], BF16, name="w_bf%d" % e, align_bytes=64)
-            nc.scalar.copy(w_bf[e][:], by_place[:].rearrange("s t q -> s q t"))
+        acc = psum.tile([P, DV], F32, name="acc", tag="bank%d" % ACC_BANK)
 
-        denom = keep.tile([P, 1], F32, name="denom")
-        sums_copy = keep.tile(list(sums.shape), F32, name="sums_copy")
-        vw_pool = work.tile([P, POOL_PAGES * DV], I32, name="vw_pool", align_bytes=64, offset=(WORK_SLOTS - 1) * SLOT_BYTES)
-        nc.sync.dma_start(
-            vw_pool[:].rearrange("p (u e) -> p u e", u=POOL_PAGES),
-            v_words.rearrange("u p e r -> p u (e r)").bitcast(I32),
-        )
-        token_scales(0, PAGES // 2)
-        token_scales(PAGES // 2, PAGES // 2)
-        cast_queries(1)
-        quantise_queries(1)
-        for e in range(PAGES):
-            gather_keys(e)
-            part_keys(e)
-        for e in range(PAGES):
-            score(e)
-        cap(0)
-        rectify(0)
-        cap(1)
-        square(0)
-        rectify(1)
-        cap(2)
-        cap(3)
-        square(2)
-        rectify(3)
-        square(1)
-        square(3)
-        scale_on_scalar(ON_SCALAR)
-
-        vw = work.tile([P, PAGES * DV], U32, name="vw", align_bytes=64, offset=5 * SLOT_BYTES)
-        vsc = work.tile([P, PAGES * DV], U8, name="vsc", align_bytes=64, offset=6 * SLOT_BYTES)
-        nc.vector.tensor_copy(vw[:], vw_pool[:].bitcast(U32).indirect(vcols[:]))
-        nc.vector.tensor_copy(vsc[:], vsc_pool[:].indirect(vcols[:]))
-        acc = psum.tile([P, DV], F32, name="acc", tag="bank%d" % TURN_BANKS[3])
-        inverse = keep.tile([P, 1], F32, name="inverse")
-        for e in (2, 1, 3):
-            scale_on_vector(e)
-        nc.vector.reciprocal(inverse[:], denom[:])
-        order = (2, 1, 3, 0)
-        for e in order:
-            w_codes = last.tile([P, NQ], U32, name="w_codes%d" % e, align_bytes=64, offset=SLOT_BYTES + e * NQ * 4)
+        def multiply(e):
+            w_codes = keep.tile([P, NQ], U32, name="w_codes%d" % e, align_bytes=64)
             w_scales = keep.tile([P, NQ], U8, name="w_scales%d" % e, align_bytes=64)
             nc.vector.quantize_mx(
-                out=w_codes[:].bitcast(FP8X4),
-                scales=w_scales[:],
-                in_=w_bf[e][:].rearrange("s q t -> s (q t)"),
+                out=w_codes[:].bitcast(FP8X4), scales=w_scales[:], in_=w_bf[e][:].rearrange("s q t -> s (q t)")
             )
             nc.tensor.matmul_mx(
                 out=acc[:],
                 lhsT=w_codes[:].bitcast(FP8X4),
                 lhsT_scale=w_scales[:],
                 rhs=vw[:, e * DV : (e + 1) * DV].bitcast(FP8X4),
-                rhs_scale=vsc[:, e * DV : (e + 1) * DV],
-                start=(e == order[0]),
-                stop=(e == order[-1]),
+                rhs_scale=vsc_plane[:, e * DV : (e + 1) * DV],
+                start=(e == 0),
+                stop=(e == PAGES - 1),
             )
+
+        cap(0, 0)
+        cap(0, 1)
+        rectify_first(0)
+        rectify_first(1)
+        cap(1, 0)
+        nc.scalar.activation(weights[0][:], positive[:], ACT.Square, accum_out=sums[:, 1:2])
+        cap(2, 0)
+        cap(3, 0)
+        cap(3, 1)
+        turn(0)
+        square_on_vector(1, 0)
+        turn(1)
+        square_on_vector(2, 0)
+        turn(2)
+        square_on_vector(3, 0)
+        square_on_vector(3, 1)
+        turn(3)
+
+        by_place = keep.tile([P, PACK, NQ], BF16, name="by_place", align_bytes=64)
+        for t in range(PACK):
+            nc.scalar.activation(by_place[:, t, :], turned[0][:, t, :], ACT.Copy, scale=vs_turned[0][:, t : t + 1])
+        nc.scalar.copy(w_bf[0][:], by_place[:].rearrange("s t q -> s q t"))
+        denom = keep.tile([P, 1], F32, name="denom")
+        sums_copy = keep.tile(list(sums.shape), F32, name="sums_copy")
+        nc.scalar.activation(sums_copy[:], sums[:], ACT.Copy, accum_out=denom[:])
+
+        scale_on_vector(1)
+        scale_on_vector(2)
+        multiply(0)
+        scale_on_vector(3)
+        inverse = keep.tile([P, 1], F32, name="inverse")
+        nc.vector.reciprocal(inverse[:], denom[:])
+        for e in range(1, PAGES):
+            multiply(e)
 
         result = keep.tile([P, DV], F32, name="result")
         nc.scalar.activation(result[:], acc[:], ACT.Copy, scale=inverse[:])

@@ -26,13 +26,12 @@ POOL_PAGES = T // PAGE
 PASSES = D // (P * PACK)
 SCALE_ROWS = 16
 KS_ROW0 = P - PASSES * SCALE_ROWS
-VS_ROW = 0
-VSC_ROW0 = 16
-VS_ON_VECTOR = 1
+VS_ON_VECTOR = 640
 PARTS = (2, 1, 1, 2)
 SCORE_BANKS = ((0, 1), (2,), (3,), (4, 5))
 TURN_BANKS = (6, 7, 0, 1)
 ACC_BANK = 2
+ORDER = (0, 2, 3, 1)
 SLOT = 4 * PAGE
 
 
@@ -42,42 +41,35 @@ def tile_attend_pkv4_rel2_cap_kernel(tc, qT, k_words, k_scales, v_words, v_scale
         lists = ctx.enter_context(tc.tile_pool(name="lists", bufs=1))
         keep = ctx.enter_context(tc.tile_pool(name="keep", bufs=1))
         ks_bytes = ctx.enter_context(tc.tile_pool(name="ks_bytes", bufs=1))
-        vsc_bytes = ctx.enter_context(tc.tile_pool(name="vsc_bytes", bufs=1))
+        early = ctx.enter_context(tc.tile_pool(name="early", bufs=1))
+        last = ctx.enter_context(tc.tile_pool(name="last", bufs=1))
         late = ctx.enter_context(tc.tile_pool(name="late", bufs=1))
         psum = ctx.enter_context(tc.psum_pool(name="psum", bufs=1))
 
         slots = lists.tile([P, N // 16], U16, name="slots")
         vcols = lists.tile([P, PAGES * DV // 16], U16, name="vcols")
         ks_pool = ks_bytes.tile([P, T], U8, name="ks_pool", align_bytes=64, offset=0)
-        vsc_pool = vsc_bytes.tile([P, POOL_PAGES * DV], U8, name="vsc_pool", align_bytes=64, offset=0)
         vs_pool = keep.tile([P, T], F32, name="vs_pool", align_bytes=64)
         kw_pool = keep.tile([P, T], I32, name="kw_pool", align_bytes=64)
         q_first = keep.tile([P, PACK * NQ], F32, name="q_first", align_bytes=64)
-        late_area = late.tile([P, 6 * PAGE], F32, name="late_area", align_bytes=64, offset=0)
+        late_area = late.tile([P, 5 * PAGE], F32, name="late_area", align_bytes=64, offset=0)
         q_raw = [area[:, 0 : PACK * NQ].rearrange("p (j w) -> p j w", j=PACK) for area in (q_first, late_area)]
         q_rows = qT[0].rearrange("(g p j) w -> g p j w", g=PASSES, j=PACK)
 
         nc.sync.dma_start(ks_pool[KS_ROW0:P, :].bitcast(I32), k_scales.rearrange("g f t -> f g t").bitcast(I32))
         nc.sync.dma_start(slots[:], offs)
-        nc.sync.dma_start(vcols[:], voffs)
+        nc.scalar.dma_start(vs_pool[P - 1 : P, :], vs[0:1, :])
         nc.sync.dma_start(q_raw[0], q_rows[0])
         nc.sync.dma_start(kw_pool[:], k_words[0].rearrange("p t b -> p (t b)").bitcast(I32))
         nc.sync.dma_start(q_raw[1], q_rows[1])
+        nc.sync.dma_start(vcols[:], voffs)
 
-        nc.vector.memset(vsc_pool[:].bitcast(I32), 0)
-        nc.scalar.dma_start(
-            vsc_pool[VSC_ROW0 : VSC_ROW0 + SCALE_ROWS, :].bitcast(I32).rearrange("f (u e) -> f u e", u=POOL_PAGES),
-            v_scales.rearrange("u f e -> f u e").bitcast(I32),
-        )
         sums = keep.tile([P, 2 + PAGES], F32, name="sums")
         nc.vector.memset(sums[:, 0:1], 1.0 / (CAP * CAP))
         warm = keep.tile([P, 1], F32, name="warm")
         nc.scalar.activation(warm[:], sums[:, 0:1], ACT.Tanh)
-        for h in range(2):
-            cols = slice(h * T // 2, (h + 1) * T // 2)
-            nc.vector.memset(vs_pool[:, cols], 0.0)
-            nc.scalar.dma_start(vs_pool[VS_ROW : VS_ROW + 1, cols], vs[0:1, cols])
         nc.vector.memset(ks_pool[0:KS_ROW0, :].bitcast(I32), 0)
+        nc.vector.memset(vs_pool[0 : P - 1, :], 0.0)
         identity = keep.tile([P, P], F32, name="identity")
         make_identity(nc, identity[:])
 
@@ -93,26 +85,13 @@ def tile_attend_pkv4_rel2_cap_kernel(tc, qT, k_words, k_scales, v_words, v_scale
                 out=q_codes[g][:].bitcast(FP8X4), scales=q_scales[g][:], in_=q_bf[g][:].rearrange("p w j -> p (w j)")
             )
 
-        vs_listed = {}
-
-        def gather_vs(first, count):
-            listed = keep.tile([P, count, PAGE], F32, name="vs_listed%d" % first, align_bytes=64)
-            looked_up = vs_pool[:].indirect(slots[:, first * PAGE // 16 : (first + count) * PAGE // 16])
-            if first == 0:
-                nc.vector.tensor_copy(listed[:].rearrange("p e n -> p (e n)"), looked_up)
-            else:
-                nc.scalar.activation(listed[:].rearrange("p e n -> p (e n)"), looked_up, ACT.Copy)
-            for e in range(first, first + count):
-                vs_listed[e] = listed[VS_ROW : VS_ROW + 1, e - first, :]
-
         ks_listed = keep.tile([P, N], U8, name="ks_listed", align_bytes=64)
         nc.vector.tensor_copy(ks_listed[:], ks_pool[:].indirect(slots[:]))
         cast_queries(0)
         quantise_queries(0)
-        vsc_listed = keep.tile([P, PAGES * DV], U8, name="vsc_listed", align_bytes=64)
-        nc.vector.tensor_copy(vsc_listed[:], vsc_pool[:].indirect(vcols[:]))
-        gather_vs(0, VS_ON_VECTOR)
-        gather_vs(VS_ON_VECTOR, PAGES - VS_ON_VECTOR)
+        vs_listed = keep.tile([P, N], F32, name="vs_listed", align_bytes=64)
+        nc.vector.tensor_copy(vs_listed[:, 0:VS_ON_VECTOR], vs_pool[:].indirect(slots[:, 0 : VS_ON_VECTOR // 16]))
+        nc.scalar.activation(vs_listed[:, VS_ON_VECTOR:N], vs_pool[:].indirect(slots[:, VS_ON_VECTOR // 16 : N // 16]), ACT.Copy)
 
         ks_planes = ks_bytes.tile([P, PASSES, N], U8, name="ks_planes", align_bytes=64, offset=0)
         for quadrant in (0, 2, 1, 3):
@@ -124,27 +103,16 @@ def tile_attend_pkv4_rel2_cap_kernel(tc, qT, k_words, k_scales, v_words, v_scale
         vs_turned = []
         for e in range(PAGES):
             vs_turned.append(keep.tile([P, PACK], F32, name="vs_turned%d" % e))
-            nc.sync.dma_start(vs_turned[e][:], vs_listed[e].rearrange("o (s t) -> o s t", t=PACK))
-        vsc_plane = vsc_bytes.tile([P, PAGES * DV], U8, name="vsc_plane", align_bytes=64, offset=0)
-        for quadrant in (0, 2, 1, 3):
-            nc.sync.dma_start(
-                vsc_plane[32 * quadrant : 32 * quadrant + 4, :].bitcast(I32),
-                vsc_listed[VSC_ROW0 + 4 * quadrant : VSC_ROW0 + 4 * quadrant + 4, :].bitcast(I32),
-            )
+            nc.sync.dma_start(vs_turned[e][:], vs_listed[P - 1 : P, e * PAGE : (e + 1) * PAGE].rearrange("o (s t) -> o s t", t=PACK))
 
         cast_queries(1)
-        vw_pool = late.tile([P, POOL_PAGES * DV], I32, name="vw_pool", align_bytes=64, offset=4 * SLOT)
-        nc.scalar.dma_start(
-            vw_pool[:].rearrange("p (u e) -> p u e", u=POOL_PAGES),
-            v_words.rearrange("u p e r -> p u (e r)").bitcast(I32),
-        )
 
         pairs = {}
         keys = {}
 
         def gather_keys(e):
             if e < 2:
-                pairs[e] = keep.tile([P, PAGE], U32, name="pairs%d" % e, align_bytes=64)
+                pairs[e] = early.tile([P, PAGE], U32, name="pairs%d" % e, align_bytes=64, offset=e * SLOT)
             else:
                 pairs[e] = late.tile([P, PAGE], U32, name="pairs%d" % e, align_bytes=64, offset=e * SLOT)
             nc.vector.tensor_copy(
@@ -167,15 +135,27 @@ def tile_attend_pkv4_rel2_cap_kernel(tc, qT, k_words, k_scales, v_words, v_scale
         gather_keys(1)
         part_keys(0, 0)
         quantise_queries(1)
+        vsc_pool = late.tile([P, POOL_PAGES * DV], U8, name="vsc_pool", align_bytes=64, offset=4 * SLOT)
+        nc.vector.memset(vsc_pool[:].bitcast(I32), 0)
+        vsc_rows = v_scales.rearrange("u (q r) e -> r q u e", r=4)
+        for r in range(4):
+            nc.scalar.dma_start(
+                vsc_pool[r:P:32, :].bitcast(I32).rearrange("q (u e) -> q u e", u=POOL_PAGES), vsc_rows[r].bitcast(I32)
+            )
         part_keys(0, 1)
         part_keys(1, 0)
+        vw_pool = early.tile([P, POOL_PAGES * DV], I32, name="vw_pool", align_bytes=64, offset=0)
+        nc.scalar.dma_start(
+            vw_pool[:].rearrange("p (u e) -> p u e", u=POOL_PAGES),
+            v_words.rearrange("u p e r -> p u (e r)").bitcast(I32),
+        )
         gather_keys(2)
         gather_keys(3)
         part_keys(2, 0)
         part_keys(3, 0)
         part_keys(3, 1)
-        vw = keep.tile([P, PAGES * DV], U32, name="vw", align_bytes=64)
-        nc.vector.tensor_copy(vw[:], vw_pool[:].bitcast(U32).indirect(vcols[:]))
+        vsc_plane = keep.tile([P, PAGES * DV], U8, name="vsc_plane", align_bytes=64)
+        nc.vector.tensor_copy(vsc_plane[:], vsc_pool[:].indirect(vcols[:]))
 
         scores = {}
         for e in range(PAGES):
@@ -202,7 +182,10 @@ def tile_attend_pkv4_rel2_cap_kernel(tc, qT, k_words, k_scales, v_words, v_scale
         w_bf = [keep.tile([P, NQ, PACK], BF16, name="w_bf%d" % e, align_bytes=64) for e in range(PAGES)]
 
         def cap(e, h):
-            capped[e, h] = keep.tile(list(scores[e, h].shape), F32, name="capped%d_%d" % (e, h))
+            if (e, h) == (PAGES - 1, 0):
+                capped[e, h] = last.tile(list(scores[e, h].shape), F32, name="capped%d_%d" % (e, h), align_bytes=64, offset=0)
+            else:
+                capped[e, h] = keep.tile(list(scores[e, h].shape), F32, name="capped%d_%d" % (e, h))
             nc.scalar.activation(capped[e, h][:], scores[e, h], ACT.Tanh, scale=1.0 / CAP)
 
         def rectify_first(h):
@@ -244,8 +227,8 @@ def tile_attend_pkv4_rel2_cap_kernel(tc, qT, k_words, k_scales, v_words, v_scale
                 lhsT_scale=w_scales[:],
                 rhs=vw[:, e * DV : (e + 1) * DV].bitcast(FP8X4),
                 rhs_scale=vsc_plane[:, e * DV : (e + 1) * DV],
-                start=(e == 0),
-                stop=(e == PAGES - 1),
+                start=(e == ORDER[0]),
+                stop=(e == ORDER[-1]),
             )
 
         cap(0, 0)
@@ -266,22 +249,26 @@ def tile_attend_pkv4_rel2_cap_kernel(tc, qT, k_words, k_scales, v_words, v_scale
         square_on_vector(3, 1)
         turn(3)
 
-        by_place = keep.tile([P, PACK, NQ], BF16, name="by_place", align_bytes=64)
-        for t in range(PACK):
-            nc.scalar.activation(by_place[:, t, :], turned[0][:, t, :], ACT.Copy, scale=vs_turned[0][:, t : t + 1])
-        nc.scalar.copy(w_bf[0][:], by_place[:].rearrange("s t q -> s q t"))
+        vw = last.tile([P, PAGES * DV], U32, name="vw", align_bytes=64, offset=0)
+        nc.vector.tensor_copy(vw[:], vw_pool[:].bitcast(U32).indirect(vcols[:]))
+
+        by_place = []
+        for e in range(2):
+            by_place.append(keep.tile([P, PACK, NQ], BF16, name="by_place%d" % e, align_bytes=64))
+            for t in range(PACK):
+                nc.scalar.activation(by_place[e][:, t, :], turned[e][:, t, :], ACT.Copy, scale=vs_turned[e][:, t : t + 1])
+        for e in range(2):
+            nc.scalar.copy(w_bf[e][:], by_place[e][:].rearrange("s t q -> s q t"))
         denom = keep.tile([P, 1], F32, name="denom")
         sums_copy = keep.tile(list(sums.shape), F32, name="sums_copy")
         nc.scalar.activation(sums_copy[:], sums[:], ACT.Copy, accum_out=denom[:])
 
-        scale_on_vector(1)
         scale_on_vector(2)
-        multiply(0)
         scale_on_vector(3)
+        for e in ORDER:
+            multiply(e)
         inverse = keep.tile([P, 1], F32, name="inverse")
         nc.vector.reciprocal(inverse[:], denom[:])
-        for e in range(1, PAGES):
-            multiply(e)
 
         result = keep.tile([P, DV], F32, name="result")
         nc.scalar.activation(result[:], acc[:], ACT.Copy, scale=inverse[:])

@@ -26,7 +26,7 @@ POOL_PAGES = T // PAGE
 PASSES = D // (P * PACK)
 SCALE_ROWS = 16
 KS_ROW0 = P - PASSES * SCALE_ROWS
-VS_ON_VECTOR = 640
+VS_ON_VECTOR = 768
 PARTS = (2, 1, 1, 2)
 SCORE_BANKS = ((0, 1), (2,), (3,), (4, 5))
 TURN_BANKS = (6, 7, 0, 1)
@@ -43,6 +43,7 @@ def tile_attend_pkv4_rel2_cap_kernel(tc, qT, k_words, k_scales, v_words, v_scale
         ks_bytes = ctx.enter_context(tc.tile_pool(name="ks_bytes", bufs=1))
         early = ctx.enter_context(tc.tile_pool(name="early", bufs=1))
         last = ctx.enter_context(tc.tile_pool(name="last", bufs=1))
+        middle = ctx.enter_context(tc.tile_pool(name="middle", bufs=1))
         late = ctx.enter_context(tc.tile_pool(name="late", bufs=1))
         psum = ctx.enter_context(tc.psum_pool(name="psum", bufs=1))
 
@@ -51,7 +52,7 @@ def tile_attend_pkv4_rel2_cap_kernel(tc, qT, k_words, k_scales, v_words, v_scale
         ks_pool = ks_bytes.tile([P, T], U8, name="ks_pool", align_bytes=64, offset=0)
         vs_pool = keep.tile([P, T], F32, name="vs_pool", align_bytes=64)
         kw_pool = keep.tile([P, T], I32, name="kw_pool", align_bytes=64)
-        q_first = keep.tile([P, PACK * NQ], F32, name="q_first", align_bytes=64)
+        q_first = middle.tile([P, PACK * NQ], F32, name="q_first", align_bytes=64, offset=0)
         late_area = late.tile([P, 5 * PAGE], F32, name="late_area", align_bytes=64, offset=0)
         q_raw = [area[:, 0 : PACK * NQ].rearrange("p (j w) -> p j w", j=PACK) for area in (q_first, late_area)]
         q_rows = qT[0].rearrange("(g p j) w -> g p j w", g=PASSES, j=PACK)
@@ -59,8 +60,8 @@ def tile_attend_pkv4_rel2_cap_kernel(tc, qT, k_words, k_scales, v_words, v_scale
         nc.sync.dma_start(ks_pool[KS_ROW0:P, :].bitcast(I32), k_scales.rearrange("g f t -> f g t").bitcast(I32))
         nc.sync.dma_start(slots[:], offs)
         nc.scalar.dma_start(vs_pool[P - 1 : P, :], vs[0:1, :])
-        nc.sync.dma_start(q_raw[0], q_rows[0])
         nc.sync.dma_start(kw_pool[:], k_words[0].rearrange("p t b -> p (t b)").bitcast(I32))
+        nc.sync.dma_start(q_raw[0], q_rows[0])
         nc.sync.dma_start(q_raw[1], q_rows[1])
         nc.sync.dma_start(vcols[:], voffs)
 
@@ -68,8 +69,8 @@ def tile_attend_pkv4_rel2_cap_kernel(tc, qT, k_words, k_scales, v_words, v_scale
         nc.vector.memset(sums[:, 0:1], 1.0 / (CAP * CAP))
         warm = keep.tile([P, 1], F32, name="warm")
         nc.scalar.activation(warm[:], sums[:, 0:1], ACT.Tanh)
-        nc.vector.memset(ks_pool[0:KS_ROW0, :].bitcast(I32), 0)
         nc.vector.memset(vs_pool[0 : P - 1, :], 0.0)
+        nc.vector.memset(ks_pool[0:KS_ROW0, :].bitcast(I32), 0)
         identity = keep.tile([P, P], F32, name="identity")
         make_identity(nc, identity[:])
 
@@ -87,8 +88,6 @@ def tile_attend_pkv4_rel2_cap_kernel(tc, qT, k_words, k_scales, v_words, v_scale
 
         ks_listed = keep.tile([P, N], U8, name="ks_listed", align_bytes=64)
         nc.vector.tensor_copy(ks_listed[:], ks_pool[:].indirect(slots[:]))
-        cast_queries(0)
-        quantise_queries(0)
         vs_listed = keep.tile([P, N], F32, name="vs_listed", align_bytes=64)
         nc.vector.tensor_copy(vs_listed[:, 0:VS_ON_VECTOR], vs_pool[:].indirect(slots[:, 0 : VS_ON_VECTOR // 16]))
         nc.scalar.activation(vs_listed[:, VS_ON_VECTOR:N], vs_pool[:].indirect(slots[:, VS_ON_VECTOR // 16 : N // 16]), ACT.Copy)
@@ -105,6 +104,7 @@ def tile_attend_pkv4_rel2_cap_kernel(tc, qT, k_words, k_scales, v_words, v_scale
             vs_turned.append(keep.tile([P, PACK], F32, name="vs_turned%d" % e))
             nc.sync.dma_start(vs_turned[e][:], vs_listed[P - 1 : P, e * PAGE : (e + 1) * PAGE].rearrange("o (s t) -> o s t", t=PACK))
 
+        cast_queries(0)
         cast_queries(1)
 
         pairs = {}
@@ -122,7 +122,7 @@ def tile_attend_pkv4_rel2_cap_kernel(tc, qT, k_words, k_scales, v_words, v_scale
         def part_keys(e, h):
             width = PAGE // PARTS[e]
             if e + h == 1:
-                part = late.tile([P, PASSES, 2 * width], U8, name="keys%d_%d" % (e, h), align_bytes=64, offset=e * SLOT)
+                part = (middle, late)[e].tile([P, PASSES, 2 * width], U8, name="keys%d_%d" % (e, h), align_bytes=64, offset=0)
             else:
                 part = keep.tile([P, PASSES, 2 * width], U8, name="keys%d_%d" % (e, h), align_bytes=64)
             nc.vector.tensor_copy(
@@ -134,6 +134,8 @@ def tile_attend_pkv4_rel2_cap_kernel(tc, qT, k_words, k_scales, v_words, v_scale
         gather_keys(0)
         gather_keys(1)
         part_keys(0, 0)
+        quantise_queries(0)
+        part_keys(0, 1)
         quantise_queries(1)
         vsc_pool = late.tile([P, POOL_PAGES * DV], U8, name="vsc_pool", align_bytes=64, offset=4 * SLOT)
         nc.vector.memset(vsc_pool[:].bitcast(I32), 0)
@@ -142,7 +144,6 @@ def tile_attend_pkv4_rel2_cap_kernel(tc, qT, k_words, k_scales, v_words, v_scale
             nc.scalar.dma_start(
                 vsc_pool[r:P:32, :].bitcast(I32).rearrange("q (u e) -> q u e", u=POOL_PAGES), vsc_rows[r].bitcast(I32)
             )
-        part_keys(0, 1)
         part_keys(1, 0)
         vw_pool = early.tile([P, POOL_PAGES * DV], I32, name="vw_pool", align_bytes=64, offset=0)
         nc.scalar.dma_start(

@@ -26,13 +26,13 @@ POOL_PAGES = T // PAGE
 PASSES = D // (P * PACK)
 SCALE_ROWS = 16
 KS_ROW0 = P - PASSES * SCALE_ROWS
-VS_ON_VECTOR = 768
+VS_ZEROED_BY_VECTOR = 1152
+VS_ON_VECTOR = 256
 PARTS = (2, 1, 1, 2)
 SCORE_BANKS = ((0, 1), (2,), (3,), (4, 5))
 TURN_BANKS = (6, 7, 0, 1)
 ACC_BANK = 2
-ORDER = (0, 2, 3, 1)
-SLOT = 4 * PAGE
+PRODUCT_ORDER = (0, 2, 3, 1)
 
 
 def tile_attend_pkv4_rel2_cap_kernel(tc, qT, k_words, k_scales, v_words, v_scales, vs, offs, voffs, out):
@@ -40,46 +40,42 @@ def tile_attend_pkv4_rel2_cap_kernel(tc, qT, k_words, k_scales, v_words, v_scale
     with ExitStack() as ctx:
         lists = ctx.enter_context(tc.tile_pool(name="lists", bufs=1))
         keep = ctx.enter_context(tc.tile_pool(name="keep", bufs=1))
-        ks_bytes = ctx.enter_context(tc.tile_pool(name="ks_bytes", bufs=1))
-        early = ctx.enter_context(tc.tile_pool(name="early", bufs=1))
         last = ctx.enter_context(tc.tile_pool(name="last", bufs=1))
-        middle = ctx.enter_context(tc.tile_pool(name="middle", bufs=1))
-        late = ctx.enter_context(tc.tile_pool(name="late", bufs=1))
         psum = ctx.enter_context(tc.psum_pool(name="psum", bufs=1))
 
         slots = lists.tile([P, N // 16], U16, name="slots")
         vcols = lists.tile([P, PAGES * DV // 16], U16, name="vcols")
-        ks_pool = ks_bytes.tile([P, T], U8, name="ks_pool", align_bytes=64, offset=0)
+        ks_pool = keep.tile([P, T + 4], U8, name="ks_pool", align_bytes=64)
         vs_pool = keep.tile([P, T], F32, name="vs_pool", align_bytes=64)
         kw_pool = keep.tile([P, T], I32, name="kw_pool", align_bytes=64)
-        q_first = middle.tile([P, PACK * NQ], F32, name="q_first", align_bytes=64, offset=0)
-        late_area = late.tile([P, 5 * PAGE], F32, name="late_area", align_bytes=64, offset=0)
-        q_raw = [area[:, 0 : PACK * NQ].rearrange("p (j w) -> p j w", j=PACK) for area in (q_first, late_area)]
+        vsc_pool = keep.tile([P, POOL_PAGES * DV], U8, name="vsc_pool", align_bytes=64)
+        vw_pool = keep.tile([P, POOL_PAGES * DV], I32, name="vw_pool", align_bytes=64)
+        q_raw = [keep.tile([P, PACK, NQ], F32, name="q_raw%d" % g, align_bytes=64) for g in range(PASSES)]
         q_rows = qT[0].rearrange("(g p j) w -> g p j w", g=PASSES, j=PACK)
 
-        nc.sync.dma_start(ks_pool[KS_ROW0:P, :].bitcast(I32), k_scales.rearrange("g f t -> f g t").bitcast(I32))
+        nc.sync.dma_start(ks_pool[KS_ROW0:P, 0:T].bitcast(I32), k_scales.rearrange("g f t -> f g t").bitcast(I32))
         nc.sync.dma_start(slots[:], offs)
-        nc.scalar.dma_start(vs_pool[P - 1 : P, :], vs[0:1, :])
-        nc.sync.dma_start(kw_pool[:], k_words[0].rearrange("p t b -> p (t b)").bitcast(I32))
-        nc.sync.dma_start(q_raw[0], q_rows[0])
-        nc.sync.dma_start(q_raw[1], q_rows[1])
+        nc.sync.dma_start(vs_pool[P - 1 : P, :], vs[0:1, :])
+        nc.sync.dma_start(q_raw[0][:], q_rows[0])
         nc.sync.dma_start(vcols[:], voffs)
+        nc.sync.dma_start(kw_pool[:], k_words[0].rearrange("p t b -> p (t b)").bitcast(I32))
+        nc.sync.dma_start(q_raw[1][:], q_rows[1])
 
-        sums = keep.tile([P, 2 + PAGES], F32, name="sums")
-        nc.vector.memset(sums[:, 0:1], 1.0 / (CAP * CAP))
-        warm = keep.tile([P, 1], F32, name="warm")
-        nc.scalar.activation(warm[:], sums[:, 0:1], ACT.Tanh)
-        nc.vector.memset(vs_pool[0 : P - 1, :], 0.0)
         nc.vector.memset(ks_pool[0:KS_ROW0, :].bitcast(I32), 0)
+        nc.vector.memset(vs_pool[0 : P - 1, 0 : VS_ZEROED_BY_VECTOR - 1], 0.0)
+        nc.vector.memset(vs_pool[0 : P - 1, VS_ZEROED_BY_VECTOR - 1 : VS_ZEROED_BY_VECTOR], 0.0)
+        nc.gpsimd.memset(vs_pool[0 : P - 1, VS_ZEROED_BY_VECTOR:T], 0.0)
+        nc.gpsimd.memset(vsc_pool[:].bitcast(I32), 0)
+        sums = keep.tile([P, 2 + PAGES], F32, name="sums")
+        nc.gpsimd.memset(sums[:, 0:1], 1.0 / (CAP * CAP))
         identity = keep.tile([P, P], F32, name="identity")
         make_identity(nc, identity[:])
 
         q_bf = [keep.tile([P, NQ, PACK], BF16, name="q_bf%d" % g, align_bytes=64) for g in range(PASSES)]
         q_codes = [keep.tile([P, NQ], U32, name="q_codes%d" % g, align_bytes=64) for g in range(PASSES)]
         q_scales = [keep.tile([P, NQ], U8, name="q_scales%d" % g, align_bytes=64) for g in range(PASSES)]
-
-        def cast_queries(g):
-            nc.scalar.copy(q_bf[g][:], q_raw[g].rearrange("p j w -> p w j"))
+        for g in range(PASSES):
+            nc.gpsimd.tensor_scalar(q_bf[g][:], q_raw[g][:].rearrange("p j w -> p w j"), 1.0, 0.0, ALU.mult, ALU.add)
 
         def quantise_queries(g):
             nc.vector.quantize_mx(
@@ -87,69 +83,56 @@ def tile_attend_pkv4_rel2_cap_kernel(tc, qT, k_words, k_scales, v_words, v_scale
             )
 
         ks_listed = keep.tile([P, N], U8, name="ks_listed", align_bytes=64)
-        nc.vector.tensor_copy(ks_listed[:], ks_pool[:].indirect(slots[:]))
+        nc.vector.tensor_copy(ks_listed[:], ks_pool[:, 0:T].indirect(slots[:]))
         vs_listed = keep.tile([P, N], F32, name="vs_listed", align_bytes=64)
         nc.vector.tensor_copy(vs_listed[:, 0:VS_ON_VECTOR], vs_pool[:].indirect(slots[:, 0 : VS_ON_VECTOR // 16]))
         nc.scalar.activation(vs_listed[:, VS_ON_VECTOR:N], vs_pool[:].indirect(slots[:, VS_ON_VECTOR // 16 : N // 16]), ACT.Copy)
+        quantise_queries(0)
 
-        ks_planes = ks_bytes.tile([P, PASSES, N], U8, name="ks_planes", align_bytes=64, offset=0)
+        ks_planes = keep.tile([P, PASSES, N], U8, name="ks_planes", align_bytes=64)
         for quadrant in (0, 2, 1, 3):
             row0 = KS_ROW0 + 4 * PASSES * quadrant
             nc.sync.dma_start(
                 ks_planes[32 * quadrant : 32 * quadrant + 4, :, :].bitcast(I32),
                 ks_listed[row0 : row0 + 4 * PASSES, :].bitcast(I32),
             )
+        vsc_rows = v_scales.rearrange("u (q r) e -> r q u e", r=4)
+        for r in range(4):
+            nc.sync.dma_start(
+                vsc_pool[r:P:32, :].bitcast(I32).rearrange("q (u e) -> q u e", u=POOL_PAGES), vsc_rows[r].bitcast(I32)
+            )
+        nc.sync.dma_start(
+            vw_pool[:].rearrange("p (u e) -> p u e", u=POOL_PAGES),
+            v_words.rearrange("u p e r -> p u (e r)").bitcast(I32),
+        )
         vs_turned = []
         for e in range(PAGES):
             vs_turned.append(keep.tile([P, PACK], F32, name="vs_turned%d" % e))
             nc.sync.dma_start(vs_turned[e][:], vs_listed[P - 1 : P, e * PAGE : (e + 1) * PAGE].rearrange("o (s t) -> o s t", t=PACK))
 
-        cast_queries(0)
-        cast_queries(1)
-
         pairs = {}
         keys = {}
 
         def gather_keys(e):
-            if e < 2:
-                pairs[e] = early.tile([P, PAGE], U32, name="pairs%d" % e, align_bytes=64, offset=e * SLOT)
-            else:
-                pairs[e] = late.tile([P, PAGE], U32, name="pairs%d" % e, align_bytes=64, offset=e * SLOT)
+            pairs[e] = keep.tile([P, PAGE], U32, name="pairs%d" % e, align_bytes=64)
             nc.vector.tensor_copy(
                 pairs[e][:], kw_pool[:].bitcast(U32).indirect(slots[:, e * PAGE // 16 : (e + 1) * PAGE // 16])
             )
 
         def part_keys(e, h):
             width = PAGE // PARTS[e]
-            if e + h == 1:
-                part = (middle, late)[e].tile([P, PASSES, 2 * width], U8, name="keys%d_%d" % (e, h), align_bytes=64, offset=0)
-            else:
-                part = keep.tile([P, PASSES, 2 * width], U8, name="keys%d_%d" % (e, h), align_bytes=64)
+            keys[e, h] = keep.tile([P, PASSES, 2 * width], U8, name="keys%d_%d" % (e, h), align_bytes=64)
             nc.vector.tensor_copy(
-                part[:].bitcast(U16),
+                keys[e, h][:].bitcast(U16),
                 pairs[e][:, h * width : (h + 1) * width].bitcast(U16).rearrange("p (n g) -> p g n", g=PASSES),
             )
-            keys[e, h] = part
 
         gather_keys(0)
         gather_keys(1)
         part_keys(0, 0)
-        quantise_queries(0)
         part_keys(0, 1)
         quantise_queries(1)
-        vsc_pool = late.tile([P, POOL_PAGES * DV], U8, name="vsc_pool", align_bytes=64, offset=4 * SLOT)
-        nc.vector.memset(vsc_pool[:].bitcast(I32), 0)
-        vsc_rows = v_scales.rearrange("u (q r) e -> r q u e", r=4)
-        for r in range(4):
-            nc.scalar.dma_start(
-                vsc_pool[r:P:32, :].bitcast(I32).rearrange("q (u e) -> q u e", u=POOL_PAGES), vsc_rows[r].bitcast(I32)
-            )
         part_keys(1, 0)
-        vw_pool = early.tile([P, POOL_PAGES * DV], I32, name="vw_pool", align_bytes=64, offset=0)
-        nc.scalar.dma_start(
-            vw_pool[:].rearrange("p (u e) -> p u e", u=POOL_PAGES),
-            v_words.rearrange("u p e r -> p u (e r)").bitcast(I32),
-        )
         gather_keys(2)
         gather_keys(3)
         part_keys(2, 0)
@@ -228,8 +211,8 @@ def tile_attend_pkv4_rel2_cap_kernel(tc, qT, k_words, k_scales, v_words, v_scale
                 lhsT_scale=w_scales[:],
                 rhs=vw[:, e * DV : (e + 1) * DV].bitcast(FP8X4),
                 rhs_scale=vsc_plane[:, e * DV : (e + 1) * DV],
-                start=(e == ORDER[0]),
-                stop=(e == ORDER[-1]),
+                start=(e == PRODUCT_ORDER[0]),
+                stop=(e == PRODUCT_ORDER[-1]),
             )
 
         cap(0, 0)
@@ -266,7 +249,7 @@ def tile_attend_pkv4_rel2_cap_kernel(tc, qT, k_words, k_scales, v_words, v_scale
 
         scale_on_vector(2)
         scale_on_vector(3)
-        for e in ORDER:
+        for e in PRODUCT_ORDER:
             multiply(e)
         inverse = keep.tile([P, 1], F32, name="inverse")
         nc.vector.reciprocal(inverse[:], denom[:])

@@ -61,6 +61,9 @@ def tile_attend_pkv4_rel2_cap_kernel(tc, qT, k_words, k_scales, v_words, v_scale
         nc.sync.dma_start(kw_pool[:], k_words[0].rearrange("p t b -> p (t b)").bitcast(I32))
         nc.sync.dma_start(q_raw[1][:], q_rows[1])
 
+        warm = keep.tile([P, 2], F32, name="warm")
+        nc.vector.memset(warm[:, 0:1], 0.0)
+        nc.scalar.activation(warm[:, 1:2], warm[:, 0:1], ACT.Tanh)
         nc.vector.memset(ks_pool[0:KS_ROW0, :].bitcast(I32), 0)
         nc.vector.memset(vs_pool[0 : P - 1, 0 : VS_ZEROED_BY_VECTOR - 1], 0.0)
         nc.vector.memset(vs_pool[0 : P - 1, VS_ZEROED_BY_VECTOR - 1 : VS_ZEROED_BY_VECTOR], 0.0)

@@ -26,13 +26,14 @@ POOL_PAGES = T // PAGE
 PASSES = D // (P * PACK)
 SCALE_ROWS = 16
 KS_ROW0 = P - PASSES * SCALE_ROWS
-VS_ZEROED_BY_VECTOR = 1152
-VS_ON_VECTOR = 256
+VS_ZEROED_BY_VECTOR = 1200
+VS_ON_VECTOR = 896
 PARTS = (2, 1, 1, 2)
 SCORE_BANKS = ((0, 1), (2,), (3,), (4, 5))
 TURN_BANKS = (6, 7, 0, 1)
 ACC_BANK = 2
 PRODUCT_ORDER = (0, 2, 3, 1)
+SLOT = 4 * PAGE
 
 
 def tile_attend_pkv4_rel2_cap_kernel(tc, qT, k_words, k_scales, v_words, v_scales, vs, offs, voffs, out):
@@ -40,6 +41,7 @@ def tile_attend_pkv4_rel2_cap_kernel(tc, qT, k_words, k_scales, v_words, v_scale
     with ExitStack() as ctx:
         lists = ctx.enter_context(tc.tile_pool(name="lists", bufs=1))
         keep = ctx.enter_context(tc.tile_pool(name="keep", bufs=1))
+        late = ctx.enter_context(tc.tile_pool(name="late", bufs=1))
         last = ctx.enter_context(tc.tile_pool(name="last", bufs=1))
         psum = ctx.enter_context(tc.psum_pool(name="psum", bufs=1))
 
@@ -50,35 +52,34 @@ def tile_attend_pkv4_rel2_cap_kernel(tc, qT, k_words, k_scales, v_words, v_scale
         kw_pool = keep.tile([P, T], I32, name="kw_pool", align_bytes=64)
         vsc_pool = keep.tile([P, POOL_PAGES * DV], U8, name="vsc_pool", align_bytes=64)
         vw_pool = keep.tile([P, POOL_PAGES * DV], I32, name="vw_pool", align_bytes=64)
-        q_raw = [keep.tile([P, PACK, NQ], F32, name="q_raw%d" % g, align_bytes=64) for g in range(PASSES)]
+        q_first = keep.tile([P, PACK * NQ], F32, name="q_first", align_bytes=64)
+        late_area = late.tile([P, 3 * PAGE], F32, name="late_area", align_bytes=64, offset=0)
+        q_raw = [area[:, 0 : PACK * NQ].rearrange("p (j w) -> p j w", j=PACK) for area in (q_first, late_area)]
         q_rows = qT[0].rearrange("(g p j) w -> g p j w", g=PASSES, j=PACK)
 
         nc.sync.dma_start(ks_pool[KS_ROW0:P, 0:T].bitcast(I32), k_scales.rearrange("g f t -> f g t").bitcast(I32))
         nc.sync.dma_start(slots[:], offs)
         nc.sync.dma_start(vs_pool[P - 1 : P, :], vs[0:1, :])
-        nc.sync.dma_start(q_raw[0][:], q_rows[0])
-        nc.sync.dma_start(vcols[:], voffs)
         nc.sync.dma_start(kw_pool[:], k_words[0].rearrange("p t b -> p (t b)").bitcast(I32))
-        nc.sync.dma_start(q_raw[1][:], q_rows[1])
+        nc.sync.dma_start(q_raw[0], q_rows[0])
+        nc.sync.dma_start(q_raw[1], q_rows[1])
+        nc.sync.dma_start(vcols[:], voffs)
 
-        warm = keep.tile([P, 2], F32, name="warm")
-        nc.vector.memset(warm[:, 0:1], 0.0)
-        nc.scalar.activation(warm[:, 1:2], warm[:, 0:1], ACT.Tanh)
+        sums = keep.tile([P, 2 + PAGES], F32, name="sums")
+        nc.vector.memset(sums[:, 0:1], 1.0 / (CAP * CAP))
+        warm = keep.tile([P, 1], F32, name="warm")
+        nc.scalar.activation(warm[:], sums[:, 0:1], ACT.Tanh)
         nc.vector.memset(ks_pool[0:KS_ROW0, :].bitcast(I32), 0)
         nc.vector.memset(vs_pool[0 : P - 1, 0 : VS_ZEROED_BY_VECTOR - 1], 0.0)
         nc.vector.memset(vs_pool[0 : P - 1, VS_ZEROED_BY_VECTOR - 1 : VS_ZEROED_BY_VECTOR], 0.0)
-        nc.gpsimd.memset(vs_pool[0 : P - 1, VS_ZEROED_BY_VECTOR:T], 0.0)
-        nc.gpsimd.memset(vsc_pool[:].bitcast(I32), 0)
-        sums = keep.tile([P, 2 + PAGES], F32, name="sums")
-        nc.gpsimd.memset(sums[:, 0:1], 1.0 / (CAP * CAP))
         identity = keep.tile([P, P], F32, name="identity")
         make_identity(nc, identity[:])
+        nc.gpsimd.memset(vs_pool[0 : P - 1, VS_ZEROED_BY_VECTOR:T], 0.0)
+        nc.gpsimd.memset(vsc_pool[:].bitcast(I32), 0)
 
         q_bf = [keep.tile([P, NQ, PACK], BF16, name="q_bf%d" % g, align_bytes=64) for g in range(PASSES)]
         q_codes = [keep.tile([P, NQ], U32, name="q_codes%d" % g, align_bytes=64) for g in range(PASSES)]
         q_scales = [keep.tile([P, NQ], U8, name="q_scales%d" % g, align_bytes=64) for g in range(PASSES)]
-        for g in range(PASSES):
-            nc.gpsimd.tensor_scalar(q_bf[g][:], q_raw[g][:].rearrange("p j w -> p w j"), 1.0, 0.0, ALU.mult, ALU.add)
 
         def quantise_queries(g):
             nc.vector.quantize_mx(
@@ -90,7 +91,8 @@ def tile_attend_pkv4_rel2_cap_kernel(tc, qT, k_words, k_scales, v_words, v_scale
         vs_listed = keep.tile([P, N], F32, name="vs_listed", align_bytes=64)
         nc.vector.tensor_copy(vs_listed[:, 0:VS_ON_VECTOR], vs_pool[:].indirect(slots[:, 0 : VS_ON_VECTOR // 16]))
         nc.scalar.activation(vs_listed[:, VS_ON_VECTOR:N], vs_pool[:].indirect(slots[:, VS_ON_VECTOR // 16 : N // 16]), ACT.Copy)
-        quantise_queries(0)
+        for g in range(PASSES):
+            nc.scalar.copy(q_bf[g][:], q_raw[g].rearrange("p j w -> p w j"))
 
         ks_planes = keep.tile([P, PASSES, N], U8, name="ks_planes", align_bytes=64)
         for quadrant in (0, 2, 1, 3):
@@ -117,14 +119,20 @@ def tile_attend_pkv4_rel2_cap_kernel(tc, qT, k_words, k_scales, v_words, v_scale
         keys = {}
 
         def gather_keys(e):
-            pairs[e] = keep.tile([P, PAGE], U32, name="pairs%d" % e, align_bytes=64)
+            if e < 2:
+                pairs[e] = keep.tile([P, PAGE], U32, name="pairs%d" % e, align_bytes=64)
+            else:
+                pairs[e] = late.tile([P, PAGE], U32, name="pairs%d" % e, align_bytes=64, offset=(e - 1) * SLOT)
             nc.vector.tensor_copy(
                 pairs[e][:], kw_pool[:].bitcast(U32).indirect(slots[:, e * PAGE // 16 : (e + 1) * PAGE // 16])
             )
 
         def part_keys(e, h):
             width = PAGE // PARTS[e]
-            keys[e, h] = keep.tile([P, PASSES, 2 * width], U8, name="keys%d_%d" % (e, h), align_bytes=64)
+            if e == 1:
+                keys[e, h] = late.tile([P, PASSES, 2 * width], U8, name="keys%d_%d" % (e, h), align_bytes=64, offset=0)
+            else:
+                keys[e, h] = keep.tile([P, PASSES, 2 * width], U8, name="keys%d_%d" % (e, h), align_bytes=64)
             nc.vector.tensor_copy(
                 keys[e, h][:].bitcast(U16),
                 pairs[e][:, h * width : (h + 1) * width].bitcast(U16).rearrange("p (n g) -> p g n", g=PASSES),
@@ -134,6 +142,7 @@ def tile_attend_pkv4_rel2_cap_kernel(tc, qT, k_words, k_scales, v_words, v_scale
         gather_keys(1)
         part_keys(0, 0)
         part_keys(0, 1)
+        quantise_queries(0)
         quantise_queries(1)
         part_keys(1, 0)
         gather_keys(2)

@@ -26,12 +26,12 @@ POOL_PAGES = T // PAGE
 PASSES = D // (P * PACK)
 SCALE_ROWS = 16
 KS_ROW0 = P - PASSES * SCALE_ROWS
-VS_ZEROED_BY_VECTOR = 1200
 VS_ON_VECTOR = 896
-PARTS = (2, 1, 1, 2)
-SCORE_BANKS = ((0, 1), (2,), (3,), (4, 5))
-TURN_BANKS = (6, 7, 0, 1)
-ACC_BANK = 2
+PARTS = (1, 1, 1, 2)
+SCORE_BANKS = ((0,), (1,), (2,), (3, 4))
+TURN_BANKS = (5, 6, 7, 0)
+ACC_BANK = 1
+SCALED_ON_SCALAR = 2
 PRODUCT_ORDER = (0, 2, 3, 1)
 SLOT = 4 * PAGE
 
@@ -43,86 +43,92 @@ def tile_attend_pkv4_rel2_cap_kernel(tc, qT, k_words, k_scales, v_words, v_scale
         keep = ctx.enter_context(tc.tile_pool(name="keep", bufs=1))
         late = ctx.enter_context(tc.tile_pool(name="late", bufs=1))
         last = ctx.enter_context(tc.tile_pool(name="last", bufs=1))
+        final = ctx.enter_context(tc.tile_pool(name="final", bufs=1))
         psum = ctx.enter_context(tc.psum_pool(name="psum", bufs=1))
 
         slots = lists.tile([P, N // 16], U16, name="slots")
         vcols = lists.tile([P, PAGES * DV // 16], U16, name="vcols")
-        ks_pool = keep.tile([P, T + 4], U8, name="ks_pool", align_bytes=64)
-        vs_pool = keep.tile([P, T], F32, name="vs_pool", align_bytes=64)
-        kw_pool = keep.tile([P, T], I32, name="kw_pool", align_bytes=64)
-        vsc_pool = keep.tile([P, POOL_PAGES * DV], U8, name="vsc_pool", align_bytes=64)
-        vw_pool = keep.tile([P, POOL_PAGES * DV], I32, name="vw_pool", align_bytes=64)
-        q_first = keep.tile([P, PACK * NQ], F32, name="q_first", align_bytes=64)
-        late_area = late.tile([P, 3 * PAGE], F32, name="late_area", align_bytes=64, offset=0)
+        ks_pool = keep.tile([P, T + 4], U8, name="ks_pool", align_bytes=256)
+        vs_pool = keep.tile([P, T], F32, name="vs_pool", align_bytes=256)
+        kw_pool = keep.tile([P, T], I32, name="kw_pool", align_bytes=256)
+        vsc_pool = keep.tile([P, POOL_PAGES * DV], U8, name="vsc_pool", align_bytes=256)
+        vw_pool = keep.tile([P, POOL_PAGES * DV], I32, name="vw_pool", align_bytes=256)
+        q_first = keep.tile([P, PACK * NQ], F32, name="q_first", align_bytes=256)
+        late_area = late.tile([P, 3 * PAGE], F32, name="late_area", align_bytes=256, offset=0)
         q_raw = [area[:, 0 : PACK * NQ].rearrange("p (j w) -> p j w", j=PACK) for area in (q_first, late_area)]
         q_rows = qT[0].rearrange("(g p j) w -> g p j w", g=PASSES, j=PACK)
 
         nc.sync.dma_start(ks_pool[KS_ROW0:P, 0:T].bitcast(I32), k_scales.rearrange("g f t -> f g t").bitcast(I32))
         nc.sync.dma_start(slots[:], offs)
-        nc.sync.dma_start(vs_pool[P - 1 : P, :], vs[0:1, :])
+        nc.scalar.dma_start(vs_pool[P - 1 : P, :], vs[0:1, :])
+        nc.sync.dma_start(vcols[:], voffs)
         nc.sync.dma_start(kw_pool[:], k_words[0].rearrange("p t b -> p (t b)").bitcast(I32))
         nc.sync.dma_start(q_raw[0], q_rows[0])
         nc.sync.dma_start(q_raw[1], q_rows[1])
-        nc.sync.dma_start(vcols[:], voffs)
 
+        nc.gpsimd.memset(vsc_pool[:].bitcast(I32), 0)
         sums = keep.tile([P, 2 + PAGES], F32, name="sums")
-        nc.vector.memset(sums[:, 0:1], 1.0 / (CAP * CAP))
-        warm = keep.tile([P, 1], F32, name="warm")
-        nc.scalar.activation(warm[:], sums[:, 0:1], ACT.Tanh)
-        nc.vector.memset(ks_pool[0:KS_ROW0, :].bitcast(I32), 0)
-        nc.vector.memset(vs_pool[0 : P - 1, 0 : VS_ZEROED_BY_VECTOR - 1], 0.0)
-        nc.vector.memset(vs_pool[0 : P - 1, VS_ZEROED_BY_VECTOR - 1 : VS_ZEROED_BY_VECTOR], 0.0)
+        nc.gpsimd.memset(sums[:, 0:1], 1.0 / (CAP * CAP))
         identity = keep.tile([P, P], F32, name="identity")
         make_identity(nc, identity[:])
-        nc.gpsimd.memset(vs_pool[0 : P - 1, VS_ZEROED_BY_VECTOR:T], 0.0)
-        nc.gpsimd.memset(vsc_pool[:].bitcast(I32), 0)
+        nc.vector.memset(ks_pool[0:KS_ROW0, :].bitcast(I32), 0)
+        nc.vector.memset(vs_pool[0 : P - 1, :], 0.0)
 
-        q_bf = [keep.tile([P, NQ, PACK], BF16, name="q_bf%d" % g, align_bytes=64) for g in range(PASSES)]
-        q_codes = [keep.tile([P, NQ], U32, name="q_codes%d" % g, align_bytes=64) for g in range(PASSES)]
-        q_scales = [keep.tile([P, NQ], U8, name="q_scales%d" % g, align_bytes=64) for g in range(PASSES)]
+        nc.scalar.dma_start(
+            vsc_pool[0 : 4 * SCALE_ROWS : 4, :].bitcast(I32).rearrange("f (u e) -> f u e", u=POOL_PAGES),
+            v_scales.rearrange("u f e -> f u e").bitcast(I32),
+        )
+        warm = keep.tile([P, 1], F32, name="warm")
+        nc.scalar.activation(warm[:], sums[:, 0:1], ACT.Tanh)
 
-        def quantise_queries(g):
-            nc.vector.quantize_mx(
-                out=q_codes[g][:].bitcast(FP8X4), scales=q_scales[g][:], in_=q_bf[g][:].rearrange("p w j -> p (w j)")
-            )
-
-        ks_listed = keep.tile([P, N], U8, name="ks_listed", align_bytes=64)
+        ks_listed = keep.tile([P, N], U8, name="ks_listed", align_bytes=256)
         nc.vector.tensor_copy(ks_listed[:], ks_pool[:, 0:T].indirect(slots[:]))
-        vs_listed = keep.tile([P, N], F32, name="vs_listed", align_bytes=64)
+        vs_listed = keep.tile([P, N], F32, name="vs_listed", align_bytes=256)
         nc.vector.tensor_copy(vs_listed[:, 0:VS_ON_VECTOR], vs_pool[:].indirect(slots[:, 0 : VS_ON_VECTOR // 16]))
         nc.scalar.activation(vs_listed[:, VS_ON_VECTOR:N], vs_pool[:].indirect(slots[:, VS_ON_VECTOR // 16 : N // 16]), ACT.Copy)
-        for g in range(PASSES):
-            nc.scalar.copy(q_bf[g][:], q_raw[g].rearrange("p j w -> p w j"))
+        vsc_listed = keep.tile([P, PAGES * DV], U8, name="vsc_listed", align_bytes=256)
+        nc.vector.tensor_copy(vsc_listed[:], vsc_pool[:].indirect(vcols[:]))
 
-        ks_planes = keep.tile([P, PASSES, N], U8, name="ks_planes", align_bytes=64)
+        q_bf = keep.tile([P, PASSES, NQ, PACK], BF16, name="q_bf", align_bytes=256)
+        for g in range(PASSES):
+            nc.scalar.copy(q_bf[:, g], q_raw[g].rearrange("p j w -> p w j"))
+
+        ks_planes = keep.tile([P, PASSES, N], U8, name="ks_planes", align_bytes=256)
         for quadrant in (0, 2, 1, 3):
             row0 = KS_ROW0 + 4 * PASSES * quadrant
             nc.sync.dma_start(
                 ks_planes[32 * quadrant : 32 * quadrant + 4, :, :].bitcast(I32),
                 ks_listed[row0 : row0 + 4 * PASSES, :].bitcast(I32),
             )
-        vsc_rows = v_scales.rearrange("u (q r) e -> r q u e", r=4)
-        for r in range(4):
-            nc.sync.dma_start(
-                vsc_pool[r:P:32, :].bitcast(I32).rearrange("q (u e) -> q u e", u=POOL_PAGES), vsc_rows[r].bitcast(I32)
-            )
+        vs_turned = {}
+
+        def turn_vs(e):
+            vs_turned[e] = keep.tile([P, PACK], F32, name="vs_turned%d" % e)
+            nc.sync.dma_start(vs_turned[e][:], vs_listed[P - 1 : P, e * PAGE : (e + 1) * PAGE].rearrange("o (s t) -> o s t", t=PACK))
+
+        for e in range(SCALED_ON_SCALAR):
+            turn_vs(e)
         nc.sync.dma_start(
             vw_pool[:].rearrange("p (u e) -> p u e", u=POOL_PAGES),
             v_words.rearrange("u p e r -> p u (e r)").bitcast(I32),
         )
-        vs_turned = []
-        for e in range(PAGES):
-            vs_turned.append(keep.tile([P, PACK], F32, name="vs_turned%d" % e))
-            nc.sync.dma_start(vs_turned[e][:], vs_listed[P - 1 : P, e * PAGE : (e + 1) * PAGE].rearrange("o (s t) -> o s t", t=PACK))
+        for e in range(SCALED_ON_SCALAR, PAGES):
+            turn_vs(e)
+        vsc_plane = keep.tile([P, PAGES * DV], U8, name="vsc_plane", align_bytes=256)
+        for quadrant in range(4):
+            nc.sync.dma_start(
+                vsc_plane[32 * quadrant : 32 * quadrant + 4, :].bitcast(I32),
+                vsc_listed[16 * quadrant : 16 * quadrant + 16 : 4, :].bitcast(I32),
+            )
 
         pairs = {}
         keys = {}
 
         def gather_keys(e):
             if e < 2:
-                pairs[e] = keep.tile([P, PAGE], U32, name="pairs%d" % e, align_bytes=64)
+                pairs[e] = keep.tile([P, PAGE], U32, name="pairs%d" % e, align_bytes=256)
             else:
-                pairs[e] = late.tile([P, PAGE], U32, name="pairs%d" % e, align_bytes=64, offset=(e - 1) * SLOT)
+                pairs[e] = late.tile([P, PAGE], U32, name="pairs%d" % e, align_bytes=256, offset=(e - 1) * SLOT)
             nc.vector.tensor_copy(
                 pairs[e][:], kw_pool[:].bitcast(U32).indirect(slots[:, e * PAGE // 16 : (e + 1) * PAGE // 16])
             )
@@ -130,9 +136,9 @@ def tile_attend_pkv4_rel2_cap_kernel(tc, qT, k_words, k_scales, v_words, v_scale
         def part_keys(e, h):
             width = PAGE // PARTS[e]
             if e == 1:
-                keys[e, h] = late.tile([P, PASSES, 2 * width], U8, name="keys%d_%d" % (e, h), align_bytes=64, offset=0)
+                keys[e, h] = late.tile([P, PASSES, 2 * width], U8, name="keys%d_%d" % (e, h), align_bytes=256, offset=0)
             else:
-                keys[e, h] = keep.tile([P, PASSES, 2 * width], U8, name="keys%d_%d" % (e, h), align_bytes=64)
+                keys[e, h] = keep.tile([P, PASSES, 2 * width], U8, name="keys%d_%d" % (e, h), align_bytes=256)
             nc.vector.tensor_copy(
                 keys[e, h][:].bitcast(U16),
                 pairs[e][:, h * width : (h + 1) * width].bitcast(U16).rearrange("p (n g) -> p g n", g=PASSES),
@@ -141,17 +147,17 @@ def tile_attend_pkv4_rel2_cap_kernel(tc, qT, k_words, k_scales, v_words, v_scale
         gather_keys(0)
         gather_keys(1)
         part_keys(0, 0)
-        part_keys(0, 1)
-        quantise_queries(0)
-        quantise_queries(1)
+        q_codes = keep.tile([P, PASSES * NQ], U32, name="q_codes", align_bytes=256)
+        q_scales = keep.tile([P, PASSES * NQ], U8, name="q_scales", align_bytes=256)
+        nc.vector.quantize_mx(
+            out=q_codes[:].bitcast(FP8X4), scales=q_scales[:], in_=q_bf[:].rearrange("p g w j -> p (g w j)")
+        )
         part_keys(1, 0)
         gather_keys(2)
         gather_keys(3)
         part_keys(2, 0)
         part_keys(3, 0)
         part_keys(3, 1)
-        vsc_plane = keep.tile([P, PAGES * DV], U8, name="vsc_plane", align_bytes=64)
-        nc.vector.tensor_copy(vsc_plane[:], vsc_pool[:].indirect(vcols[:]))
 
         scores = {}
         for e in range(PAGES):
@@ -162,8 +168,8 @@ def tile_attend_pkv4_rel2_cap_kernel(tc, qT, k_words, k_scales, v_words, v_scale
                 for g in range(PASSES):
                     nc.tensor.matmul_mx(
                         out=bank[:],
-                        lhsT=q_codes[g][:].bitcast(FP8X4),
-                        lhsT_scale=q_scales[g][:],
+                        lhsT=q_codes[:, g * NQ : (g + 1) * NQ].bitcast(FP8X4),
+                        lhsT_scale=q_scales[:, g * NQ : (g + 1) * NQ],
                         rhs=keys[e, h][:, g, :].bitcast(FP4X4),
                         rhs_scale=ks_planes[:, g, slot0 : slot0 + width],
                         start=(g == 0),
@@ -172,36 +178,43 @@ def tile_attend_pkv4_rel2_cap_kernel(tc, qT, k_words, k_scales, v_words, v_scale
                 scores[e, h] = bank[:].rearrange("q (s t) -> q t s", t=PACK)
 
         capped = {}
-        weights = [keep.tile([P, PACK, P], F32, name="weights%d" % e) for e in range(PAGES)]
-        positive = keep.tile([P, PACK, P], F32, name="positive")
-        turned = {}
-        w_bf = [keep.tile([P, NQ, PACK], BF16, name="w_bf%d" % e, align_bytes=64) for e in range(PAGES)]
-
-        def cap(e, h):
+        for e, h in scores:
             if (e, h) == (PAGES - 1, 0):
-                capped[e, h] = last.tile(list(scores[e, h].shape), F32, name="capped%d_%d" % (e, h), align_bytes=64, offset=0)
+                capped[e, h] = last.tile(list(scores[e, h].shape), F32, name="capped%d_%d" % (e, h), align_bytes=256, offset=0)
             else:
-                capped[e, h] = keep.tile(list(scores[e, h].shape), F32, name="capped%d_%d" % (e, h))
+                capped[e, h] = keep.tile(list(scores[e, h].shape), F32, name="capped%d_%d" % (e, h), align_bytes=256)
             nc.scalar.activation(capped[e, h][:], scores[e, h], ACT.Tanh, scale=1.0 / CAP)
 
-        def rectify_first(h):
-            width = P // PARTS[0]
-            nc.scalar.activation(positive[:, :, h * width : (h + 1) * width], capped[0, h][:], ACT.Relu)
-
-        def square_on_vector(e, h):
+        turned = []
+        for e in range(PAGES):
+            weights = keep.tile([P, PACK, P], F32, name="weights%d" % e, align_bytes=256)
             width = P // PARTS[e]
-            column = 1 + e + h
-            nc.vector.scalar_tensor_tensor(
-                weights[e][:, :, h * width : (h + 1) * width], capped[e, h][:], 0.0, capped[e, h][:], ALU.max, ALU.mult,
-                accum_out=sums[:, column : column + 1],
-            )
-
-        def turn(e):
-            turned[e] = psum.tile([P, PACK, NQ], F32, name="turned%d" % e, tag="bank%d" % TURN_BANKS[e])
+            for h in range(PARTS[e]):
+                column = 1 + e + h
+                nc.vector.scalar_tensor_tensor(
+                    weights[:, :, h * width : (h + 1) * width], capped[e, h][:], 0.0, capped[e, h][:], ALU.max, ALU.mult,
+                    accum_out=sums[:, column : column + 1],
+                )
+            turned.append(psum.tile([P, PACK, NQ], F32, name="turned%d" % e, tag="bank%d" % TURN_BANKS[e]))
             for t in range(PACK):
-                nc.tensor.transpose(turned[e][:, t, :], weights[e][:, t, :], identity[:])
+                nc.tensor.transpose(turned[e][:, t, :], weights[:, t, :], identity[:])
 
-        def scale_on_vector(e):
+        vw = last.tile([P, PAGES * DV], U32, name="vw", align_bytes=256, offset=0)
+        nc.vector.tensor_copy(vw[:], vw_pool[:].bitcast(U32).indirect(vcols[:]))
+
+        w_bf = [keep.tile([P, NQ, PACK], BF16, name="w_bf%d" % e, align_bytes=256) for e in range(PAGES)]
+        by_place = []
+        for e in range(SCALED_ON_SCALAR):
+            by_place.append(final.tile([P, PACK, NQ], BF16, name="by_place%d" % e, align_bytes=256, offset=e * 2 * PAGE))
+            for t in range(PACK):
+                nc.scalar.activation(by_place[e][:, t, :], turned[e][:, t, :], ACT.Copy, scale=vs_turned[e][:, t : t + 1])
+        for e in range(SCALED_ON_SCALAR):
+            nc.scalar.copy(w_bf[e][:], by_place[e][:].rearrange("s t q -> s q t"))
+        denom = keep.tile([P, 1], F32, name="denom")
+        sums_copy = final.tile(list(sums.shape), F32, name="sums_copy", align_bytes=256, offset=0)
+        nc.scalar.activation(sums_copy[:], sums[:], ACT.Copy, accum_out=denom[:])
+
+        for e in range(SCALED_ON_SCALAR, PAGES):
             nc.vector.tensor_tensor(
                 w_bf[e][:],
                 turned[e][:].rearrange("s t q -> s q t"),
@@ -210,10 +223,9 @@ def tile_attend_pkv4_rel2_cap_kernel(tc, qT, k_words, k_scales, v_words, v_scale
             )
 
         acc = psum.tile([P, DV], F32, name="acc", tag="bank%d" % ACC_BANK)
-
-        def multiply(e):
-            w_codes = keep.tile([P, NQ], U32, name="w_codes%d" % e, align_bytes=64)
-            w_scales = keep.tile([P, NQ], U8, name="w_scales%d" % e, align_bytes=64)
+        for e in PRODUCT_ORDER:
+            w_codes = keep.tile([P, NQ], U32, name="w_codes%d" % e, align_bytes=256)
+            w_scales = keep.tile([P, NQ], U8, name="w_scales%d" % e, align_bytes=256)
             nc.vector.quantize_mx(
                 out=w_codes[:].bitcast(FP8X4), scales=w_scales[:], in_=w_bf[e][:].rearrange("s q t -> s (q t)")
             )
@@ -226,46 +238,9 @@ def tile_attend_pkv4_rel2_cap_kernel(tc, qT, k_words, k_scales, v_words, v_scale
                 start=(e == PRODUCT_ORDER[0]),
                 stop=(e == PRODUCT_ORDER[-1]),
             )
-
-        cap(0, 0)
-        cap(0, 1)
-        rectify_first(0)
-        rectify_first(1)
-        cap(1, 0)
-        nc.scalar.activation(weights[0][:], positive[:], ACT.Square, accum_out=sums[:, 1:2])
-        cap(2, 0)
-        cap(3, 0)
-        cap(3, 1)
-        turn(0)
-        square_on_vector(1, 0)
-        turn(1)
-        square_on_vector(2, 0)
-        turn(2)
-        square_on_vector(3, 0)
-        square_on_vector(3, 1)
-        turn(3)
-
-        vw = last.tile([P, PAGES * DV], U32, name="vw", align_bytes=64, offset=0)
-        nc.vector.tensor_copy(vw[:], vw_pool[:].bitcast(U32).indirect(vcols[:]))
-
-        by_place = []
-        for e in range(2):
-            by_place.append(keep.tile([P, PACK, NQ], BF16, name="by_place%d" % e, align_bytes=64))
-            for t in range(PACK):
-                nc.scalar.activation(by_place[e][:, t, :], turned[e][:, t, :], ACT.Copy, scale=vs_turned[e][:, t : t + 1])
-        for e in range(2):
-            nc.scalar.copy(w_bf[e][:], by_place[e][:].rearrange("s t q -> s q t"))
-        denom = keep.tile([P, 1], F32, name="denom")
-        sums_copy = keep.tile(list(sums.shape), F32, name="sums_copy")
-        nc.scalar.activation(sums_copy[:], sums[:], ACT.Copy, accum_out=denom[:])
-
-        scale_on_vector(2)
-        scale_on_vector(3)
-        for e in PRODUCT_ORDER:
-            multiply(e)
         inverse = keep.tile([P, 1], F32, name="inverse")
         nc.vector.reciprocal(inverse[:], denom[:])
 
-        result = keep.tile([P, DV], F32, name="result")
+        result = keep.tile([P, DV], F32, name="result", align_bytes=256)
         nc.scalar.activation(result[:], acc[:], ACT.Copy, scale=inverse[:])
         nc.sync.dma_start(out[0], result[:])

from contextlib import ExitStack

import concourse.mybir as mybir
from concourse.masks import make_identity

N, T, D, DV, NQ = 2048, 4096, 1024, 128, 128
PAGE = 512
CAP = 2.0
FLOPS = 2 * NQ * N * (D + DV)

F32 = mybir.dt.float32
BF16 = mybir.dt.bfloat16
I32 = mybir.dt.int32
U32 = mybir.dt.uint32
U16 = mybir.dt.uint16
U8 = mybir.dt.uint8
FP8X4 = mybir.dt.float8_e4m3fn_x4
FP4X4 = mybir.dt.float4_e2m1fn_x4
ACT = mybir.ActivationFunctionType
ALU = mybir.AluOpType

P = 128
PACK = 4
PAGES = N // PAGE
POOL_PAGES = T // PAGE
PASSES = D // (P * PACK)
SCALE_ROWS = 16
KS_ROW0 = P - PASSES * SCALE_ROWS
VS_ON_VECTOR = 896
PARTS = (1, 1, 1, 2)
SCORE_BANKS = ((0,), (1,), (2,), (3, 4))
TURN_BANKS = (5, 6, 7, 0)
ACC_BANK = 1
SCALED_ON_SCALAR = 2
PRODUCT_ORDER = (0, 2, 3, 1)
SLOT = 4 * PAGE


def tile_attend_pkv4_rel2_cap_kernel(tc, qT, k_words, k_scales, v_words, v_scales, vs, offs, voffs, out):
    nc = tc.nc
    with ExitStack() as ctx:
        lists = ctx.enter_context(tc.tile_pool(name="lists", bufs=1))
        keep = ctx.enter_context(tc.tile_pool(name="keep", bufs=1))
        late = ctx.enter_context(tc.tile_pool(name="late", bufs=1))
        last = ctx.enter_context(tc.tile_pool(name="last", bufs=1))
        final = ctx.enter_context(tc.tile_pool(name="final", bufs=1))
        psum = ctx.enter_context(tc.psum_pool(name="psum", bufs=1))

        slots = lists.tile([P, N // 16], U16, name="slots")
        vcols = lists.tile([P, PAGES * DV // 16], U16, name="vcols")
        ks_pool = keep.tile([P, T + 4], U8, name="ks_pool", align_bytes=256)
        vs_pool = keep.tile([P, T], F32, name="vs_pool", align_bytes=256)
        kw_pool = keep.tile([P, T], I32, name="kw_pool", align_bytes=256)
        vsc_pool = keep.tile([P, POOL_PAGES * DV], U8, name="vsc_pool", align_bytes=256)
        vw_pool = keep.tile([P, POOL_PAGES * DV], I32, name="vw_pool", align_bytes=256)
        q_first = keep.tile([P, PACK * NQ], F32, name="q_first", align_bytes=256)
        late_area = late.tile([P, 3 * PAGE], F32, name="late_area", align_bytes=256, offset=0)
        q_raw = [area[:, 0 : PACK * NQ].rearrange("p (j w) -> p j w", j=PACK) for area in (q_first, late_area)]
        q_rows = qT[0].rearrange("(g p j) w -> g p j w", g=PASSES, j=PACK)

        nc.sync.dma_start(ks_pool[KS_ROW0:P, 0:T].bitcast(I32), k_scales.rearrange("g f t -> f g t").bitcast(I32))
        nc.sync.dma_start(slots[:], offs)
        nc.scalar.dma_start(vs_pool[P - 1 : P, :], vs[0:1, :])
        nc.sync.dma_start(vcols[:], voffs)
        nc.sync.dma_start(kw_pool[:], k_words[0].rearrange("p t b -> p (t b)").bitcast(I32))
        nc.sync.dma_start(q_raw[0], q_rows[0])
        nc.sync.dma_start(q_raw[1], q_rows[1])

        nc.gpsimd.memset(vsc_pool[:].bitcast(I32), 0)
        sums = keep.tile([P, 2 + PAGES], F32, name="sums")
        nc.gpsimd.memset(sums[:, 0:1], 1.0 / (CAP * CAP))
        identity = keep.tile([P, P], F32, name="identity")
        make_identity(nc, identity[:])
        nc.vector.memset(ks_pool[0:KS_ROW0, :].bitcast(I32), 0)
        nc.vector.memset(vs_pool[0 : P - 1, :], 0.0)

        nc.scalar.dma_start(
            vsc_pool[0 : 4 * SCALE_ROWS : 4, :].bitcast(I32).rearrange("f (u e) -> f u e", u=POOL_PAGES),
            v_scales.rearrange("u f e -> f u e").bitcast(I32),
        )
        warm = keep.tile([P, 1], F32, name="warm")
        nc.scalar.activation(warm[:], sums[:, 0:1], ACT.Tanh)

        ks_listed = keep.tile([P, N], U8, name="ks_listed", align_bytes=256)
        nc.vector.tensor_copy(ks_listed[:], ks_pool[:, 0:T].indirect(slots[:]))
        vs_listed = keep.tile([P, N], F32, name="vs_listed", align_bytes=256)
        nc.vector.tensor_copy(vs_listed[:, 0:VS_ON_VECTOR], vs_pool[:].indirect(slots[:, 0 : VS_ON_VECTOR // 16]))
        nc.scalar.activation(vs_listed[:, VS_ON_VECTOR:N], vs_pool[:].indirect(slots[:, VS_ON_VECTOR // 16 : N // 16]), ACT.Copy)
        vsc_listed = keep.tile([P, PAGES * DV], U8, name="vsc_listed", align_bytes=256)
        nc.vector.tensor_copy(vsc_listed[:], vsc_pool[:].indirect(vcols[:]))

        q_bf = keep.tile([P, PASSES, NQ, PACK], BF16, name="q_bf", align_bytes=256)
        for g in range(PASSES):
            nc.scalar.copy(q_bf[:, g], q_raw[g].rearrange("p j w -> p w j"))

        ks_planes = keep.tile([P, PASSES, N], U8, name="ks_planes", align_bytes=256)
        for quadrant in (0, 2, 1, 3):
            row0 = KS_ROW0 + 4 * PASSES * quadrant
            nc.sync.dma_start(
                ks_planes[32 * quadrant : 32 * quadrant + 4, :, :].bitcast(I32),
                ks_listed[row0 : row0 + 4 * PASSES, :].bitcast(I32),
            )
        vs_turned = {}

        def turn_vs(e):
            vs_turned[e] = keep.tile([P, PACK], F32, name="vs_turned%d" % e)
            nc.sync.dma_start(vs_turned[e][:], vs_listed[P - 1 : P, e * PAGE : (e + 1) * PAGE].rearrange("o (s t) -> o s t", t=PACK))

        for e in range(SCALED_ON_SCALAR):
            turn_vs(e)
        nc.sync.dma_start(
            vw_pool[:].rearrange("p (u e) -> p u e", u=POOL_PAGES),
            v_words.rearrange("u p e r -> p u (e r)").bitcast(I32),
        )
        for e in range(SCALED_ON_SCALAR, PAGES):
            turn_vs(e)
        vsc_plane = keep.tile([P, PAGES * DV], U8, name="vsc_plane", align_bytes=256)
        for quadrant in range(4):
            nc.sync.dma_start(
                vsc_plane[32 * quadrant : 32 * quadrant + 4, :].bitcast(I32),
                vsc_listed[16 * quadrant : 16 * quadrant + 16 : 4, :].bitcast(I32),
            )

        pairs = {}
        keys = {}

        def gather_keys(e):
            if e < 2:
                pairs[e] = keep.tile([P, PAGE], U32, name="pairs%d" % e, align_bytes=256)
            else:
                pairs[e] = late.tile([P, PAGE], U32, name="pairs%d" % e, align_bytes=256, offset=(e - 1) * SLOT)
            nc.vector.tensor_copy(
                pairs[e][:], kw_pool[:].bitcast(U32).indirect(slots[:, e * PAGE // 16 : (e + 1) * PAGE // 16])
            )

        def part_keys(e, h):
            width = PAGE // PARTS[e]
            if e == 1:
                keys[e, h] = late.tile([P, PASSES, 2 * width], U8, name="keys%d_%d" % (e, h), align_bytes=256, offset=0)
            else:
                keys[e, h] = keep.tile([P, PASSES, 2 * width], U8, name="keys%d_%d" % (e, h), align_bytes=256)
            nc.vector.tensor_copy(
                keys[e, h][:].bitcast(U16),
                pairs[e][:, h * width : (h + 1) * width].bitcast(U16).rearrange("p (n g) -> p g n", g=PASSES),
            )

        gather_keys(0)
        gather_keys(1)
        part_keys(0, 0)
        q_codes = keep.tile([P, PASSES * NQ], U32, name="q_codes", align_bytes=256)
        q_scales = keep.tile([P, PASSES * NQ], U8, name="q_scales", align_bytes=256)
        nc.vector.quantize_mx(
            out=q_codes[:].bitcast(FP8X4), scales=q_scales[:], in_=q_bf[:].rearrange("p g w j -> p (g w j)")
        )
        part_keys(1, 0)
        gather_keys(2)
        gather_keys(3)
        part_keys(2, 0)
        part_keys(3, 0)
        part_keys(3, 1)

        scores = {}
        for e in range(PAGES):
            width = PAGE // PARTS[e]
            for h in range(PARTS[e]):
                bank = psum.tile([P, width], F32, name="scores%d_%d" % (e, h), tag="bank%d" % SCORE_BANKS[e][h])
                slot0 = e * PAGE + h * width
                for g in range(PASSES):
                    nc.tensor.matmul_mx(
                        out=bank[:],
                        lhsT=q_codes[:, g * NQ : (g + 1) * NQ].bitcast(FP8X4),
                        lhsT_scale=q_scales[:, g * NQ : (g + 1) * NQ],
                        rhs=keys[e, h][:, g, :].bitcast(FP4X4),
                        rhs_scale=ks_planes[:, g, slot0 : slot0 + width],
                        start=(g == 0),
                        stop=(g == PASSES - 1),
                    )
                scores[e, h] = bank[:].rearrange("q (s t) -> q t s", t=PACK)

        capped = {}
        for e, h in scores:
            if (e, h) == (PAGES - 1, 0):
                capped[e, h] = last.tile(list(scores[e, h].shape), F32, name="capped%d_%d" % (e, h), align_bytes=256, offset=0)
            else:
                capped[e, h] = keep.tile(list(scores[e, h].shape), F32, name="capped%d_%d" % (e, h), align_bytes=256)
            nc.scalar.activation(capped[e, h][:], scores[e, h], ACT.Tanh, scale=1.0 / CAP)

        turned = []
        for e in range(PAGES):
            weights = keep.tile([P, PACK, P], F32, name="weights%d" % e, align_bytes=256)
            width = P // PARTS[e]
            for h in range(PARTS[e]):
                column = 1 + e + h
                nc.vector.scalar_tensor_tensor(
                    weights[:, :, h * width : (h + 1) * width], capped[e, h][:], 0.0, capped[e, h][:], ALU.max, ALU.mult,
                    accum_out=sums[:, column : column + 1],
                )
            turned.append(psum.tile([P, PACK, NQ], F32, name="turned%d" % e, tag="bank%d" % TURN_BANKS[e]))
            for t in range(PACK):
                nc.tensor.transpose(turned[e][:, t, :], weights[:, t, :], identity[:])

        vw = last.tile([P, PAGES * DV], U32, name="vw", align_bytes=256, offset=0)
        nc.vector.tensor_copy(vw[:], vw_pool[:].bitcast(U32).indirect(vcols[:]))

        w_bf = [keep.tile([P, NQ, PACK], BF16, name="w_bf%d" % e, align_bytes=256) for e in range(PAGES)]
        by_place = []
        for e in range(SCALED_ON_SCALAR):
            by_place.append(final.tile([P, PACK, NQ], BF16, name="by_place%d" % e, align_bytes=256, offset=e * 2 * PAGE))
            for t in range(PACK):
                nc.scalar.activation(by_place[e][:, t, :], turned[e][:, t, :], ACT.Copy, scale=vs_turned[e][:, t : t + 1])
        for e in range(SCALED_ON_SCALAR):
            nc.scalar.copy(w_bf[e][:], by_place[e][:].rearrange("s t q -> s q t"))
        denom = keep.tile([P, 1], F32, name="denom")
        sums_copy = final.tile(list(sums.shape), F32, name="sums_copy", align_bytes=256, offset=0)
        nc.scalar.activation(sums_copy[:], sums[:], ACT.Copy, accum_out=denom[:])

        for e in range(SCALED_ON_SCALAR, PAGES):
            nc.vector.tensor_tensor(
                w_bf[e][:],
                turned[e][:].rearrange("s t q -> s q t"),
                vs_turned[e][:].unsqueeze(1).to_broadcast([P, NQ, PACK]),
                ALU.mult,
            )

        acc = psum.tile([P, DV], F32, name="acc", tag="bank%d" % ACC_BANK)
        for e in PRODUCT_ORDER:
            w_codes = keep.tile([P, NQ], U32, name="w_codes%d" % e, align_bytes=256)
            w_scales = keep.tile([P, NQ], U8, name="w_scales%d" % e, align_bytes=256)
            nc.vector.quantize_mx(
                out=w_codes[:].bitcast(FP8X4), scales=w_scales[:], in_=w_bf[e][:].rearrange("s q t -> s (q t)")
            )
            nc.tensor.matmul_mx(
                out=acc[:],
                lhsT=w_codes[:].bitcast(FP8X4),
                lhsT_scale=w_scales[:],
                rhs=vw[:, e * DV : (e + 1) * DV].bitcast(FP8X4),
                rhs_scale=vsc_plane[:, e * DV : (e + 1) * DV],
                start=(e == PRODUCT_ORDER[0]),
                stop=(e == PRODUCT_ORDER[-1]),
            )
        inverse = keep.tile([P, 1], F32, name="inverse")
        nc.vector.reciprocal(inverse[:], denom[:])

        result = keep.tile([P, DV], F32, name="result", align_bytes=256)
        nc.scalar.activation(result[:], acc[:], ACT.Copy, scale=inverse[:])
        nc.sync.dma_start(out[0], result[:])
